import numpy as np
import ml_dtypes


def mxq(x, axis, fmt="e4m3"):
    dtype, down = {"e4m3": (ml_dtypes.float8_e4m3fn, 7), "e5m2": (ml_dtypes.float8_e5m2, 14)}[fmt]
    v = np.moveaxis(np.asarray(x, np.float32).astype(ml_dtypes.bfloat16).astype(np.float64), axis, -1)
    blocks = v.reshape(v.shape[:-1] + (-1, 32))
    amax = np.abs(blocks).max(-1, keepdims=True)
    byte = np.maximum(np.where(amax > 0, np.frexp(amax)[1] - 1 + 127, 0) - down, 1)
    scale = np.exp2(byte - 127.0)
    codes = (blocks / scale).astype(np.float32).astype(dtype).astype(np.float64)
    return np.moveaxis((codes * scale).reshape(v.shape), -1, axis)


WIDE = False


def mx_kscale(k):
    if not WIDE:
        return np.ones(k)
    levels = np.array([10, -10, 5, -5, 0])
    if k % 512:
        return np.exp2(np.random.permutation(np.resize(levels, k // 32))).repeat(32)
    a = np.empty((k // 512, 16))
    for p in range(k // 512):
        a[p, :8] = np.random.permutation(np.resize(levels, 8))
        for g in range(8):
            far = levels[np.abs(levels - a[p, g]) >= 10]
            a[p, g + 8] = far[np.random.randint(len(far))]
    return np.exp2(a.ravel()).repeat(32)


def f64(x):
    return np.asarray(x).astype(np.float64)


def striped(idx):
    return np.tile(idx.reshape(-1, 16).T, (8, 1)).astype(np.uint16)


def unstriped(offs):
    return offs[:16].T.reshape(-1).astype(np.int64)


E2M1 = np.array([0.0, 0.5, 1.0, 1.5, 2.0, 3.0, 4.0, 6.0, -0.0, -0.5, -1.0, -1.5, -2.0, -3.0, -4.0, -6.0])


def pack_weight(w, fmt):
    k, n = w.shape
    w = f64(np.asarray(w, np.float32).astype(ml_dtypes.bfloat16)).reshape(k // 32, 32, n)
    amax = np.abs(w).max(1)
    if fmt == "e4m3":
        byte = np.frexp(amax)[1] - 1 + 127 - 7
    else:
        mant, ex = np.frexp(amax / 6.0)
        byte = np.where(mant > 0.5, ex, ex - 1) + 127
    byte = np.clip(np.where(amax > 0, byte, 1), 1, 254)
    scaled = (w * np.exp2(127.0 - byte)[:, None, :]).reshape(k, n).astype(np.float32)
    by_word = np.ascontiguousarray(scaled.reshape(k // 512, 128, 4, n).transpose(0, 1, 3, 2))
    if fmt == "e4m3":
        words = by_word.astype(ml_dtypes.float8_e4m3fn).view(np.uint8)
    else:
        c = by_word.astype(ml_dtypes.float4_e2m1fn).view(np.uint8) & 0xF
        words = (c[..., 0::2] | (c[..., 1::2] << 4)).reshape(k // 512, 128, 2 * n)
    return np.ascontiguousarray(words), np.ascontiguousarray(byte.astype(np.uint8).reshape(k // 512, 16, n))


def unpack_weight(words, scales, fmt):
    g, _, n = scales.shape
    words = np.ascontiguousarray(words).reshape(g, 128, n, -1)
    if fmt == "e4m3":
        vals = words.view(ml_dtypes.float8_e4m3fn).astype(np.float64)
    else:
        nib = np.empty((g, 128, n, 4), np.uint8)
        nib[..., 0::2] = words & 0xF
        nib[..., 1::2] = words >> 4
        vals = E2M1[nib]
    vals = vals * np.repeat(np.exp2(scales.astype(np.float64) - 127.0), 8, axis=1)[..., None]
    return vals.transpose(0, 1, 3, 2).reshape(g * 512, n)


def gelu(v):
    return 0.5 * v * (1.0 + np.tanh(np.sqrt(2.0 / np.pi) * (v + 0.044715 * v**3)))


K, T, S, H, T2, P, N = 1024, 4096, 1024, 1024, 2048, 1024, 512

def setup_inputs():
    n = np.random.standard_normal
    s = mx_kscale(K)[:, None]
    u = mx_kscale(H)[:, None]
    tab_words, tab_scales = pack_weight(n((K, T)) * s, "e4m3")
    w1_words, w1_scales = pack_weight(n((K, H)) / np.sqrt(K) / s * u.T, "e2m1")
    f = n((H, N)) / np.sqrt(H)
    sq_words, sq_scales = pack_weight(f * f / (u * u), "e4m3")
    return {
        "tab_words": tab_words, "tab_scales": tab_scales,
        "offs": striped(np.random.permutation(T)[:S]),
        "w1_words": w1_words, "w1_scales": w1_scales,
        "wgs": np.exp(0.3 * n((128, S))).astype(np.float32),
        "page0": (n((H, T2)) * u).astype(np.float32),
        "offs2": striped(np.random.permutation(T2)[:S]),
        "offs3": striped(np.random.permutation(T2)[:P]),
        "fw": (f / u).astype(np.float32),
        "sq_words": sq_words, "sq_scales": sq_scales,
    }

def reference(tab_words, tab_scales, offs, w1_words, w1_scales, wgs, page0, offs2, offs3, fw, sq_words, sq_scales):
    v = unpack_weight(tab_words, tab_scales, "e4m3")[:, unstriped(offs)]
    w1 = unpack_weight(w1_words, w1_scales, "e2m1")
    sq = unpack_weight(sq_words, sq_scales, "e4m3")
    h = w1.T @ v
    page = f64(page0).copy()
    page[:, unstriped(offs2)] = np.tile(f64(wgs), (H // 128, 1)) * h
    x = page[:, unstriped(offs3)]
    z = x * x
    a = mxq(f64(fw), 0, "e4m3").T @ mxq(x, 0, "e4m3")
    b = sq.T @ mxq(z, 0, "e4m3")
    return 0.5 * (a * a - b)

@@ -1,0 +1,286 @@
+from contextlib import ExitStack
+
+import concourse.mybir as mybir
+
+K, T, S, H, T2, M, N = 1024, 4096, 1024, 1024, 2048, 1024, 512
+FLOPS = 2 * K * H * S + 2 * 2 * H * N * M
+
+F32 = mybir.dt.float32
+BF16 = mybir.dt.bfloat16
+I32 = mybir.dt.int32
+U32 = mybir.dt.uint32
+U16 = mybir.dt.uint16
+U8 = mybir.dt.uint8
+FP8X4 = mybir.dt.float8_e4m3fn_x4
+FP4X4 = mybir.dt.float4_e2m1fn_x4
+MULT = mybir.AluOpType.mult
+ADD = mybir.AluOpType.add
+SQUARE = mybir.ActivationFunctionType.Square
+
+P = 128
+PACK = 4
+HALF = 512
+LIST_HALF = HALF // 16
+W1_COL = S
+SQ_COL = S + H
+PLANE_W = S + H + N
+
+
+def tile_list_gift_interactions_kernel(
+    tc, tab_words, tab_scales, offs, w1_words, w1_scales, wgs, page0, offs2, offs3, fw, sq_words, sq_scales, out
+):
+    nc = tc.nc
+    with ExitStack() as ctx:
+        lists = ctx.enter_context(tc.tile_pool(name="lists", bufs=1))
+        keep = ctx.enter_context(tc.tile_pool(name="keep", bufs=1))
+        ring = ctx.enter_context(tc.tile_pool(name="ring", bufs=1))
+        psum = ctx.enter_context(tc.psum_pool(name="psum", bufs=8))
+
+        idx = lists.tile([P, S // 16], U16, name="idx")
+        idx2 = lists.tile([P, S // 16], U16, name="idx2")
+        idx3 = lists.tile([P, M // 16], U16, name="idx3")
+
+        tab_sc = keep.tile([P, T], U8, name="tab_sc", align_bytes=64)
+        w1_sc = keep.tile([P, H], U8, name="w1_sc", align_bytes=64)
+        sc_rows = keep.tile([P, PLANE_W], U8, name="sc_rows", align_bytes=64)
+        planes = [sc_rows, keep.tile([P, PLANE_W], U8, name="plane1", align_bytes=64)]
+        w1_raw = keep.tile([P, 2 * 2 * H], U8, name="w1_raw", align_bytes=64)
+        w1_perm = keep.tile([P, 2 * 2 * H], U8, name="w1_perm", align_bytes=64)
+        tab = [ring.tile([P, T], I32, name="tab%d" % k, tag="big%d" % k, align_bytes=64) for k in range(2)]
+        wg = [keep.tile([P, S], F32, name="wg%d" % t) for t in range(PACK)]
+
+        for lo, hi in ((32, 64), (64, 128)):
+            nc.vector.memset(tab_sc[lo:hi, :].bitcast(I32), 0)
+            nc.gpsimd.memset(w1_sc[lo:hi, :].bitcast(I32), 0)
+            nc.gpsimd.memset(sc_rows[lo:hi, SQ_COL:].bitcast(I32), 0)
+        nc.gpsimd.memset(planes[1][:].bitcast(I32), 0)
+
+        def load_page(i):
+            a, t = divmod(i, PACK)
+            page = ring.tile([P, T2], F32, name="page%d" % i, tag="page", bufs=6)
+            rows = page0[HALF * a : HALF * (a + 1), :].rearrange("(p t) c -> t p c", t=PACK)
+            nc.sync.dma_start(out=page[:], in_=rows[t])
+            return page
+
+        def load_wg(t):
+            rows = wgs.rearrange("(q t) j -> t q j", t=PACK)[t]
+            for q in (0, 2, 1, 3):
+                nc.sync.dma_start(out=wg[t][32 * q : 32 * (q + 1), :], in_=rows)
+
+        nc.sync.dma_start(idx[:], offs)
+        nc.sync.dma_start(out=tab_sc[0:32, :].bitcast(I32), in_=tab_scales.rearrange("a q c -> (a q) c").bitcast(I32))
+        nc.sync.dma_start(out=w1_sc[0:32, :].bitcast(I32), in_=w1_scales.rearrange("a q c -> (a q) c").bitcast(I32))
+        nc.sync.dma_start(
+            out=sc_rows[0:32, SQ_COL:].bitcast(I32), in_=sq_scales.rearrange("a q c -> (a q) c").bitcast(I32)
+        )
+        nc.sync.dma_start(
+            out=w1_raw[:].bitcast(I32).rearrange("p (k c) -> p k c", k=2),
+            in_=w1_words.bitcast(I32).rearrange("k p c -> p k c"),
+        )
+        for k in range(2):
+            nc.sync.dma_start(out=tab[k][:], in_=tab_words[k].rearrange("p c i -> p (c i)").bitcast(I32))
+        pages = [load_page(0)]
+        nc.sync.dma_start(idx2[:], offs2)
+        load_wg(0)
+        nc.sync.dma_start(idx3[:], offs3)
+        pages.append(load_page(1))
+        load_wg(1)
+        fw_raw = [ring.tile([P, PACK * N], F32, name="fw_raw%d" % a, tag="stage%d" % a) for a in range(2)]
+        for a in range(2):
+            nc.sync.dma_start(
+                out=fw_raw[a][:], in_=fw[HALF * a : HALF * (a + 1), :].rearrange("(p i) n -> p (i n)", i=PACK)
+            )
+        pages.append(load_page(2))
+        load_wg(2)
+        pages.append(load_page(3))
+        load_wg(3)
+        sq_codes = keep.tile([P, 2 * N], I32, name="sq_codes", align_bytes=64)
+        nc.sync.dma_start(
+            out=sq_codes[:].rearrange("p (a c) -> p a c", a=2),
+            in_=sq_words.rearrange("a p c i -> p a (c i)").bitcast(I32),
+        )
+        pages.extend([load_page(4), load_page(5)])
+
+        got_sc = keep.tile([P, S], U8, name="got_sc", align_bytes=64)
+        nc.vector.tensor_copy(
+            out=sc_rows[:, W1_COL:SQ_COL].rearrange("p (a t m) -> p a t m", a=2, t=PACK),
+            in_=w1_sc[:].rearrange("p (a m t) -> p a t m", a=2, t=PACK),
+        )
+        nc.vector.tensor_copy(got_sc[:], tab_sc[:].indirect(idx[:]))
+        nc.vector.tensor_copy(out=sc_rows[:, 0:S].bitcast(I32), in_=got_sc[:].bitcast(I32))
+        for k in range(2):
+            for q in range(1 - k, 4):
+                nc.gpsimd.dma_start(
+                    out=planes[k][32 * q : 32 * q + 4, :].bitcast(I32),
+                    in_=sc_rows[16 * k + 4 * q : 16 * k + 4 * q + 4, :].bitcast(I32),
+                )
+        nc.vector.tensor_copy(
+            out=w1_perm[:].bitcast(U16).rearrange("p (g t m) -> p g t m", g=4, t=PACK),
+            in_=w1_raw[:].bitcast(U16).rearrange("p (g m t) -> p g t m", g=4, t=PACK),
+        )
+        v0 = keep.tile([P, S], U32, name="v0", align_bytes=64)
+        nc.vector.tensor_copy(v0[:], tab[0][:].bitcast(U32).indirect(idx[:]))
+        v1 = [keep.tile([P, HALF], U32, name="v1_%d" % j, align_bytes=64) for j in range(2)]
+        for j in range(2):
+            nc.vector.tensor_copy(
+                v1[j][:], tab[1][:].bitcast(U32).indirect(idx[:, LIST_HALF * j : LIST_HALF * (j + 1)])
+            )
+
+        def make_h(i):
+            h = ring.tile([P, S], F32, name="h%d" % i, tag="h%d" % (i % 4), align_bytes=64)
+            for j in range(2):
+                cols = slice(HALF * j, HALF * (j + 1))
+                acc = psum.tile([P, HALF], F32, name="acc", tag="acc")
+                for k in range(2):
+                    first = 2 * (H * k + P * i)
+                    nc.tensor.matmul_mx(
+                        out=acc[:],
+                        lhsT=w1_perm[:, first : first + 2 * P].bitcast(FP4X4),
+                        lhsT_scale=planes[k][:, W1_COL + P * i : W1_COL + P * (i + 1)],
+                        rhs=(v0[:, cols] if k == 0 else v1[j][:]).bitcast(FP8X4),
+                        rhs_scale=planes[k][:, cols],
+                        start=(k == 0),
+                        stop=(k == 1),
+                    )
+                nc.scalar.copy(out=h[:, cols], in_=acc[:])
+            return h
+
+        def scatter(i, h):
+            pieces = 2 if i == 0 else 1
+            width = S // pieces
+            for j in range(pieces):
+                cols = slice(width * j, width * (j + 1))
+                nc.vector.tensor_tensor(
+                    pages[i][:].indirect(idx2[:, width // 16 * j : width // 16 * (j + 1)]),
+                    h[:, cols],
+                    wg[i % PACK][:, cols],
+                    MULT,
+                )
+
+        def weave(flat, t):
+            return flat.rearrange("p (t c i) -> p c t i", t=t, i=4)
+
+        def woven(tile, lo, hi):
+            return tile[:].rearrange("p (c i t) -> p c t i", i=4, t=PACK)[:, :, lo:hi, :]
+
+        def quantize(codes, scales, src):
+            nc.vector.quantize_mx(out=codes.bitcast(FP8X4), scales=scales, in_=src)
+
+        fw_codes = keep.tile([P, 2 * N], U32, name="fw_codes", align_bytes=64)
+        fw_sc = keep.tile([P, 2 * N], U8, name="fw_sc", align_bytes=64)
+        fw_bf = keep.tile([P, 2 * N * PACK], BF16, name="fw_bf", align_bytes=64)
+
+        xg0 = ring.tile([P, PACK * M], F32, name="xg0", tag="big0", align_bytes=64)
+        xg1 = ring.tile([P, PACK * M], F32, name="xg1", tag="big1", align_bytes=64)
+
+        def gather(i):
+            t = i % PACK
+            if i < PACK:
+                nc.vector.tensor_copy(xg0[:, M * t : M * (t + 1)], pages[i][:].indirect(idx3[:]))
+                return
+            for j in range(2):
+                gather_half(i, j)
+
+        def gather_half(i, j):
+            t = i % PACK
+            first = 2 * M * j + HALF * t
+            nc.vector.tensor_copy(
+                xg1[:, first : first + HALF], pages[i][:].indirect(idx3[:, LIST_HALF * j : LIST_HALF * (j + 1)])
+            )
+
+        hs = [make_h(i) for i in range(4)]
+        for a in range(2):
+            part = fw_bf[:, PACK * N * a : PACK * N * (a + 1)]
+            nc.scalar.copy(
+                out=part.rearrange("p (c i t) -> p c t i", i=4, t=PACK), in_=weave(fw_raw[a][:], PACK)
+            )
+
+        x_bf = [[None, None], [None, None]]
+        z_bf = [[None, None], [None, None]]
+        x_codes = [keep.tile([P, M], U32, name="x_codes%d" % a, align_bytes=64) for a in range(2)]
+        x_sc = [keep.tile([P, M], U8, name="x_sc%d" % a, align_bytes=64) for a in range(2)]
+        z_sc = [keep.tile([P, M], U8, name="z_sc%d" % a, align_bytes=64) for a in range(2)]
+        z_codes = [None, keep.tile([P, M], U32, name="z_codes1", align_bytes=64)]
+        halves = [slice(0, HALF), slice(HALF, M)]
+
+        def new_bf(kind, a, j):
+            return ring.tile([P, PACK * HALF], BF16, name="%s_bf%d%d" % (kind, a, j), tag="%s_bf%d%d" % (kind, a if kind == "z" else 0, j), align_bytes=64)
+
+        for i in range(8):
+            scatter(i, hs[i])
+            if i + 4 < 8:
+                hs.append(make_h(i + 4))
+            if i >= 1:
+                gather(i - 1)
+                if i + 5 < 8:
+                    pages.append(load_page(i + 5))
+            if i == 2:
+                quantize(fw_codes[:], fw_sc[:], fw_bf[:])
+            if i == 4:
+                planes0 = xg0[:].rearrange("p (t m) -> p t m", t=PACK)
+                for j in range(2):
+                    x_bf[0][j] = new_bf("x", 0, j)
+                    src = planes0[:, :, halves[j]].rearrange("p t (c i) -> p c t i", i=4)
+                    nc.scalar.copy(out=woven(x_bf[0][j], 0, PACK), in_=src)
+                for j in range(2):
+                    z_bf[0][j] = new_bf("z", 0, j)
+                    src = planes0[:, :, halves[j]].rearrange("p t (c i) -> p c t i", i=4)
+                    nc.scalar.activation(out=woven(z_bf[0][j], 0, PACK), in_=src, func=SQUARE)
+            if i == 5:
+                for j in range(2):
+                    quantize(x_codes[0][:, halves[j]], x_sc[0][:, halves[j]], x_bf[0][j][:])
+            if i == 6:
+                for j in range(2):
+                    src = weave(xg1[:, 2 * M * j : 2 * M * j + M], 2)
+                    x_bf[1][j] = new_bf("x", 1, j)
+                    nc.scalar.copy(out=woven(x_bf[1][j], 0, 2), in_=src)
+                    z_bf[1][j] = new_bf("z", 1, j)
+                    nc.scalar.activation(out=woven(z_bf[1][j], 0, 2), in_=src, func=SQUARE)
+
+        z_codes[0] = ring.tile([P, M], U32, name="z_codes0", tag="h3", align_bytes=64)
+
+        def product(acc, kind, n, a, j):
+            ncols = slice(N * a + P * n, N * a + P * (n + 1))
+            if kind == "a":
+                lhs, lhs_sc, rhs, rhs_sc = fw_codes[:, ncols], fw_sc[:, ncols], x_codes[a], x_sc[a]
+            else:
+                lhs, lhs_sc = sq_codes[:, ncols], planes[a][:, SQ_COL + P * n : SQ_COL + P * (n + 1)]
+                rhs, rhs_sc = z_codes[a], z_sc[a]
+            nc.tensor.matmul_mx(
+                out=acc[:],
+                lhsT=lhs.bitcast(FP8X4),
+                lhsT_scale=lhs_sc,
+                rhs=rhs[:, halves[j]].bitcast(FP8X4),
+                rhs_scale=rhs_sc[:, halves[j]],
+                start=(a == 0),
+                stop=(a == 1),
+            )
+
+        staged = [ring.tile([P, PACK * N], F32, name="staged%d" % j, tag="stage%d" % j) for j in range(2)]
+
+        for j in range(2):
+            acc_a = [psum.tile([P, HALF], F32, name="acc", tag="acc") for n in range(4)]
+            for n in range(4):
+                product(acc_a[n], "a", n, 0, j)
+            gather_half(7, j)
+            quantize(z_codes[0][:, halves[j]], z_sc[0][:, halves[j]], z_bf[0][j][:])
+            src = weave(xg1[:, 2 * M * j + M : 2 * M * (j + 1)], 2)
+            nc.scalar.activation(out=woven(z_bf[1][j], 2, PACK), in_=src, func=SQUARE)
+            nc.vector.tensor_copy(out=woven(x_bf[1][j], 2, PACK), in_=src)
+            quantize(x_codes[1][:, halves[j]], x_sc[1][:, halves[j]], x_bf[1][j][:])
+            quantize(z_codes[1][:, halves[j]], z_sc[1][:, halves[j]], z_bf[1][j][:])
+            acc_b = [psum.tile([P, HALF], F32, name="acc", tag="acc") for n in range(4)]
+            for n in range(4):
+                product(acc_b[n], "b", n, 0, j)
+            for n in range(4):
+                product(acc_a[n], "a", n, 1, j)
+            for n in range(4):
+                product(acc_b[n], "b", n, 1, j)
+            for n in range(4):
+                half_sq = ring.tile([P, HALF], F32, name="half_sq", tag="half_sq", bufs=4)
+                nc.scalar.activation(out=half_sq[:], in_=acc_a[n][:], func=SQUARE, scale=0.5**0.5)
+                res = staged[j][:, HALF * n : HALF * (n + 1)]
+                nc.vector.scalar_tensor_tensor(
+                    out=res, in0=acc_b[n][:], scalar=-0.5, in1=half_sq[:], op0=MULT, op1=ADD
+                )
+                nc.sync.dma_start(out=out[P * n : P * (n + 1), halves[j]], in_=res)

@@ -33,105 +33,122 @@ def tile_list_gift_interactions_kernel(
     with ExitStack() as ctx:
         lists = ctx.enter_context(tc.tile_pool(name="lists", bufs=1))
         keep = ctx.enter_context(tc.tile_pool(name="keep", bufs=1))
-        ring = ctx.enter_context(tc.tile_pool(name="ring", bufs=1))
         psum = ctx.enter_context(tc.psum_pool(name="psum", bufs=8))
 
         idx = lists.tile([P, S // 16], U16, name="idx")
         idx2 = lists.tile([P, S // 16], U16, name="idx2")
         idx3 = lists.tile([P, M // 16], U16, name="idx3")
 
-        tab_sc = keep.tile([P, T], U8, name="tab_sc", align_bytes=64)
-        w1_sc = keep.tile([P, H], U8, name="w1_sc", align_bytes=64)
         sc_rows = keep.tile([P, PLANE_W], U8, name="sc_rows", align_bytes=64)
         planes = [sc_rows, keep.tile([P, PLANE_W], U8, name="plane1", align_bytes=64)]
         w1_raw = keep.tile([P, 2 * 2 * H], U8, name="w1_raw", align_bytes=64)
         w1_perm = keep.tile([P, 2 * 2 * H], U8, name="w1_perm", align_bytes=64)
-        tab = [ring.tile([P, T], I32, name="tab%d" % k, tag="big%d" % k, align_bytes=64) for k in range(2)]
-        wg = [keep.tile([P, S], F32, name="wg%d" % t) for t in range(PACK)]
+        tab = [keep.tile([P, T], I32, name="tab%d" % k, tag="big%d" % k, align_bytes=64) for k in range(2)]
+        v0 = keep.tile([P, S], U32, name="v0", align_bytes=64)
+        v1 = [keep.tile([P, HALF], U32, name="v1_%d" % j, align_bytes=64) for j in range(2)]
+        wg_first = keep.tile([P, HALF], F32, name="wg_first")
 
-        for lo, hi in ((32, 64), (64, 128)):
-            nc.vector.memset(tab_sc[lo:hi, :].bitcast(I32), 0)
-            nc.gpsimd.memset(w1_sc[lo:hi, :].bitcast(I32), 0)
-            nc.gpsimd.memset(sc_rows[lo:hi, SQ_COL:].bitcast(I32), 0)
-        nc.gpsimd.memset(planes[1][:].bitcast(I32), 0)
-
-        def load_page(i):
+        def page_rows(i):
             a, t = divmod(i, PACK)
-            page = ring.tile([P, T2], F32, name="page%d" % i, tag="page", bufs=6)
-            rows = page0[HALF * a : HALF * (a + 1), :].rearrange("(p t) c -> t p c", t=PACK)
-            nc.sync.dma_start(out=page[:], in_=rows[t])
-            return page
+            return page0[HALF * a : HALF * (a + 1), :].rearrange("(p t) c -> t p c", t=PACK)[t]
 
-        def load_wg(t):
+        def load_wg(dst, t, cols):
             rows = wgs.rearrange("(q t) j -> t q j", t=PACK)[t]
             for q in (0, 2, 1, 3):
-                nc.sync.dma_start(out=wg[t][32 * q : 32 * (q + 1), :], in_=rows)
+                nc.sync.dma_start(out=dst[32 * q : 32 * (q + 1), :], in_=rows[:, cols])
 
-        nc.sync.dma_start(idx[:], offs)
-        nc.sync.dma_start(out=tab_sc[0:32, :].bitcast(I32), in_=tab_scales.rearrange("a q c -> (a q) c").bitcast(I32))
-        nc.sync.dma_start(out=w1_sc[0:32, :].bitcast(I32), in_=w1_scales.rearrange("a q c -> (a q) c").bitcast(I32))
-        nc.sync.dma_start(
-            out=sc_rows[0:32, SQ_COL:].bitcast(I32), in_=sq_scales.rearrange("a q c -> (a q) c").bitcast(I32)
-        )
-        nc.sync.dma_start(
-            out=w1_raw[:].bitcast(I32).rearrange("p (k c) -> p k c", k=2),
-            in_=w1_words.bitcast(I32).rearrange("k p c -> p k c"),
-        )
-        for k in range(2):
-            nc.sync.dma_start(out=tab[k][:], in_=tab_words[k].rearrange("p c i -> p (c i)").bitcast(I32))
+        halves = [slice(0, HALF), slice(HALF, M)]
+        with tc.tile_pool(name="head", bufs=1) as head:
+            tab_sc = head.tile([P, T], U8, name="tab_sc", align_bytes=64)
+            w1_sc = head.tile([P, H], U8, name="w1_sc", align_bytes=64)
+            got_sc = head.tile([P, S], U8, name="got_sc", align_bytes=64)
+
+            for lo, hi in ((32, 64), (64, 128)):
+                nc.vector.memset(tab_sc[lo:hi, :].bitcast(I32), 0)
+                nc.gpsimd.memset(w1_sc[lo:hi, :].bitcast(I32), 0)
+                nc.gpsimd.memset(sc_rows[lo:hi, SQ_COL:].bitcast(I32), 0)
+            nc.gpsimd.memset(planes[1][:].bitcast(I32), 0)
+
+            nc.sync.dma_start(idx[:], offs)
+            nc.sync.dma_start(out=tab_sc[0:32, :].bitcast(I32), in_=tab_scales.rearrange("a q c -> (a q) c").bitcast(I32))
+            nc.sync.dma_start(out=w1_sc[0:32, :].bitcast(I32), in_=w1_scales.rearrange("a q c -> (a q) c").bitcast(I32))
+            nc.sync.dma_start(
+                out=sc_rows[0:32, SQ_COL:].bitcast(I32), in_=sq_scales.rearrange("a q c -> (a q) c").bitcast(I32)
+            )
+            nc.sync.dma_start(idx2[:], offs2)
+            nc.sync.dma_start(idx3[:], offs3)
+            nc.sync.dma_start(
+                out=w1_raw[:].bitcast(I32).rearrange("p (k c) -> p k c", k=2),
+                in_=w1_words.bitcast(I32).rearrange("k p c -> p k c"),
+            )
+            load_wg(wg_first, 0, halves[0])
+            for k in range(2):
+                nc.sync.dma_start(out=tab[k][:], in_=tab_words[k].rearrange("p c i -> p (c i)").bitcast(I32))
+            nc.vector.tensor_copy(got_sc[:], tab_sc[:].indirect(idx[:]))
+            nc.vector.tensor_copy(
+                out=sc_rows[:, W1_COL:SQ_COL].rearrange("p (a t m) -> p a t m", a=2, t=PACK),
+                in_=w1_sc[:].rearrange("p (a m t) -> p a t m", a=2, t=PACK),
+            )
+            nc.vector.tensor_copy(out=sc_rows[:, 0:S].bitcast(I32), in_=got_sc[:].bitcast(I32))
+
+        def move_scales(cols, spare_queue):
+            for k in range(2):
+                for q in range(1 - k, 4):
+                    queue = spare_queue if (k, q) == (1, 3) else nc.sync
+                    queue.dma_start(
+                        out=planes[k][32 * q : 32 * q + 4, cols].bitcast(I32),
+                        in_=sc_rows[16 * k + 4 * q : 16 * k + 4 * q + 4, cols].bitcast(I32),
+                    )
+
+        move_scales(slice(0, W1_COL + HALF), nc.gpsimd)
+        ring = ctx.enter_context(tc.tile_pool(name="ring", bufs=1))
+        wg_second = ring.tile([P, HALF], F32, name="wg_second")
+        wg = [None] + [ring.tile([P, S], F32, name="wg%d" % t, tag="wg%d" % t, align_bytes=64) for t in range(1, PACK)]
+        hx = ring.tile([P, 9 * S], F32, name="hx")
+
+        def load_page(i):
+            page = ring.tile([P, T2], F32, name="page%d" % i, tag="page", bufs=6)
+            nc.sync.dma_start(out=page[:], in_=page_rows(i))
+            return page
+
         pages = [load_page(0)]
-        nc.sync.dma_start(idx2[:], offs2)
-        load_wg(0)
-        nc.sync.dma_start(idx3[:], offs3)
+        load_wg(wg_second, 0, halves[1])
         pages.append(load_page(1))
-        load_wg(1)
-        fw_raw = [ring.tile([P, PACK * N], F32, name="fw_raw%d" % a, tag="stage%d" % a) for a in range(2)]
+        load_wg(wg[1], 1, slice(0, S))
+        move_scales(slice(W1_COL + HALF, PLANE_W), nc.sync)
+        fw_raw = [keep.tile([P, PACK * N], F32, name="fw_raw%d" % a, tag="big%d" % a, align_bytes=64) for a in range(2)]
         for a in range(2):
             nc.sync.dma_start(
                 out=fw_raw[a][:], in_=fw[HALF * a : HALF * (a + 1), :].rearrange("(p i) n -> p (i n)", i=PACK)
             )
         pages.append(load_page(2))
-        load_wg(2)
+        load_wg(wg[2], 2, slice(0, S))
         pages.append(load_page(3))
-        load_wg(3)
-        sq_codes = keep.tile([P, 2 * N], I32, name="sq_codes", align_bytes=64)
+        load_wg(wg[3], 3, slice(0, S))
+        sq_codes = ring.tile([P, 2 * N], I32, name="sq_codes", align_bytes=64)
         nc.sync.dma_start(
             out=sq_codes[:].rearrange("p (a c) -> p a c", a=2),
             in_=sq_words.rearrange("a p c i -> p a (c i)").bitcast(I32),
         )
         pages.extend([load_page(4), load_page(5)])
 
-        got_sc = keep.tile([P, S], U8, name="got_sc", align_bytes=64)
-        nc.vector.tensor_copy(
-            out=sc_rows[:, W1_COL:SQ_COL].rearrange("p (a t m) -> p a t m", a=2, t=PACK),
-            in_=w1_sc[:].rearrange("p (a m t) -> p a t m", a=2, t=PACK),
-        )
-        nc.vector.tensor_copy(got_sc[:], tab_sc[:].indirect(idx[:]))
-        nc.vector.tensor_copy(out=sc_rows[:, 0:S].bitcast(I32), in_=got_sc[:].bitcast(I32))
-        for k in range(2):
-            for q in range(1 - k, 4):
-                nc.gpsimd.dma_start(
-                    out=planes[k][32 * q : 32 * q + 4, :].bitcast(I32),
-                    in_=sc_rows[16 * k + 4 * q : 16 * k + 4 * q + 4, :].bitcast(I32),
-                )
         nc.vector.tensor_copy(
             out=w1_perm[:].bitcast(U16).rearrange("p (g t m) -> p g t m", g=4, t=PACK),
             in_=w1_raw[:].bitcast(U16).rearrange("p (g m t) -> p g t m", g=4, t=PACK),
         )
-        v0 = keep.tile([P, S], U32, name="v0", align_bytes=64)
         nc.vector.tensor_copy(v0[:], tab[0][:].bitcast(U32).indirect(idx[:]))
-        v1 = [keep.tile([P, HALF], U32, name="v1_%d" % j, align_bytes=64) for j in range(2)]
         for j in range(2):
             nc.vector.tensor_copy(
                 v1[j][:], tab[1][:].bitcast(U32).indirect(idx[:, LIST_HALF * j : LIST_HALF * (j + 1)])
             )
 
         def make_h(i):
-            h = ring.tile([P, S], F32, name="h%d" % i, tag="h%d" % (i % 4), align_bytes=64)
+            h = hx[:, S * i : S * (i + 1)]
             for j in range(2):
                 cols = slice(HALF * j, HALF * (j + 1))
                 acc = psum.tile([P, HALF], F32, name="acc", tag="acc")
-                for k in range(2):
+                order = (0, 1) if (i, j) == (0, 0) else (1, 0)
+                for k in order:
                     first = 2 * (H * k + P * i)
                     nc.tensor.matmul_mx(
                         out=acc[:],
@@ -139,21 +156,21 @@ def tile_list_gift_interactions_kernel(
                         lhsT_scale=planes[k][:, W1_COL + P * i : W1_COL + P * (i + 1)],
                         rhs=(v0[:, cols] if k == 0 else v1[j][:]).bitcast(FP8X4),
                         rhs_scale=planes[k][:, cols],
-                        start=(k == 0),
-                        stop=(k == 1),
+                        start=(k == order[0]),
+                        stop=(k == order[1]),
                     )
                 nc.scalar.copy(out=h[:, cols], in_=acc[:])
             return h
 
         def scatter(i, h):
-            pieces = 2 if i == 0 else 1
+            pieces = 2 if i % PACK == 0 else 1
             width = S // pieces
             for j in range(pieces):
                 cols = slice(width * j, width * (j + 1))
                 nc.vector.tensor_tensor(
                     pages[i][:].indirect(idx2[:, width // 16 * j : width // 16 * (j + 1)]),
                     h[:, cols],
-                    wg[i % PACK][:, cols],
+                    (wg_first, wg_second)[j][:] if i % PACK == 0 else wg[i % PACK][:],
                     MULT,
                 )
 
@@ -166,29 +183,26 @@ def tile_list_gift_interactions_kernel(
         def quantize(codes, scales, src):
             nc.vector.quantize_mx(out=codes.bitcast(FP8X4), scales=scales, in_=src)
 
-        fw_codes = keep.tile([P, 2 * N], U32, name="fw_codes", align_bytes=64)
-        fw_sc = keep.tile([P, 2 * N], U8, name="fw_sc", align_bytes=64)
-        fw_bf = keep.tile([P, 2 * N * PACK], BF16, name="fw_bf", align_bytes=64)
+        fw_codes = ring.tile([P, 2 * N], U32, name="fw_codes", align_bytes=64)
+        fw_sc = ring.tile([P, 2 * N], U8, name="fw_sc", align_bytes=64)
+        fw_bf = ring.tile([P, 2 * N * PACK], BF16, name="fw_bf", align_bytes=64)
 
-        xg0 = ring.tile([P, PACK * M], F32, name="xg0", tag="big0", align_bytes=64)
-        xg1 = ring.tile([P, PACK * M], F32, name="xg1", tag="big1", align_bytes=64)
 
         def gather(i):
-            t = i % PACK
-            if i < PACK:
-                nc.vector.tensor_copy(xg0[:, M * t : M * (t + 1)], pages[i][:].indirect(idx3[:]))
+            if i < 6:
+                nc.vector.tensor_copy(hx[:, M * (i + 1) : M * (i + 2)], pages[i][:].indirect(idx3[:]))
                 return
             for j in range(2):
                 gather_half(i, j)
 
         def gather_half(i, j):
             t = i % PACK
-            first = 2 * M * j + HALF * t
+            first = M * (7 + j) + HALF * (t - 2)
             nc.vector.tensor_copy(
-                xg1[:, first : first + HALF], pages[i][:].indirect(idx3[:, LIST_HALF * j : LIST_HALF * (j + 1)])
+                hx[:, first : first + HALF], pages[i][:].indirect(idx3[:, LIST_HALF * j : LIST_HALF * (j + 1)])
             )
 
-        hs = [make_h(i) for i in range(4)]
+        hs = [make_h(i) for i in range(8)]
         for a in range(2):
             part = fw_bf[:, PACK * N * a : PACK * N * (a + 1)]
             nc.scalar.copy(
@@ -197,19 +211,16 @@ def tile_list_gift_interactions_kernel(
 
         x_bf = [[None, None], [None, None]]
         z_bf = [[None, None], [None, None]]
-        x_codes = [keep.tile([P, M], U32, name="x_codes%d" % a, align_bytes=64) for a in range(2)]
-        x_sc = [keep.tile([P, M], U8, name="x_sc%d" % a, align_bytes=64) for a in range(2)]
-        z_sc = [keep.tile([P, M], U8, name="z_sc%d" % a, align_bytes=64) for a in range(2)]
-        z_codes = [None, keep.tile([P, M], U32, name="z_codes1", align_bytes=64)]
-        halves = [slice(0, HALF), slice(HALF, M)]
+        x_codes = [ring.tile([P, M], U32, name="x_codes%d" % a, align_bytes=64) for a in range(2)]
+        x_sc = [ring.tile([P, M], U8, name="x_sc%d" % a, align_bytes=64) for a in range(2)]
+        z_sc = [ring.tile([P, M], U8, name="z_sc%d" % a, align_bytes=64) for a in range(2)]
+        z_codes = [None, ring.tile([P, M], U32, name="z_codes1", align_bytes=64)]
 
         def new_bf(kind, a, j):
             return ring.tile([P, PACK * HALF], BF16, name="%s_bf%d%d" % (kind, a, j), tag="%s_bf%d%d" % (kind, a if kind == "z" else 0, j), align_bytes=64)
 
         for i in range(8):
             scatter(i, hs[i])
-            if i + 4 < 8:
-                hs.append(make_h(i + 4))
             if i >= 1:
                 gather(i - 1)
                 if i + 5 < 8:
@@ -217,7 +228,7 @@ def tile_list_gift_interactions_kernel(
             if i == 2:
                 quantize(fw_codes[:], fw_sc[:], fw_bf[:])
             if i == 4:
-                planes0 = xg0[:].rearrange("p (t m) -> p t m", t=PACK)
+                planes0 = hx[:, M : 5 * M].rearrange("p (t m) -> p t m", t=PACK)
                 for j in range(2):
                     x_bf[0][j] = new_bf("x", 0, j)
                     src = planes0[:, :, halves[j]].rearrange("p t (c i) -> p c t i", i=4)
@@ -231,13 +242,14 @@ def tile_list_gift_interactions_kernel(
                     quantize(x_codes[0][:, halves[j]], x_sc[0][:, halves[j]], x_bf[0][j][:])
             if i == 6:
                 for j in range(2):
-                    src = weave(xg1[:, 2 * M * j : 2 * M * j + M], 2)
+                    src = hx[:, 5 * M : 7 * M].rearrange("p (t m) -> p t m", t=2)[:, :, halves[j]]
+                    src = src.rearrange("p t (c i) -> p c t i", i=4)
                     x_bf[1][j] = new_bf("x", 1, j)
                     nc.scalar.copy(out=woven(x_bf[1][j], 0, 2), in_=src)
                     z_bf[1][j] = new_bf("z", 1, j)
                     nc.scalar.activation(out=woven(z_bf[1][j], 0, 2), in_=src, func=SQUARE)
 
-        z_codes[0] = ring.tile([P, M], U32, name="z_codes0", tag="h3", align_bytes=64)
+        z_codes[0] = ring.tile([P, M], U32, name="z_codes0", tag="wg3", align_bytes=64)
 
         def product(acc, kind, n, a, j):
             ncols = slice(N * a + P * n, N * a + P * (n + 1))
@@ -256,7 +268,7 @@ def tile_list_gift_interactions_kernel(
                 stop=(a == 1),
             )
 
-        staged = [ring.tile([P, PACK * N], F32, name="staged%d" % j, tag="stage%d" % j) for j in range(2)]
+        staged = [keep.tile([P, PACK * N], F32, name="staged%d" % j, tag="big%d" % j, align_bytes=64) for j in range(2)]
 
         for j in range(2):
             acc_a = [psum.tile([P, HALF], F32, name="acc", tag="acc") for n in range(4)]
@@ -264,7 +276,7 @@ def tile_list_gift_interactions_kernel(
                 product(acc_a[n], "a", n, 0, j)
             gather_half(7, j)
             quantize(z_codes[0][:, halves[j]], z_sc[0][:, halves[j]], z_bf[0][j][:])
-            src = weave(xg1[:, 2 * M * j + M : 2 * M * (j + 1)], 2)
+            src = weave(hx[:, M * (7 + j) : M * (8 + j)], 2)
             nc.scalar.activation(out=woven(z_bf[1][j], 2, PACK), in_=src, func=SQUARE)
             nc.vector.tensor_copy(out=woven(x_bf[1][j], 2, PACK), in_=src)
             quantize(x_codes[1][:, halves[j]], x_sc[1][:, halves[j]], x_bf[1][j][:])
@@ -279,8 +291,12 @@ def tile_list_gift_interactions_kernel(
             for n in range(4):
                 half_sq = ring.tile([P, HALF], F32, name="half_sq", tag="half_sq", bufs=4)
                 nc.scalar.activation(out=half_sq[:], in_=acc_a[n][:], func=SQUARE, scale=0.5**0.5)
-                res = staged[j][:, HALF * n : HALF * (n + 1)]
-                nc.vector.scalar_tensor_tensor(
-                    out=res, in0=acc_b[n][:], scalar=-0.5, in1=half_sq[:], op0=MULT, op1=ADD
-                )
-                nc.sync.dma_start(out=out[P * n : P * (n + 1), halves[j]], in_=res)
+                pieces = 2 if (j, n) == (1, 3) else 1
+                width = HALF // pieces
+                for piece in range(pieces):
+                    cols = slice(width * piece, width * (piece + 1))
+                    res = staged[j][:, HALF * n : HALF * (n + 1)][:, cols]
+                    nc.vector.scalar_tensor_tensor(
+                        out=res, in0=acc_b[n][:, cols], scalar=-0.5, in1=half_sq[:, cols], op0=MULT, op1=ADD
+                    )
+                    nc.sync.dma_start(out=out[P * n : P * (n + 1), halves[j]][:, cols], in_=res)

@@ -24,6 +24,7 @@ LIST_HALF = HALF // 16
 W1_COL = S
 SQ_COL = S + H
 PLANE_W = S + H + N
+FIRST = 256
 
 
 def tile_list_gift_interactions_kernel(
@@ -46,7 +47,7 @@ def tile_list_gift_interactions_kernel(
         tab = [keep.tile([P, T], I32, name="tab%d" % k, tag="big%d" % k, align_bytes=64) for k in range(2)]
         v0 = keep.tile([P, S], U32, name="v0", align_bytes=64)
         v1 = [keep.tile([P, HALF], U32, name="v1_%d" % j, align_bytes=64) for j in range(2)]
-        wg_first = keep.tile([P, HALF], F32, name="wg_first")
+        wg_first = keep.tile([P, FIRST], F32, name="wg_first")
 
         def page_rows(i):
             a, t = divmod(i, PACK)
@@ -55,7 +56,7 @@ def tile_list_gift_interactions_kernel(
         def load_wg(dst, t, cols):
             rows = wgs.rearrange("(q t) j -> t q j", t=PACK)[t]
             for q in (0, 2, 1, 3):
-                nc.sync.dma_start(out=dst[32 * q : 32 * (q + 1), :], in_=rows[:, cols])
+                nc.sync.dma_start(out=dst[32 * q : 32 * (q + 1), cols], in_=rows[:, cols])
 
         halves = [slice(0, HALF), slice(HALF, M)]
         with tc.tile_pool(name="head", bufs=1) as head:
@@ -81,9 +82,9 @@ def tile_list_gift_interactions_kernel(
                 out=w1_raw[:].bitcast(I32).rearrange("p (k c) -> p k c", k=2),
                 in_=w1_words.bitcast(I32).rearrange("k p c -> p k c"),
             )
-            load_wg(wg_first, 0, halves[0])
-            for k in range(2):
-                nc.sync.dma_start(out=tab[k][:], in_=tab_words[k].rearrange("p c i -> p (c i)").bitcast(I32))
+            nc.sync.dma_start(out=tab[0][:], in_=tab_words[0].rearrange("p c i -> p (c i)").bitcast(I32))
+            load_wg(wg_first, 0, slice(0, FIRST))
+            nc.sync.dma_start(out=tab[1][:], in_=tab_words[1].rearrange("p c i -> p (c i)").bitcast(I32))
             nc.vector.tensor_copy(got_sc[:], tab_sc[:].indirect(idx[:]))
             nc.vector.tensor_copy(
                 out=sc_rows[:, W1_COL:SQ_COL].rearrange("p (a t m) -> p a t m", a=2, t=PACK),
@@ -102,8 +103,7 @@ def tile_list_gift_interactions_kernel(
 
         move_scales(slice(0, W1_COL + HALF), nc.gpsimd)
         ring = ctx.enter_context(tc.tile_pool(name="ring", bufs=1))
-        wg_second = ring.tile([P, HALF], F32, name="wg_second")
-        wg = [None] + [ring.tile([P, S], F32, name="wg%d" % t, tag="wg%d" % t, align_bytes=64) for t in range(1, PACK)]
+        wg = [ring.tile([P, S], F32, name="wg%d" % t, tag="wg%d" % t, align_bytes=64) for t in range(PACK)]
         hx = ring.tile([P, 9 * S], F32, name="hx")
 
         def load_page(i):
@@ -112,7 +112,7 @@ def tile_list_gift_interactions_kernel(
             return page
 
         pages = [load_page(0)]
-        load_wg(wg_second, 0, halves[1])
+        load_wg(wg[0], 0, slice(FIRST, S))
         pages.append(load_page(1))
         load_wg(wg[1], 1, slice(0, S))
         move_scales(slice(W1_COL + HALF, PLANE_W), nc.sync)
@@ -125,6 +125,7 @@ def tile_list_gift_interactions_kernel(
         load_wg(wg[2], 2, slice(0, S))
         pages.append(load_page(3))
         load_wg(wg[3], 3, slice(0, S))
+        load_wg(wg[0], 0, slice(0, FIRST))
         sq_codes = ring.tile([P, 2 * N], I32, name="sq_codes", align_bytes=64)
         nc.sync.dma_start(
             out=sq_codes[:].rearrange("p (a c) -> p a c", a=2),
@@ -159,19 +160,18 @@ def tile_list_gift_interactions_kernel(
                         start=(k == order[0]),
                         stop=(k == order[1]),
                     )
-                nc.scalar.copy(out=h[:, cols], in_=acc[:])
+                if (i, j) == (0, 0):
+                    nc.scalar.copy(out=h[:, 0:FIRST], in_=acc[:, 0:FIRST])
+                    nc.scalar.copy(out=h[:, FIRST:HALF], in_=acc[:, FIRST:HALF])
+                else:
+                    nc.scalar.copy(out=h[:, cols], in_=acc[:])
             return h
 
         def scatter(i, h):
-            pieces = 2 if i % PACK == 0 else 1
-            width = S // pieces
-            for j in range(pieces):
-                cols = slice(width * j, width * (j + 1))
+            pieces = [(0, FIRST, wg_first), (FIRST, S, wg[0])] if i == 0 else [(0, S, wg[i % PACK])]
+            for lo, hi, weights in pieces:
                 nc.vector.tensor_tensor(
-                    pages[i][:].indirect(idx2[:, width // 16 * j : width // 16 * (j + 1)]),
-                    h[:, cols],
-                    (wg_first, wg_second)[j][:] if i % PACK == 0 else wg[i % PACK][:],
-                    MULT,
+                    pages[i][:].indirect(idx2[:, lo // 16 : hi // 16]), h[:, lo:hi], weights[:, lo:hi], MULT
                 )
 
         def weave(flat, t):
@@ -189,15 +189,10 @@ def tile_list_gift_interactions_kernel(
 
 
         def gather(i):
-            if i < 6:
-                nc.vector.tensor_copy(hx[:, M * (i + 1) : M * (i + 2)], pages[i][:].indirect(idx3[:]))
-                return
-            for j in range(2):
-                gather_half(i, j)
+            nc.vector.tensor_copy(hx[:, M * (i + 1) : M * (i + 2)], pages[i][:].indirect(idx3[:]))
 
         def gather_half(i, j):
-            t = i % PACK
-            first = M * (7 + j) + HALF * (t - 2)
+            first = M * (i + 1) + HALF * j
             nc.vector.tensor_copy(
                 hx[:, first : first + HALF], pages[i][:].indirect(idx3[:, LIST_HALF * j : LIST_HALF * (j + 1)])
             )
@@ -240,14 +235,6 @@ def tile_list_gift_interactions_kernel(
             if i == 5:
                 for j in range(2):
                     quantize(x_codes[0][:, halves[j]], x_sc[0][:, halves[j]], x_bf[0][j][:])
-            if i == 6:
-                for j in range(2):
-                    src = hx[:, 5 * M : 7 * M].rearrange("p (t m) -> p t m", t=2)[:, :, halves[j]]
-                    src = src.rearrange("p t (c i) -> p c t i", i=4)
-                    x_bf[1][j] = new_bf("x", 1, j)
-                    nc.scalar.copy(out=woven(x_bf[1][j], 0, 2), in_=src)
-                    z_bf[1][j] = new_bf("z", 1, j)
-                    nc.scalar.activation(out=woven(z_bf[1][j], 0, 2), in_=src, func=SQUARE)
 
         z_codes[0] = ring.tile([P, M], U32, name="z_codes0", tag="wg3", align_bytes=64)
 
@@ -270,23 +257,25 @@ def tile_list_gift_interactions_kernel(
 
         staged = [keep.tile([P, PACK * N], F32, name="staged%d" % j, tag="big%d" % j, align_bytes=64) for j in range(2)]
 
+        planes1 = hx[:, 5 * M : 9 * M].rearrange("p (t m) -> p t m", t=PACK)
         for j in range(2):
-            acc_a = [psum.tile([P, HALF], F32, name="acc", tag="acc") for n in range(4)]
+            acc_a, acc_b = [], []
             for n in range(4):
-                product(acc_a[n], "a", n, 0, j)
+                acc_a.append(psum.tile([P, HALF], F32, name="acc", tag="acc"))
+                acc_b.append(psum.tile([P, HALF], F32, name="acc", tag="acc"))
             gather_half(7, j)
             quantize(z_codes[0][:, halves[j]], z_sc[0][:, halves[j]], z_bf[0][j][:])
-            src = weave(hx[:, M * (7 + j) : M * (8 + j)], 2)
-            nc.scalar.activation(out=woven(z_bf[1][j], 2, PACK), in_=src, func=SQUARE)
-            nc.vector.tensor_copy(out=woven(x_bf[1][j], 2, PACK), in_=src)
+            src = planes1[:, :, halves[j]].rearrange("p t (c i) -> p c t i", i=4)
+            z_bf[1][j] = new_bf("z", 1, j)
+            nc.scalar.activation(out=woven(z_bf[1][j], 0, PACK), in_=src, func=SQUARE)
+            x_bf[1][j] = new_bf("x", 1, j)
+            nc.vector.tensor_copy(out=woven(x_bf[1][j], 0, PACK), in_=src)
             quantize(x_codes[1][:, halves[j]], x_sc[1][:, halves[j]], x_bf[1][j][:])
             quantize(z_codes[1][:, halves[j]], z_sc[1][:, halves[j]], z_bf[1][j][:])
-            acc_b = [psum.tile([P, HALF], F32, name="acc", tag="acc") for n in range(4)]
             for n in range(4):
-                product(acc_b[n], "b", n, 0, j)
-            for n in range(4):
+                product(acc_a[n], "a", n, 0, j)
                 product(acc_a[n], "a", n, 1, j)
-            for n in range(4):
+                product(acc_b[n], "b", n, 0, j)
                 product(acc_b[n], "b", n, 1, j)
             for n in range(4):
                 half_sq = ring.tile([P, HALF], F32, name="half_sq", tag="half_sq", bufs=4)

@@ -115,16 +115,16 @@ def tile_list_gift_interactions_kernel(
         load_wg(wg[0], 0, slice(FIRST, S))
         pages.append(load_page(1))
         load_wg(wg[1], 1, slice(0, S))
+        pages.append(load_page(2))
+        load_wg(wg[2], 2, slice(0, S))
+        pages.append(load_page(3))
         move_scales(slice(W1_COL + HALF, PLANE_W), nc.sync)
+        load_wg(wg[3], 3, slice(0, S))
         fw_raw = [keep.tile([P, PACK * N], F32, name="fw_raw%d" % a, tag="big%d" % a, align_bytes=64) for a in range(2)]
         for a in range(2):
             nc.sync.dma_start(
                 out=fw_raw[a][:], in_=fw[HALF * a : HALF * (a + 1), :].rearrange("(p i) n -> p (i n)", i=PACK)
             )
-        pages.append(load_page(2))
-        load_wg(wg[2], 2, slice(0, S))
-        pages.append(load_page(3))
-        load_wg(wg[3], 3, slice(0, S))
         load_wg(wg[0], 0, slice(0, FIRST))
         sq_codes = ring.tile([P, 2 * N], I32, name="sq_codes", align_bytes=64)
         nc.sync.dma_start(
@@ -220,7 +220,7 @@ def tile_list_gift_interactions_kernel(
                 gather(i - 1)
                 if i + 5 < 8:
                     pages.append(load_page(i + 5))
-            if i == 2:
+            if i == 4:
                 quantize(fw_codes[:], fw_sc[:], fw_bf[:])
             if i == 4:
                 planes0 = hx[:, M : 5 * M].rearrange("p (t m) -> p t m", t=PACK)
@@ -259,10 +259,6 @@ def tile_list_gift_interactions_kernel(
 
         planes1 = hx[:, 5 * M : 9 * M].rearrange("p (t m) -> p t m", t=PACK)
         for j in range(2):
-            acc_a, acc_b = [], []
-            for n in range(4):
-                acc_a.append(psum.tile([P, HALF], F32, name="acc", tag="acc"))
-                acc_b.append(psum.tile([P, HALF], F32, name="acc", tag="acc"))
             gather_half(7, j)
             quantize(z_codes[0][:, halves[j]], z_sc[0][:, halves[j]], z_bf[0][j][:])
             src = planes1[:, :, halves[j]].rearrange("p t (c i) -> p c t i", i=4)
@@ -272,6 +268,11 @@ def tile_list_gift_interactions_kernel(
             nc.vector.tensor_copy(out=woven(x_bf[1][j], 0, PACK), in_=src)
             quantize(x_codes[1][:, halves[j]], x_sc[1][:, halves[j]], x_bf[1][j][:])
             quantize(z_codes[1][:, halves[j]], z_sc[1][:, halves[j]], z_bf[1][j][:])
+        for j in range(2):
+            acc_a, acc_b = [], []
+            for n in range(4):
+                acc_a.append(psum.tile([P, HALF], F32, name="acc", tag="acc"))
+                acc_b.append(psum.tile([P, HALF], F32, name="acc", tag="acc"))
             for n in range(4):
                 product(acc_a[n], "a", n, 0, j)
                 product(acc_a[n], "a", n, 1, j)

@@ -19,12 +19,13 @@ SQUARE = mybir.ActivationFunctionType.Square
 
 P = 128
 PACK = 4
+SLICES = 8
 HALF = 512
 LIST_HALF = HALF // 16
 W1_COL = S
-SQ_COL = S + H
-PLANE_W = S + H + N
+PLANE_W = S + H
 FIRST = 256
+PAGE_BUFS = 6
 
 
 def tile_list_gift_interactions_kernel(
@@ -34,120 +35,128 @@ def tile_list_gift_interactions_kernel(
     with ExitStack() as ctx:
         lists = ctx.enter_context(tc.tile_pool(name="lists", bufs=1))
         keep = ctx.enter_context(tc.tile_pool(name="keep", bufs=1))
-        psum = ctx.enter_context(tc.psum_pool(name="psum", bufs=8))
+        psum = ctx.enter_context(tc.psum_pool(name="psum", bufs=1))
 
         idx = lists.tile([P, S // 16], U16, name="idx")
         idx2 = lists.tile([P, S // 16], U16, name="idx2")
         idx3 = lists.tile([P, M // 16], U16, name="idx3")
 
-        sc_rows = keep.tile([P, PLANE_W], U8, name="sc_rows", align_bytes=64)
-        planes = [sc_rows, keep.tile([P, PLANE_W], U8, name="plane1", align_bytes=64)]
-        w1_raw = keep.tile([P, 2 * 2 * H], U8, name="w1_raw", align_bytes=64)
+        planes = [keep.tile([P, PLANE_W], U8, name="plane%d" % k, align_bytes=64) for k in range(2)]
         w1_perm = keep.tile([P, 2 * 2 * H], U8, name="w1_perm", align_bytes=64)
-        tab = [keep.tile([P, T], I32, name="tab%d" % k, tag="big%d" % k, align_bytes=64) for k in range(2)]
+        tab1 = keep.tile([P, T], I32, name="tab1", tag="big1", align_bytes=64)
         v0 = keep.tile([P, S], U32, name="v0", align_bytes=64)
         v1 = [keep.tile([P, HALF], U32, name="v1_%d" % j, align_bytes=64) for j in range(2)]
         wg_first = keep.tile([P, FIRST], F32, name="wg_first")
+        pages = [keep.tile([P, T2], F32, name="page0")]
 
         def page_rows(i):
             a, t = divmod(i, PACK)
             return page0[HALF * a : HALF * (a + 1), :].rearrange("(p t) c -> t p c", t=PACK)[t]
 
-        def load_wg(dst, t, cols):
+        def load_wg(queue, dst, t, cols):
             rows = wgs.rearrange("(q t) j -> t q j", t=PACK)[t]
             for q in (0, 2, 1, 3):
-                nc.sync.dma_start(out=dst[32 * q : 32 * (q + 1), cols], in_=rows[:, cols])
+                queue.dma_start(out=dst[32 * q : 32 * (q + 1), cols], in_=rows[:, cols])
 
         halves = [slice(0, HALF), slice(HALF, M)]
         with tc.tile_pool(name="head", bufs=1) as head:
             tab_sc = head.tile([P, T], U8, name="tab_sc", align_bytes=64)
             w1_sc = head.tile([P, H], U8, name="w1_sc", align_bytes=64)
             got_sc = head.tile([P, S], U8, name="got_sc", align_bytes=64)
-
-            for lo, hi in ((32, 64), (64, 128)):
-                nc.vector.memset(tab_sc[lo:hi, :].bitcast(I32), 0)
-                nc.gpsimd.memset(w1_sc[lo:hi, :].bitcast(I32), 0)
-                nc.gpsimd.memset(sc_rows[lo:hi, SQ_COL:].bitcast(I32), 0)
-            nc.gpsimd.memset(planes[1][:].bitcast(I32), 0)
+            w1_raw = head.tile([P, 2 * 2 * H], U8, name="w1_raw", align_bytes=64)
+            tab = [head.tile([P, T], I32, name="tab0", align_bytes=64), tab1]
 
             nc.sync.dma_start(idx[:], offs)
             nc.sync.dma_start(out=tab_sc[0:32, :].bitcast(I32), in_=tab_scales.rearrange("a q c -> (a q) c").bitcast(I32))
             nc.sync.dma_start(out=w1_sc[0:32, :].bitcast(I32), in_=w1_scales.rearrange("a q c -> (a q) c").bitcast(I32))
             nc.sync.dma_start(
-                out=sc_rows[0:32, SQ_COL:].bitcast(I32), in_=sq_scales.rearrange("a q c -> (a q) c").bitcast(I32)
-            )
-            nc.sync.dma_start(idx2[:], offs2)
-            nc.sync.dma_start(idx3[:], offs3)
-            nc.sync.dma_start(
                 out=w1_raw[:].bitcast(I32).rearrange("p (k c) -> p k c", k=2),
                 in_=w1_words.bitcast(I32).rearrange("k p c -> p k c"),
             )
             nc.sync.dma_start(out=tab[0][:], in_=tab_words[0].rearrange("p c i -> p (c i)").bitcast(I32))
-            load_wg(wg_first, 0, slice(0, FIRST))
             nc.sync.dma_start(out=tab[1][:], in_=tab_words[1].rearrange("p c i -> p (c i)").bitcast(I32))
+            nc.sync.dma_start(out=pages[0][:], in_=page_rows(0))
+            nc.sync.dma_start(idx2[:], offs2)
+            nc.sync.dma_start(idx3[:], offs3)
+            load_wg(nc.gpsimd, wg_first, 0, slice(0, FIRST))
+
+            for lo, hi in ((32, 64), (64, 128)):
+                nc.vector.memset(tab_sc[lo:hi, :].bitcast(I32), 0)
+            for lo, hi in ((32, 64), (64, 128)):
+                nc.vector.memset(w1_sc[lo:hi, :].bitcast(I32), 0)
+            nc.vector.memset(planes[1][:].bitcast(I32), 0)
+
             nc.vector.tensor_copy(got_sc[:], tab_sc[:].indirect(idx[:]))
             nc.vector.tensor_copy(
-                out=sc_rows[:, W1_COL:SQ_COL].rearrange("p (a t m) -> p a t m", a=2, t=PACK),
+                out=planes[0][:, W1_COL:].rearrange("p (a t m) -> p a t m", a=2, t=PACK),
                 in_=w1_sc[:].rearrange("p (a m t) -> p a t m", a=2, t=PACK),
             )
-            nc.vector.tensor_copy(out=sc_rows[:, 0:S].bitcast(I32), in_=got_sc[:].bitcast(I32))
+            nc.vector.tensor_copy(out=planes[0][:, 0:S].bitcast(I32), in_=got_sc[:].bitcast(I32))
 
-        def move_scales(cols, spare_queue):
             for k in range(2):
                 for q in range(1 - k, 4):
-                    queue = spare_queue if (k, q) == (1, 3) else nc.sync
+                    queue = nc.gpsimd if (k, q) == (1, 3) else nc.scalar
                     queue.dma_start(
-                        out=planes[k][32 * q : 32 * q + 4, cols].bitcast(I32),
-                        in_=sc_rows[16 * k + 4 * q : 16 * k + 4 * q + 4, cols].bitcast(I32),
+                        out=planes[k][32 * q : 32 * q + 4, :].bitcast(I32),
+                        in_=planes[0][16 * k + 4 * q : 16 * k + 4 * q + 4, :].bitcast(I32),
                     )
 
-        move_scales(slice(0, W1_COL + HALF), nc.gpsimd)
-        ring = ctx.enter_context(tc.tile_pool(name="ring", bufs=1))
-        wg = [ring.tile([P, S], F32, name="wg%d" % t, tag="wg%d" % t, align_bytes=64) for t in range(PACK)]
-        hx = ring.tile([P, 9 * S], F32, name="hx")
-
-        def load_page(i):
-            page = ring.tile([P, T2], F32, name="page%d" % i, tag="page", bufs=6)
-            nc.sync.dma_start(out=page[:], in_=page_rows(i))
-            return page
-
-        pages = [load_page(0)]
-        load_wg(wg[0], 0, slice(FIRST, S))
-        pages.append(load_page(1))
-        load_wg(wg[1], 1, slice(0, S))
-        pages.append(load_page(2))
-        load_wg(wg[2], 2, slice(0, S))
-        pages.append(load_page(3))
-        move_scales(slice(W1_COL + HALF, PLANE_W), nc.sync)
-        load_wg(wg[3], 3, slice(0, S))
-        fw_raw = [keep.tile([P, PACK * N], F32, name="fw_raw%d" % a, tag="big%d" % a, align_bytes=64) for a in range(2)]
-        for a in range(2):
-            nc.sync.dma_start(
-                out=fw_raw[a][:], in_=fw[HALF * a : HALF * (a + 1), :].rearrange("(p i) n -> p (i n)", i=PACK)
+            nc.vector.tensor_copy(v0[:], tab[0][:].bitcast(U32).indirect(idx[:]))
+            nc.vector.tensor_copy(
+                out=w1_perm[:].bitcast(U16).rearrange("p (g t m) -> p g t m", g=4, t=PACK),
+                in_=w1_raw[:].bitcast(U16).rearrange("p (g m t) -> p g t m", g=4, t=PACK),
             )
-        load_wg(wg[0], 0, slice(0, FIRST))
-        sq_codes = ring.tile([P, 2 * N], I32, name="sq_codes", align_bytes=64)
-        nc.sync.dma_start(
-            out=sq_codes[:].rearrange("p (a c) -> p a c", a=2),
-            in_=sq_words.rearrange("a p c i -> p a (c i)").bitcast(I32),
-        )
-        pages.extend([load_page(4), load_page(5)])
 
-        nc.vector.tensor_copy(
-            out=w1_perm[:].bitcast(U16).rearrange("p (g t m) -> p g t m", g=4, t=PACK),
-            in_=w1_raw[:].bitcast(U16).rearrange("p (g m t) -> p g t m", g=4, t=PACK),
-        )
-        nc.vector.tensor_copy(v0[:], tab[0][:].bitcast(U32).indirect(idx[:]))
         for j in range(2):
             nc.vector.tensor_copy(
                 v1[j][:], tab[1][:].bitcast(U32).indirect(idx[:, LIST_HALF * j : LIST_HALF * (j + 1)])
             )
 
+        ring = ctx.enter_context(tc.tile_pool(name="ring", bufs=1))
+        wg = [ring.tile([P, S], F32, name="wg%d" % t, tag="wg%d" % t, align_bytes=64) for t in range(PACK)]
+        hx = ring.tile([P, (SLICES + 1) * S], F32, name="hx")
+
+        def load_page(i):
+            page = ring.tile([P, T2], F32, name="page%d" % i, tag="page", bufs=PAGE_BUFS)
+            nc.sync.dma_start(out=page[:], in_=page_rows(i))
+            return page
+
+        load_wg(nc.sync, wg[0], 0, slice(FIRST, S))
+        for t in range(1, PACK):
+            pages.append(load_page(t))
+            load_wg(nc.sync, wg[t], t, slice(0, S))
+        pages.append(load_page(4))
+        fw_raw = [
+            (ring, keep)[a].tile([P, PACK * N], F32, name="fw_raw%d" % a, tag="big%d" % a, align_bytes=64) for a in range(2)
+        ]
+        for a in range(2):
+            nc.sync.dma_start(
+                out=fw_raw[a][:], in_=fw[HALF * a : HALF * (a + 1), :].rearrange("(p i) n -> p (i n)", i=PACK)
+            )
+        pages.extend([load_page(5), load_page(6)])
+        sq_codes = ring.tile([P, 2 * N], I32, name="sq_codes", align_bytes=64)
+        nc.sync.dma_start(
+            out=sq_codes[:].rearrange("p (a c) -> p a c", a=2),
+            in_=sq_words.rearrange("a p c i -> p a (c i)").bitcast(I32),
+        )
+        sq_sc = ring.tile([P, N], U8, name="sq_sc", align_bytes=64)
+        nc.vector.memset(sq_sc[:].bitcast(I32), 0)
+        for q in range(4):
+            nc.sync.dma_start(
+                out=sq_sc[32 * q : 32 * q + 8, :].bitcast(I32), in_=sq_scales[:, 4 * q : 4 * q + 4, :].bitcast(I32)
+            )
+
+        def bank(b):
+            return psum.tile([P, HALF], F32, name="bank%d" % b, tag="bank%d" % b)
+
+        def slot(s):
+            return hx[:, S * s : S * (s + 1)]
+
         def make_h(i):
-            h = hx[:, S * i : S * (i + 1)]
+            h = slot(i if i < 6 else i + 1)
             for j in range(2):
-                cols = slice(HALF * j, HALF * (j + 1))
-                acc = psum.tile([P, HALF], F32, name="acc", tag="acc")
+                cols = halves[j]
+                acc = bank((2 * i + j) % 8)
                 order = (0, 1) if (i, j) == (0, 0) else (1, 0)
                 for k in order:
                     first = 2 * (H * k + P * i)
@@ -167,126 +176,147 @@ def tile_list_gift_interactions_kernel(
                     nc.scalar.copy(out=h[:, cols], in_=acc[:])
             return h
 
-        def scatter(i, h):
+        def scatter(i):
             pieces = [(0, FIRST, wg_first), (FIRST, S, wg[0])] if i == 0 else [(0, S, wg[i % PACK])]
             for lo, hi, weights in pieces:
                 nc.vector.tensor_tensor(
-                    pages[i][:].indirect(idx2[:, lo // 16 : hi // 16]), h[:, lo:hi], weights[:, lo:hi], MULT
+                    pages[i][:].indirect(idx2[:, lo // 16 : hi // 16]), hs[i][:, lo:hi], weights[:, lo:hi], MULT
                 )
 
-        def weave(flat, t):
-            return flat.rearrange("p (t c i) -> p c t i", t=t, i=4)
+        def gather(i, lo=0, hi=M):
+            nc.vector.tensor_copy(slot(i + 1)[:, lo:hi], pages[i][:].indirect(idx3[:, lo // 16 : hi // 16]))
 
         def woven(tile, lo, hi):
             return tile[:].rearrange("p (c i t) -> p c t i", i=4, t=PACK)[:, :, lo:hi, :]
 
+        def x_rows(a, j, lo, hi):
+            rows = hx[:, M * (PACK * a + 1) : M * (PACK * a + 5)].rearrange("p (t m) -> p t m", t=PACK)
+            return rows[:, lo:hi, halves[j]].rearrange("p t (c i) -> p c t i", i=4)
+
         def quantize(codes, scales, src):
             nc.vector.quantize_mx(out=codes.bitcast(FP8X4), scales=scales, in_=src)
+
+        hs = [make_h(i) for i in range(SLICES)]
+        nc.scalar.copy(out=wg[0][:, 0:FIRST], in_=wg_first[:])
 
         fw_codes = ring.tile([P, 2 * N], U32, name="fw_codes", align_bytes=64)
         fw_sc = ring.tile([P, 2 * N], U8, name="fw_sc", align_bytes=64)
         fw_bf = ring.tile([P, 2 * N * PACK], BF16, name="fw_bf", align_bytes=64)
-
-
-        def gather(i):
-            nc.vector.tensor_copy(hx[:, M * (i + 1) : M * (i + 2)], pages[i][:].indirect(idx3[:]))
-
-        def gather_half(i, j):
-            first = M * (i + 1) + HALF * j
-            nc.vector.tensor_copy(
-                hx[:, first : first + HALF], pages[i][:].indirect(idx3[:, LIST_HALF * j : LIST_HALF * (j + 1)])
-            )
-
-        hs = [make_h(i) for i in range(8)]
         for a in range(2):
             part = fw_bf[:, PACK * N * a : PACK * N * (a + 1)]
             nc.scalar.copy(
-                out=part.rearrange("p (c i t) -> p c t i", i=4, t=PACK), in_=weave(fw_raw[a][:], PACK)
+                out=part.rearrange("p (c i t) -> p c t i", i=4, t=PACK),
+                in_=fw_raw[a][:].rearrange("p (t c i) -> p c t i", t=PACK, i=4),
             )
 
-        x_bf = [[None, None], [None, None]]
-        z_bf = [[None, None], [None, None]]
-        x_codes = [ring.tile([P, M], U32, name="x_codes%d" % a, align_bytes=64) for a in range(2)]
-        x_sc = [ring.tile([P, M], U8, name="x_sc%d" % a, align_bytes=64) for a in range(2)]
-        z_sc = [ring.tile([P, M], U8, name="z_sc%d" % a, align_bytes=64) for a in range(2)]
-        z_codes = [None, ring.tile([P, M], U32, name="z_codes1", align_bytes=64)]
+        bf = {}
+        codes = {}
+        scales = {}
+        for kind in "xz":
+            for a in range(2):
+                for j in range(2):
+                    name = "%s%d%d" % (kind, a, j)
+                    bf[kind, a, j] = ring.tile([P, PACK * HALF], BF16, name="bf_" + name, align_bytes=64)
+                    scales[kind, a, j] = ring.tile([P, HALF], U8, name="sc_" + name, align_bytes=64)
+        for j in range(2):
+            pair = ring.tile([P, M], U32, name="codes1%d" % j, align_bytes=64)
+            codes["x", 1, j], codes["z", 1, j] = pair[:, halves[0]], pair[:, halves[1]]
 
-        def new_bf(kind, a, j):
-            return ring.tile([P, PACK * HALF], BF16, name="%s_bf%d%d" % (kind, a, j), tag="%s_bf%d%d" % (kind, a if kind == "z" else 0, j), align_bytes=64)
+        def round_x(engine_copy, a, j, lo, hi):
+            engine_copy(out=woven(bf["x", a, j], lo, hi), in_=x_rows(a, j, lo, hi))
 
-        for i in range(8):
-            scatter(i, hs[i])
-            if i >= 1:
-                gather(i - 1)
-                if i + 5 < 8:
-                    pages.append(load_page(i + 5))
+        def round_z(a, j, lo, hi):
+            nc.scalar.activation(out=woven(bf["z", a, j], lo, hi), in_=x_rows(a, j, lo, hi), func=SQUARE)
+
+        def quantize_part(kind, a, j):
+            quantize(codes[kind, a, j], scales[kind, a, j][:], bf[kind, a, j][:])
+
+        def pass0_codes(j, t):
+            pair = ring.tile([P, M], U32, name="codes0%d" % j, tag="wg%d" % t, align_bytes=64)
+            codes["x", 0, j], codes["z", 0, j] = pair[:, halves[0]], pair[:, halves[1]]
+
+        scatter(0)
+        for i in range(1, 6):
+            scatter(i)
+            gather(i - 1)
+            if i == 2:
+                pages.append(load_page(7))
             if i == 4:
                 quantize(fw_codes[:], fw_sc[:], fw_bf[:])
-            if i == 4:
-                planes0 = hx[:, M : 5 * M].rearrange("p (t m) -> p t m", t=PACK)
-                for j in range(2):
-                    x_bf[0][j] = new_bf("x", 0, j)
-                    src = planes0[:, :, halves[j]].rearrange("p t (c i) -> p c t i", i=4)
-                    nc.scalar.copy(out=woven(x_bf[0][j], 0, PACK), in_=src)
-                for j in range(2):
-                    z_bf[0][j] = new_bf("z", 0, j)
-                    src = planes0[:, :, halves[j]].rearrange("p t (c i) -> p c t i", i=4)
-                    nc.scalar.activation(out=woven(z_bf[0][j], 0, PACK), in_=src, func=SQUARE)
-            if i == 5:
-                for j in range(2):
-                    quantize(x_codes[0][:, halves[j]], x_sc[0][:, halves[j]], x_bf[0][j][:])
-
-        z_codes[0] = ring.tile([P, M], U32, name="z_codes0", tag="wg3", align_bytes=64)
+                for j in (1, 0):
+                    round_x(nc.scalar.copy, 0, j, 0, PACK)
+                    round_z(0, j, 0, PACK)
+        gather(5)
+        for j in range(2):
+            round_x(nc.scalar.copy, 1, j, 0, 2)
+            round_z(1, j, 0, 2)
+        scatter(6)
+        pass0_codes(1, 2)
+        quantize_part("x", 0, 1)
+        quantize_part("z", 0, 1)
+        gather(6)
+        for j in range(2):
+            round_z(1, j, 2, 3)
+        scatter(7)
+        pass0_codes(0, 3)
 
         def product(acc, kind, n, a, j):
             ncols = slice(N * a + P * n, N * a + P * (n + 1))
-            if kind == "a":
-                lhs, lhs_sc, rhs, rhs_sc = fw_codes[:, ncols], fw_sc[:, ncols], x_codes[a], x_sc[a]
+            if kind == "x":
+                lhs, lhs_sc = fw_codes[:, ncols], fw_sc[:, ncols]
             else:
-                lhs, lhs_sc = sq_codes[:, ncols], planes[a][:, SQ_COL + P * n : SQ_COL + P * (n + 1)]
-                rhs, rhs_sc = z_codes[a], z_sc[a]
+                lhs, lhs_sc = sq_codes[:, ncols], sq_sc[4 * a : P, P * n : P * (n + 1)]
             nc.tensor.matmul_mx(
                 out=acc[:],
                 lhsT=lhs.bitcast(FP8X4),
                 lhsT_scale=lhs_sc,
-                rhs=rhs[:, halves[j]].bitcast(FP8X4),
-                rhs_scale=rhs_sc[:, halves[j]],
+                rhs=codes[kind, a, j].bitcast(FP8X4),
+                rhs_scale=scales[kind, a, j][:],
                 start=(a == 0),
                 stop=(a == 1),
             )
 
-        staged = [keep.tile([P, PACK * N], F32, name="staged%d" % j, tag="big%d" % j, align_bytes=64) for j in range(2)]
+        staged = [
+            (ring, keep)[j].tile([P, PACK * N], F32, name="staged%d" % j, tag="big%d" % j, align_bytes=64) for j in range(2)
+        ]
 
-        planes1 = hx[:, 5 * M : 9 * M].rearrange("p (t m) -> p t m", t=PACK)
+        quantize_part("x", 0, 0)
+        gather(7, 0, HALF)
+        round_z(1, 0, 3, 4)
+        quantize_part("z", 0, 0)
+        round_x(nc.vector.tensor_copy, 1, 0, 2, 4)
+        gather(7, HALF, M)
+        round_z(1, 1, 3, 4)
+        quantize_part("x", 1, 0)
+        quantize_part("z", 1, 0)
+        round_x(nc.vector.tensor_copy, 1, 1, 2, 4)
+        quantize_part("z", 1, 1)
+        quantize_part("x", 1, 1)
+
         for j in range(2):
-            gather_half(7, j)
-            quantize(z_codes[0][:, halves[j]], z_sc[0][:, halves[j]], z_bf[0][j][:])
-            src = planes1[:, :, halves[j]].rearrange("p t (c i) -> p c t i", i=4)
-            z_bf[1][j] = new_bf("z", 1, j)
-            nc.scalar.activation(out=woven(z_bf[1][j], 0, PACK), in_=src, func=SQUARE)
-            x_bf[1][j] = new_bf("x", 1, j)
-            nc.vector.tensor_copy(out=woven(x_bf[1][j], 0, PACK), in_=src)
-            quantize(x_codes[1][:, halves[j]], x_sc[1][:, halves[j]], x_bf[1][j][:])
-            quantize(z_codes[1][:, halves[j]], z_sc[1][:, halves[j]], z_bf[1][j][:])
-        for j in range(2):
-            acc_a, acc_b = [], []
-            for n in range(4):
-                acc_a.append(psum.tile([P, HALF], F32, name="acc", tag="acc"))
-                acc_b.append(psum.tile([P, HALF], F32, name="acc", tag="acc"))
-            for n in range(4):
-                product(acc_a[n], "a", n, 0, j)
-                product(acc_a[n], "a", n, 1, j)
-                product(acc_b[n], "b", n, 0, j)
-                product(acc_b[n], "b", n, 1, j)
+            acc = {}
+            for kind, first_bank in (("x", 0), ("z", 4)):
+                for n in range(4):
+                    acc[kind, n] = bank(first_bank + n)
+            if j == 0:
+                for a in range(2):
+                    for kind in "xz":
+                        for n in range(4):
+                            product(acc[kind, n], kind, n, a, j)
+            else:
+                for kind in "xz":
+                    for n in range(4):
+                        for a in range(2):
+                            product(acc[kind, n], kind, n, a, j)
             for n in range(4):
                 half_sq = ring.tile([P, HALF], F32, name="half_sq", tag="half_sq", bufs=4)
-                nc.scalar.activation(out=half_sq[:], in_=acc_a[n][:], func=SQUARE, scale=0.5**0.5)
+                nc.scalar.activation(out=half_sq[:], in_=acc["x", n][:], func=SQUARE, scale=0.5**0.5)
                 pieces = 2 if (j, n) == (1, 3) else 1
                 width = HALF // pieces
                 for piece in range(pieces):
                     cols = slice(width * piece, width * (piece + 1))
                     res = staged[j][:, HALF * n : HALF * (n + 1)][:, cols]
                     nc.vector.scalar_tensor_tensor(
-                        out=res, in0=acc_b[n][:, cols], scalar=-0.5, in1=half_sq[:, cols], op0=MULT, op1=ADD
+                        out=res, in0=acc["z", n][:, cols], scalar=-0.5, in1=half_sq[:, cols], op0=MULT, op1=ADD
                     )
                     nc.sync.dma_start(out=out[P * n : P * (n + 1), halves[j]][:, cols], in_=res)

@@ -66,40 +66,41 @@ def tile_list_gift_interactions_kernel(
             w1_raw = head.tile([P, 2 * 2 * H], U8, name="w1_raw", align_bytes=64)
             tab = [head.tile([P, T], I32, name="tab0", align_bytes=64), tab1]
 
+            nc.sync.dma_start(out=w1_sc[0:32, :].bitcast(I32), in_=w1_scales.rearrange("a q c -> (a q) c").bitcast(I32))
             nc.sync.dma_start(idx[:], offs)
             nc.sync.dma_start(out=tab_sc[0:32, :].bitcast(I32), in_=tab_scales.rearrange("a q c -> (a q) c").bitcast(I32))
-            nc.sync.dma_start(out=w1_sc[0:32, :].bitcast(I32), in_=w1_scales.rearrange("a q c -> (a q) c").bitcast(I32))
             nc.sync.dma_start(
                 out=w1_raw[:].bitcast(I32).rearrange("p (k c) -> p k c", k=2),
                 in_=w1_words.bitcast(I32).rearrange("k p c -> p k c"),
             )
             nc.sync.dma_start(out=tab[0][:], in_=tab_words[0].rearrange("p c i -> p (c i)").bitcast(I32))
             nc.sync.dma_start(out=tab[1][:], in_=tab_words[1].rearrange("p c i -> p (c i)").bitcast(I32))
-            nc.sync.dma_start(out=pages[0][:], in_=page_rows(0))
-            nc.sync.dma_start(idx2[:], offs2)
-            nc.sync.dma_start(idx3[:], offs3)
-            load_wg(nc.gpsimd, wg_first, 0, slice(0, FIRST))
 
-            for lo, hi in ((32, 64), (64, 128)):
-                nc.vector.memset(tab_sc[lo:hi, :].bitcast(I32), 0)
             for lo, hi in ((32, 64), (64, 128)):
                 nc.vector.memset(w1_sc[lo:hi, :].bitcast(I32), 0)
+            for lo, hi in ((32, 64), (64, 128)):
+                nc.vector.memset(tab_sc[lo:hi, :].bitcast(I32), 0)
             nc.vector.memset(planes[1][:].bitcast(I32), 0)
 
-            nc.vector.tensor_copy(got_sc[:], tab_sc[:].indirect(idx[:]))
             nc.vector.tensor_copy(
                 out=planes[0][:, W1_COL:].rearrange("p (a t m) -> p a t m", a=2, t=PACK),
                 in_=w1_sc[:].rearrange("p (a m t) -> p a t m", a=2, t=PACK),
             )
+            nc.vector.tensor_copy(got_sc[:], tab_sc[:].indirect(idx[:]))
             nc.vector.tensor_copy(out=planes[0][:, 0:S].bitcast(I32), in_=got_sc[:].bitcast(I32))
 
             for k in range(2):
                 for q in range(1 - k, 4):
-                    queue = nc.gpsimd if (k, q) == (1, 3) else nc.scalar
+                    queue = nc.sync if (k, q) == (1, 3) else nc.scalar
                     queue.dma_start(
                         out=planes[k][32 * q : 32 * q + 4, :].bitcast(I32),
                         in_=planes[0][16 * k + 4 * q : 16 * k + 4 * q + 4, :].bitcast(I32),
                     )
+
+            load_wg(nc.sync, wg_first, 0, slice(0, FIRST))
+            nc.sync.dma_start(idx2[:], offs2)
+            nc.sync.dma_start(out=pages[0][:], in_=page_rows(0))
+            nc.sync.dma_start(idx3[:], offs3)
 
             nc.vector.tensor_copy(v0[:], tab[0][:].bitcast(U32).indirect(idx[:]))
             nc.vector.tensor_copy(

@@ -1,6 +1,7 @@
 from contextlib import ExitStack
 
 import concourse.mybir as mybir
+from concourse.masks import make_identity
 
 K, T, S, H, T2, M, N = 1024, 4096, 1024, 1024, 2048, 1024, 512
 FLOPS = 2 * K * H * S + 2 * 2 * H * N * M
@@ -24,8 +25,8 @@ HALF = 512
 LIST_HALF = HALF // 16
 W1_COL = S
 PLANE_W = S + H
-FIRST = 256
 PAGE_BUFS = 6
+FIRST = 256
 
 
 def tile_list_gift_interactions_kernel(
@@ -43,38 +44,63 @@ def tile_list_gift_interactions_kernel(
 
         planes = [keep.tile([P, PLANE_W], U8, name="plane%d" % k, align_bytes=64) for k in range(2)]
         w1_perm = keep.tile([P, 2 * 2 * H], U8, name="w1_perm", align_bytes=64)
+        tab0 = keep.tile([P, T], I32, name="tab0", tag="big0", align_bytes=64)
         tab1 = keep.tile([P, T], I32, name="tab1", tag="big1", align_bytes=64)
+        w1_raw = keep.tile([P, 2 * 2 * H], U8, name="w1_raw", align_bytes=64)
+        wgs_raw = keep.tile([P, S], F32, name="wgs_raw")
         v0 = keep.tile([P, S], U32, name="v0", align_bytes=64)
         v1 = [keep.tile([P, HALF], U32, name="v1_%d" % j, align_bytes=64) for j in range(2)]
-        wg_first = keep.tile([P, FIRST], F32, name="wg_first")
-        pages = [keep.tile([P, T2], F32, name="page0")]
+        wg = [keep.tile([P, S], F32, name="wg%d" % t, tag="wg%d" % t, align_bytes=64) for t in range(PACK)]
 
         def page_rows(i):
             a, t = divmod(i, PACK)
             return page0[HALF * a : HALF * (a + 1), :].rearrange("(p t) c -> t p c", t=PACK)[t]
 
-        def load_wg(queue, dst, t, cols):
-            rows = wgs.rearrange("(q t) j -> t q j", t=PACK)[t]
-            for q in (0, 2, 1, 3):
-                queue.dma_start(out=dst[32 * q : 32 * (q + 1), cols], in_=rows[:, cols])
+        def bank(b):
+            return psum.tile([P, HALF], F32, name="bank%d" % b, tag="bank%d" % b)
 
         halves = [slice(0, HALF), slice(HALF, M)]
         with tc.tile_pool(name="head", bufs=1) as head:
             tab_sc = head.tile([P, T], U8, name="tab_sc", align_bytes=64)
             w1_sc = head.tile([P, H], U8, name="w1_sc", align_bytes=64)
             got_sc = head.tile([P, S], U8, name="got_sc", align_bytes=64)
-            w1_raw = head.tile([P, 2 * 2 * H], U8, name="w1_raw", align_bytes=64)
-            tab = [head.tile([P, T], I32, name="tab0", align_bytes=64), tab1]
+            ident = keep.tile([P, P], F32, name="ident")
+            make_identity(nc, ident[:])
 
             nc.sync.dma_start(out=w1_sc[0:32, :].bitcast(I32), in_=w1_scales.rearrange("a q c -> (a q) c").bitcast(I32))
             nc.sync.dma_start(idx[:], offs)
             nc.sync.dma_start(out=tab_sc[0:32, :].bitcast(I32), in_=tab_scales.rearrange("a q c -> (a q) c").bitcast(I32))
+            nc.sync.dma_start(out=wgs_raw[:], in_=wgs)
+            nc.sync.dma_start(idx2[:], offs2)
+            nc.sync.dma_start(idx3[:], offs3)
             nc.sync.dma_start(
                 out=w1_raw[:].bitcast(I32).rearrange("p (k c) -> p k c", k=2),
                 in_=w1_words.bitcast(I32).rearrange("k p c -> p k c"),
             )
-            nc.sync.dma_start(out=tab[0][:], in_=tab_words[0].rearrange("p c i -> p (c i)").bitcast(I32))
-            nc.sync.dma_start(out=tab[1][:], in_=tab_words[1].rearrange("p c i -> p (c i)").bitcast(I32))
+            nc.sync.dma_start(out=tab0[:], in_=tab_words[0].rearrange("p c i -> p (c i)").bitcast(I32))
+            nc.sync.dma_start(out=tab1[:], in_=tab_words[1].rearrange("p c i -> p (c i)").bitcast(I32))
+
+            def turn(src, b):
+                acc = bank(b)
+                for c in range(4):
+                    nc.tensor.transpose(acc[:, P * c : P * (c + 1)], src[:, P * c : P * (c + 1)], ident[:])
+                return acc
+
+            turned = [turn(wgs_raw[:, halves[j]], 6 + j) for j in range(2)]
+
+            def deal_weights(t, first_bank):
+                dealt = keep.tile([P, S], F32, name="dealt", tag="dealt", bufs=2)
+                for j in range(2):
+                    rows = turned[j][:].rearrange("p (c q t) -> p c t q", c=4, t=PACK)[:, :, t, :]
+                    nc.scalar.copy(
+                        out=dealt[:, halves[j]].rearrange("p (c g q) -> p c g q", c=4, g=4),
+                        in_=rows.unsqueeze(2).to_broadcast([P, 4, 4, 32]),
+                    )
+                for j in range(2):
+                    nc.scalar.copy(out=wg[t][:, halves[j]], in_=turn(dealt[:, halves[j]], first_bank + j)[:])
+
+            deal_weights(0, 2)
+            deal_weights(1, 4)
 
             for lo, hi in ((32, 64), (64, 128)):
                 nc.vector.memset(w1_sc[lo:hi, :].bitcast(I32), 0)
@@ -89,32 +115,15 @@ def tile_list_gift_interactions_kernel(
             nc.vector.tensor_copy(got_sc[:], tab_sc[:].indirect(idx[:]))
             nc.vector.tensor_copy(out=planes[0][:, 0:S].bitcast(I32), in_=got_sc[:].bitcast(I32))
 
-            for k in range(2):
-                for q in range(1 - k, 4):
-                    queue = nc.sync if (k, q) == (1, 3) else nc.scalar
-                    queue.dma_start(
-                        out=planes[k][32 * q : 32 * q + 4, :].bitcast(I32),
-                        in_=planes[0][16 * k + 4 * q : 16 * k + 4 * q + 4, :].bitcast(I32),
-                    )
-
-            load_wg(nc.sync, wg_first, 0, slice(0, FIRST))
-            nc.sync.dma_start(idx2[:], offs2)
-            nc.sync.dma_start(out=pages[0][:], in_=page_rows(0))
-            nc.sync.dma_start(idx3[:], offs3)
-
-            nc.vector.tensor_copy(v0[:], tab[0][:].bitcast(U32).indirect(idx[:]))
-            nc.vector.tensor_copy(
-                out=w1_perm[:].bitcast(U16).rearrange("p (g t m) -> p g t m", g=4, t=PACK),
-                in_=w1_raw[:].bitcast(U16).rearrange("p (g m t) -> p g t m", g=4, t=PACK),
-            )
-
-        for j in range(2):
-            nc.vector.tensor_copy(
-                v1[j][:], tab[1][:].bitcast(U32).indirect(idx[:, LIST_HALF * j : LIST_HALF * (j + 1)])
-            )
+        def move_scales(k):
+            for q in range(1 - k, 4):
+                queue = nc.gpsimd if (k, q) == (1, 3) else nc.sync
+                queue.dma_start(
+                    out=planes[k][32 * q : 32 * q + 4, :].bitcast(I32),
+                    in_=planes[0][16 * k + 4 * q : 16 * k + 4 * q + 4, :].bitcast(I32),
+                )
 
         ring = ctx.enter_context(tc.tile_pool(name="ring", bufs=1))
-        wg = [ring.tile([P, S], F32, name="wg%d" % t, tag="wg%d" % t, align_bytes=64) for t in range(PACK)]
         hx = ring.tile([P, (SLICES + 1) * S], F32, name="hx")
 
         def load_page(i):
@@ -122,19 +131,26 @@ def tile_list_gift_interactions_kernel(
             nc.sync.dma_start(out=page[:], in_=page_rows(i))
             return page
 
-        load_wg(nc.sync, wg[0], 0, slice(FIRST, S))
-        for t in range(1, PACK):
-            pages.append(load_page(t))
-            load_wg(nc.sync, wg[t], t, slice(0, S))
-        pages.append(load_page(4))
+        move_scales(0)
+        move_scales(1)
+        pages = [load_page(i) for i in range(5)]
+
+        nc.vector.tensor_copy(
+            out=w1_perm[:].bitcast(U16).rearrange("p (g t m) -> p g t m", g=4, t=PACK),
+            in_=w1_raw[:].bitcast(U16).rearrange("p (g m t) -> p g t m", g=4, t=PACK),
+        )
+        nc.vector.tensor_copy(v0[:], tab0[:].bitcast(U32).indirect(idx[:]))
+        for j in range(2):
+            nc.vector.tensor_copy(v1[j][:], tab1[:].bitcast(U32).indirect(idx[:, LIST_HALF * j : LIST_HALF * (j + 1)]))
+
         fw_raw = [
-            (ring, keep)[a].tile([P, PACK * N], F32, name="fw_raw%d" % a, tag="big%d" % a, align_bytes=64) for a in range(2)
+            keep.tile([P, PACK * N], F32, name="fw_raw%d" % a, tag="big%d" % a, align_bytes=64) for a in range(2)
         ]
         for a in range(2):
             nc.sync.dma_start(
                 out=fw_raw[a][:], in_=fw[HALF * a : HALF * (a + 1), :].rearrange("(p i) n -> p (i n)", i=PACK)
             )
-        pages.extend([load_page(5), load_page(6)])
+        pages.append(load_page(5))
         sq_codes = ring.tile([P, 2 * N], I32, name="sq_codes", align_bytes=64)
         nc.sync.dma_start(
             out=sq_codes[:].rearrange("p (a c) -> p a c", a=2),
@@ -147,41 +163,35 @@ def tile_list_gift_interactions_kernel(
                 out=sq_sc[32 * q : 32 * q + 8, :].bitcast(I32), in_=sq_scales[:, 4 * q : 4 * q + 4, :].bitcast(I32)
             )
 
-        def bank(b):
-            return psum.tile([P, HALF], F32, name="bank%d" % b, tag="bank%d" % b)
-
         def slot(s):
             return hx[:, S * s : S * (s + 1)]
 
         def make_h(i):
             h = slot(i if i < 6 else i + 1)
-            for j in range(2):
-                cols = halves[j]
-                acc = bank((2 * i + j) % 8)
-                order = (0, 1) if (i, j) == (0, 0) else (1, 0)
+            pieces = [(0, FIRST, 0), (FIRST, HALF, 4)] if i == 0 else [(0, HALF, (2 * i) % 8)]
+            for lo, hi, b in pieces + [(HALF, S, (2 * i + 1) % 8)]:
+                cols = slice(lo, hi)
+                j = lo // HALF
+                acc = bank(b)[:, 0 : hi - lo]
+                order = (0, 1) if (i, lo) == (0, 0) else (1, 0)
                 for k in order:
                     first = 2 * (H * k + P * i)
                     nc.tensor.matmul_mx(
-                        out=acc[:],
+                        out=acc,
                         lhsT=w1_perm[:, first : first + 2 * P].bitcast(FP4X4),
                         lhsT_scale=planes[k][:, W1_COL + P * i : W1_COL + P * (i + 1)],
-                        rhs=(v0[:, cols] if k == 0 else v1[j][:]).bitcast(FP8X4),
+                        rhs=(v0[:, cols] if k == 0 else v1[j][:, lo - HALF * j : hi - HALF * j]).bitcast(FP8X4),
                         rhs_scale=planes[k][:, cols],
                         start=(k == order[0]),
                         stop=(k == order[1]),
                     )
-                if (i, j) == (0, 0):
-                    nc.scalar.copy(out=h[:, 0:FIRST], in_=acc[:, 0:FIRST])
-                    nc.scalar.copy(out=h[:, FIRST:HALF], in_=acc[:, FIRST:HALF])
-                else:
-                    nc.scalar.copy(out=h[:, cols], in_=acc[:])
+                nc.scalar.copy(out=h[:, cols], in_=acc)
             return h
 
         def scatter(i):
-            pieces = [(0, FIRST, wg_first), (FIRST, S, wg[0])] if i == 0 else [(0, S, wg[i % PACK])]
-            for lo, hi, weights in pieces:
+            for lo, hi in [(0, FIRST), (FIRST, S)] if i == 0 else [(0, S)]:
                 nc.vector.tensor_tensor(
-                    pages[i][:].indirect(idx2[:, lo // 16 : hi // 16]), hs[i][:, lo:hi], weights[:, lo:hi], MULT
+                    pages[i][:].indirect(idx2[:, lo // 16 : hi // 16]), hs[i][:, lo:hi], wg[i % PACK][:, lo:hi], MULT
                 )
 
         def gather(i, lo=0, hi=M):
@@ -197,8 +207,10 @@ def tile_list_gift_interactions_kernel(
         def quantize(codes, scales, src):
             nc.vector.quantize_mx(out=codes.bitcast(FP8X4), scales=scales, in_=src)
 
-        hs = [make_h(i) for i in range(SLICES)]
-        nc.scalar.copy(out=wg[0][:, 0:FIRST], in_=wg_first[:])
+        hs = [make_h(0), make_h(1)]
+        deal_weights(2, 0)
+        deal_weights(3, 2)
+        hs.extend([make_h(i) for i in range(2, SLICES)])
 
         fw_codes = ring.tile([P, 2 * N], U32, name="fw_codes", align_bytes=64)
         fw_sc = ring.tile([P, 2 * N], U8, name="fw_sc", align_bytes=64)
@@ -233,15 +245,15 @@ def tile_list_gift_interactions_kernel(
             quantize(codes[kind, a, j], scales[kind, a, j][:], bf[kind, a, j][:])
 
         def pass0_codes(j, t):
-            pair = ring.tile([P, M], U32, name="codes0%d" % j, tag="wg%d" % t, align_bytes=64)
+            pair = keep.tile([P, M], U32, name="codes0%d" % j, tag="wg%d" % t, align_bytes=64)
             codes["x", 0, j], codes["z", 0, j] = pair[:, halves[0]], pair[:, halves[1]]
 
         scatter(0)
         for i in range(1, 6):
             scatter(i)
             gather(i - 1)
-            if i == 2:
-                pages.append(load_page(7))
+            if i <= 2:
+                pages.append(load_page(i + 5))
             if i == 4:
                 quantize(fw_codes[:], fw_sc[:], fw_bf[:])
                 for j in (1, 0):
@@ -278,7 +290,7 @@ def tile_list_gift_interactions_kernel(
             )
 
         staged = [
-            (ring, keep)[j].tile([P, PACK * N], F32, name="staged%d" % j, tag="big%d" % j, align_bytes=64) for j in range(2)
+            keep.tile([P, PACK * N], F32, name="staged%d" % j, tag="big%d" % j, align_bytes=64) for j in range(2)
         ]
 
         quantize_part("x", 0, 0)

@@ -45,7 +45,6 @@ def tile_list_gift_interactions_kernel(
         planes = [keep.tile([P, PLANE_W], U8, name="plane%d" % k, align_bytes=64) for k in range(2)]
         w1_perm = keep.tile([P, 2 * 2 * H], U8, name="w1_perm", align_bytes=64)
         tab0 = keep.tile([P, T], I32, name="tab0", tag="big0", align_bytes=64)
-        tab1 = keep.tile([P, T], I32, name="tab1", tag="big1", align_bytes=64)
         w1_raw = keep.tile([P, 2 * 2 * H], U8, name="w1_raw", align_bytes=64)
         wgs_raw = keep.tile([P, S], F32, name="wgs_raw")
         v0 = keep.tile([P, S], U32, name="v0", align_bytes=64)
@@ -78,7 +77,6 @@ def tile_list_gift_interactions_kernel(
                 in_=w1_words.bitcast(I32).rearrange("k p c -> p k c"),
             )
             nc.sync.dma_start(out=tab0[:], in_=tab_words[0].rearrange("p c i -> p (c i)").bitcast(I32))
-            nc.sync.dma_start(out=tab1[:], in_=tab_words[1].rearrange("p c i -> p (c i)").bitcast(I32))
 
             def turn(src, b):
                 acc = bank(b)
@@ -115,15 +113,15 @@ def tile_list_gift_interactions_kernel(
             nc.vector.tensor_copy(got_sc[:], tab_sc[:].indirect(idx[:]))
             nc.vector.tensor_copy(out=planes[0][:, 0:S].bitcast(I32), in_=got_sc[:].bitcast(I32))
 
-        def move_scales(k):
-            for q in range(1 - k, 4):
-                queue = nc.gpsimd if (k, q) == (1, 3) else nc.sync
-                queue.dma_start(
-                    out=planes[k][32 * q : 32 * q + 4, :].bitcast(I32),
-                    in_=planes[0][16 * k + 4 * q : 16 * k + 4 * q + 4, :].bitcast(I32),
+        def move_scales(k, cols):
+            for q in ((1, 2, 3), (0, 2, 1, 3))[k]:
+                nc.sync.dma_start(
+                    out=planes[k][32 * q : 32 * q + 4, cols].bitcast(I32),
+                    in_=planes[0][16 * k + 4 * q : 16 * k + 4 * q + 4, cols].bitcast(I32),
                 )
 
         ring = ctx.enter_context(tc.tile_pool(name="ring", bufs=1))
+        tab1 = ring.tile([P, T], I32, name="tab1", tag="big1", align_bytes=64)
         hx = ring.tile([P, (SLICES + 1) * S], F32, name="hx")
 
         def load_page(i):
@@ -131,9 +129,13 @@ def tile_list_gift_interactions_kernel(
             nc.sync.dma_start(out=page[:], in_=page_rows(i))
             return page
 
-        move_scales(0)
-        move_scales(1)
-        pages = [load_page(i) for i in range(5)]
+        move_scales(0, slice(0, W1_COL + P))
+        nc.sync.dma_start(out=tab1[:], in_=tab_words[1].rearrange("p c i -> p (c i)").bitcast(I32))
+        move_scales(1, slice(0, W1_COL + P))
+        pages = [load_page(0)]
+        for k in range(2):
+            move_scales(k, slice(W1_COL + P, PLANE_W))
+        pages.extend([load_page(i) for i in range(1, 5)])
 
         nc.vector.tensor_copy(
             out=w1_perm[:].bitcast(U16).rearrange("p (g t m) -> p g t m", g=4, t=PACK),
@@ -144,7 +146,7 @@ def tile_list_gift_interactions_kernel(
             nc.vector.tensor_copy(v1[j][:], tab1[:].bitcast(U32).indirect(idx[:, LIST_HALF * j : LIST_HALF * (j + 1)]))
 
         fw_raw = [
-            keep.tile([P, PACK * N], F32, name="fw_raw%d" % a, tag="big%d" % a, align_bytes=64) for a in range(2)
+            (keep, ring)[a].tile([P, PACK * N], F32, name="fw_raw%d" % a, tag="big%d" % a, align_bytes=64) for a in range(2)
         ]
         for a in range(2):
             nc.sync.dma_start(
@@ -290,7 +292,7 @@ def tile_list_gift_interactions_kernel(
             )
 
         staged = [
-            keep.tile([P, PACK * N], F32, name="staged%d" % j, tag="big%d" % j, align_bytes=64) for j in range(2)
+            (keep, ring)[j].tile([P, PACK * N], F32, name="staged%d" % j, tag="big%d" % j, align_bytes=64) for j in range(2)
         ]
 
         quantize_part("x", 0, 0)

@@ -46,7 +46,7 @@ def tile_list_gift_interactions_kernel(
         w1_perm = keep.tile([P, 2 * 2 * H], U8, name="w1_perm", align_bytes=64)
         tab0 = keep.tile([P, T], I32, name="tab0", tag="big0", align_bytes=64)
         w1_raw = keep.tile([P, 2 * 2 * H], U8, name="w1_raw", align_bytes=64)
-        wgs_raw = keep.tile([P, S], F32, name="wgs_raw")
+        wgs_raw = keep.tile([P, S], F32, name="wgs_raw", tag="dealt", bufs=2)
         v0 = keep.tile([P, S], U32, name="v0", align_bytes=64)
         v1 = [keep.tile([P, HALF], U32, name="v1_%d" % j, align_bytes=64) for j in range(2)]
         wg = [keep.tile([P, S], F32, name="wg%d" % t, tag="wg%d" % t, align_bytes=64) for t in range(PACK)]
@@ -122,7 +122,7 @@ def tile_list_gift_interactions_kernel(
 
         ring = ctx.enter_context(tc.tile_pool(name="ring", bufs=1))
         tab1 = ring.tile([P, T], I32, name="tab1", tag="big1", align_bytes=64)
-        hx = ring.tile([P, (SLICES + 1) * S], F32, name="hx")
+        xs = ring.tile([P, SLICES * M], F32, name="xs")
 
         def load_page(i):
             page = ring.tile([P, T2], F32, name="page%d" % i, tag="page", bufs=PAGE_BUFS)
@@ -135,7 +135,34 @@ def tile_list_gift_interactions_kernel(
         pages = [load_page(0)]
         for k in range(2):
             move_scales(k, slice(W1_COL + P, PLANE_W))
-        pages.extend([load_page(i) for i in range(1, 5)])
+        fw_parts = [(1, P * q, P * (q + 1)) for q in range(4)] + [(0, P * q, P * (q + 1)) for q in range(4)]
+        fw_bf = ring.tile([P, 2 * N * PACK], BF16, name="fw_bf", align_bytes=64)
+
+        def load_fw(i):
+            a, lo, hi = fw_parts[i - 1]
+            if i == SLICES - 1:
+                raw = ring.tile([P, PACK * P], F32, name="fw_late", tag="late", align_bytes=64)[:]
+            else:
+                first = M * (i - 1) + {6: M - 2 * P, SLICES: HALF - 2 * P}.get(i, 0)
+                raw = xs[:, first : first + PACK * P]
+            nc.sync.dma_start(
+                out=raw.rearrange("p (t n) -> p t n", t=PACK),
+                in_=fw[HALF * a : HALF * (a + 1), lo:hi].rearrange("(p t) n -> p t n", t=PACK),
+            )
+            return raw
+
+        def load_page_and_fw(i):
+            pages.append(load_page(i))
+            return load_fw(i)
+
+        def round_fw(i, raw):
+            a, lo, hi = fw_parts[i - 1]
+            nc.scalar.copy(
+                out=fw_bf[:, PACK * (N * a + lo) : PACK * (N * a + hi)].rearrange("p (c i t) -> p c t i", i=4, t=PACK),
+                in_=raw.rearrange("p (t c i) -> p c t i", t=PACK, i=4),
+            )
+
+        fw_raw = [load_page_and_fw(i) for i in range(1, PAGE_BUFS)]
 
         nc.vector.tensor_copy(
             out=w1_perm[:].bitcast(U16).rearrange("p (g t m) -> p g t m", g=4, t=PACK),
@@ -145,19 +172,8 @@ def tile_list_gift_interactions_kernel(
         for j in range(2):
             nc.vector.tensor_copy(v1[j][:], tab1[:].bitcast(U32).indirect(idx[:, LIST_HALF * j : LIST_HALF * (j + 1)]))
 
-        fw_raw = [
-            (keep, ring)[a].tile([P, PACK * N], F32, name="fw_raw%d" % a, tag="big%d" % a, align_bytes=64) for a in range(2)
-        ]
-        for a in range(2):
-            nc.sync.dma_start(
-                out=fw_raw[a][:], in_=fw[HALF * a : HALF * (a + 1), :].rearrange("(p i) n -> p (i n)", i=PACK)
-            )
-        pages.append(load_page(5))
+        h_rows = [(keep, ring)[a].tile([P, PACK * S], F32, name="h%d" % a, tag="big%d" % a, align_bytes=64) for a in range(2)]
         sq_codes = ring.tile([P, 2 * N], I32, name="sq_codes", align_bytes=64)
-        nc.sync.dma_start(
-            out=sq_codes[:].rearrange("p (a c) -> p a c", a=2),
-            in_=sq_words.rearrange("a p c i -> p a (c i)").bitcast(I32),
-        )
         sq_sc = ring.tile([P, N], U8, name="sq_sc", align_bytes=64)
         nc.vector.memset(sq_sc[:].bitcast(I32), 0)
         for q in range(4):
@@ -166,10 +182,10 @@ def tile_list_gift_interactions_kernel(
             )
 
         def slot(s):
-            return hx[:, S * s : S * (s + 1)]
+            return xs[:, M * s : M * (s + 1)]
 
         def make_h(i):
-            h = slot(i if i < 6 else i + 1)
+            h = h_rows[i // PACK][:, S * (i % PACK) : S * (i % PACK + 1)]
             pieces = [(0, FIRST, 0), (FIRST, HALF, 4)] if i == 0 else [(0, HALF, (2 * i) % 8)]
             for lo, hi, b in pieces + [(HALF, S, (2 * i + 1) % 8)]:
                 cols = slice(lo, hi)
@@ -197,14 +213,16 @@ def tile_list_gift_interactions_kernel(
                 )
 
         def gather(i, lo=0, hi=M):
-            nc.vector.tensor_copy(slot(i + 1)[:, lo:hi], pages[i][:].indirect(idx3[:, lo // 16 : hi // 16]))
+            nc.vector.tensor_copy(slot(i)[:, lo:hi], pages[i][:].indirect(idx3[:, lo // 16 : hi // 16]))
 
-        def woven(tile, lo, hi):
-            return tile[:].rearrange("p (c i t) -> p c t i", i=4, t=PACK)[:, :, lo:hi, :]
+        def woven(tile, lo, hi, first, width):
+            part = tile[:, PACK * first : PACK * (first + width)]
+            return part.rearrange("p (c i t) -> p c t i", i=4, t=PACK)[:, :, lo:hi, :]
 
-        def x_rows(a, j, lo, hi):
-            rows = hx[:, M * (PACK * a + 1) : M * (PACK * a + 5)].rearrange("p (t m) -> p t m", t=PACK)
-            return rows[:, lo:hi, halves[j]].rearrange("p t (c i) -> p c t i", i=4)
+        def x_rows(a, j, lo, hi, first, width):
+            rows = xs[:, M * PACK * a : M * PACK * (a + 1)].rearrange("p (t m) -> p t m", t=PACK)
+            cols = slice(HALF * j + first, HALF * j + first + width)
+            return rows[:, lo:hi, cols].rearrange("p t (c i) -> p c t i", i=4)
 
         def quantize(codes, scales, src):
             nc.vector.quantize_mx(out=codes.bitcast(FP8X4), scales=scales, in_=src)
@@ -216,13 +234,8 @@ def tile_list_gift_interactions_kernel(
 
         fw_codes = ring.tile([P, 2 * N], U32, name="fw_codes", align_bytes=64)
         fw_sc = ring.tile([P, 2 * N], U8, name="fw_sc", align_bytes=64)
-        fw_bf = ring.tile([P, 2 * N * PACK], BF16, name="fw_bf", align_bytes=64)
-        for a in range(2):
-            part = fw_bf[:, PACK * N * a : PACK * N * (a + 1)]
-            nc.scalar.copy(
-                out=part.rearrange("p (c i t) -> p c t i", i=4, t=PACK),
-                in_=fw_raw[a][:].rearrange("p (t c i) -> p c t i", t=PACK, i=4),
-            )
+        for i in range(1, PAGE_BUFS):
+            round_fw(i, fw_raw[i - 1])
 
         bf = {}
         codes = {}
@@ -231,49 +244,64 @@ def tile_list_gift_interactions_kernel(
             for a in range(2):
                 for j in range(2):
                     name = "%s%d%d" % (kind, a, j)
-                    bf[kind, a, j] = ring.tile([P, PACK * HALF], BF16, name="bf_" + name, align_bytes=64)
-                    scales[kind, a, j] = ring.tile([P, HALF], U8, name="sc_" + name, align_bytes=64)
+                    if a == 1:
+                        bf[kind, a, j] = ring.tile([P, PACK * HALF], BF16, name="bf_" + name, align_bytes=64)[:]
+                        scales[kind, a, j] = ring.tile([P, HALF], U8, name="sc_" + name, align_bytes=64)[:]
+        bf0 = [ring.tile([P, 2 * PACK * HALF], BF16, name="bf0%d" % j, align_bytes=64) for j in range(2)]
+        sc0 = [ring.tile([P, M], U8, name="sc0%d" % j, align_bytes=64) for j in range(2)]
+        for j in range(2):
+            for u, kind in enumerate("xz"):
+                bf[kind, 0, j] = bf0[j][:, PACK * HALF * u : PACK * HALF * (u + 1)]
+                scales[kind, 0, j] = sc0[j][:, halves[u]]
         for j in range(2):
             pair = ring.tile([P, M], U32, name="codes1%d" % j, align_bytes=64)
             codes["x", 1, j], codes["z", 1, j] = pair[:, halves[0]], pair[:, halves[1]]
 
-        def round_x(engine_copy, a, j, lo, hi):
-            engine_copy(out=woven(bf["x", a, j], lo, hi), in_=x_rows(a, j, lo, hi))
+        def round_x(engine_copy, a, j, lo, hi, first=0, width=HALF):
+            engine_copy(out=woven(bf["x", a, j], lo, hi, first, width), in_=x_rows(a, j, lo, hi, first, width))
 
-        def round_z(a, j, lo, hi):
-            nc.scalar.activation(out=woven(bf["z", a, j], lo, hi), in_=x_rows(a, j, lo, hi), func=SQUARE)
+        def round_z(a, j, lo, hi, first=0, width=HALF):
+            nc.scalar.activation(
+                out=woven(bf["z", a, j], lo, hi, first, width), in_=x_rows(a, j, lo, hi, first, width), func=SQUARE
+            )
 
         def quantize_part(kind, a, j):
-            quantize(codes[kind, a, j], scales[kind, a, j][:], bf[kind, a, j][:])
+            quantize(codes[kind, a, j], scales[kind, a, j], bf[kind, a, j])
 
-        def pass0_codes(j, t):
-            pair = keep.tile([P, M], U32, name="codes0%d" % j, tag="wg%d" % t, align_bytes=64)
-            codes["x", 0, j], codes["z", 0, j] = pair[:, halves[0]], pair[:, halves[1]]
+        pass0 = [ring.tile([P, M], U32, name="codes0%d" % j, align_bytes=64) for j in range(2)]
+        for j in range(2):
+            codes["x", 0, j], codes["z", 0, j] = pass0[j][:, halves[0]], pass0[j][:, halves[1]]
 
         scatter(0)
-        for i in range(1, 6):
+        for i in range(1, SLICES - 1):
             scatter(i)
             gather(i - 1)
             if i <= 2:
-                pages.append(load_page(i + 5))
+                round_fw(i + 5, load_page_and_fw(i + 5))
+            if i == 2:
+                round_fw(SLICES, load_fw(SLICES))
+            if i == 1:
+                nc.sync.dma_start(
+                    out=sq_codes[:].rearrange("p (a c) -> p a c", a=2),
+                    in_=sq_words.rearrange("a p c i -> p a (c i)").bitcast(I32),
+                )
             if i == 4:
-                quantize(fw_codes[:], fw_sc[:], fw_bf[:])
+                quantize(fw_codes[:, N:], fw_sc[:, N:], fw_bf[:, PACK * N :])
                 for j in (1, 0):
-                    round_x(nc.scalar.copy, 0, j, 0, PACK)
-                    round_z(0, j, 0, PACK)
-        gather(5)
+                    for first in range(0, HALF, P):
+                        round_x(nc.scalar.copy, 0, j, 0, PACK, first, P)
+                        round_z(0, j, 0, PACK, first, P)
+            if i == 5:
+                quantize_part("x", 0, 0)
+                quantize(pass0[1][:], sc0[1][:], bf0[1][:])
         for j in range(2):
             round_x(nc.scalar.copy, 1, j, 0, 2)
-            round_z(1, j, 0, 2)
-        scatter(6)
-        pass0_codes(1, 2)
-        quantize_part("x", 0, 1)
-        quantize_part("z", 0, 1)
         gather(6)
         for j in range(2):
-            round_z(1, j, 2, 3)
+            round_z(1, j, 0, 3)
         scatter(7)
-        pass0_codes(0, 3)
+        codes["z", 0, 0] = ring.tile([P, HALF], U32, name="codes_z00", tag="late", align_bytes=64)[:]
+        quantize_part("z", 0, 0)
 
         def product(acc, kind, n, a, j):
             ncols = slice(N * a + P * n, N * a + P * (n + 1))
@@ -286,7 +314,7 @@ def tile_list_gift_interactions_kernel(
                 lhsT=lhs.bitcast(FP8X4),
                 lhsT_scale=lhs_sc,
                 rhs=codes[kind, a, j].bitcast(FP8X4),
-                rhs_scale=scales[kind, a, j][:],
+                rhs_scale=scales[kind, a, j],
                 start=(a == 0),
                 stop=(a == 1),
             )
@@ -295,10 +323,9 @@ def tile_list_gift_interactions_kernel(
             (keep, ring)[j].tile([P, PACK * N], F32, name="staged%d" % j, tag="big%d" % j, align_bytes=64) for j in range(2)
         ]
 
-        quantize_part("x", 0, 0)
         gather(7, 0, HALF)
         round_z(1, 0, 3, 4)
-        quantize_part("z", 0, 0)
+        quantize(fw_codes[:, :N], fw_sc[:, :N], fw_bf[:, : PACK * N])
         round_x(nc.vector.tensor_copy, 1, 0, 2, 4)
         gather(7, HALF, M)
         round_z(1, 1, 3, 4)
@@ -315,14 +342,16 @@ def tile_list_gift_interactions_kernel(
                     acc[kind, n] = bank(first_bank + n)
             if j == 0:
                 for a in range(2):
-                    for kind in "xz":
+                    for kind in ("zx", "xz")[a]:
                         for n in range(4):
                             product(acc[kind, n], kind, n, a, j)
             else:
-                for kind in "xz":
-                    for n in range(4):
-                        for a in range(2):
-                            product(acc[kind, n], kind, n, a, j)
+                for a in range(2):
+                    for n in range(2):
+                        product(acc["x", n], "x", n, a, j)
+                for kind, n in (("x", 2), ("z", 0), ("x", 3), ("z", 1), ("z", 2), ("z", 3)):
+                    for a in range(2):
+                        product(acc[kind, n], kind, n, a, j)
             for n in range(4):
                 half_sq = ring.tile([P, HALF], F32, name="half_sq", tag="half_sq", bufs=4)
                 nc.scalar.activation(out=half_sq[:], in_=acc["x", n][:], func=SQUARE, scale=0.5**0.5)

@@ -23,10 +23,12 @@ PACK = 4
 SLICES = 8
 HALF = 512
 LIST_HALF = HALF // 16
-W1_COL = S
+W1_COL = HALF
+V_COL = (0, HALF + H)
 PLANE_W = S + H
+EARLY_W = W1_COL + 2 * P
 PAGE_BUFS = 6
-FIRST = 256
+FIRST = 384
 
 
 def tile_list_gift_interactions_kernel(
@@ -107,11 +109,14 @@ def tile_list_gift_interactions_kernel(
             nc.vector.memset(planes[1][:].bitcast(I32), 0)
 
             nc.vector.tensor_copy(
-                out=planes[0][:, W1_COL:].rearrange("p (a t m) -> p a t m", a=2, t=PACK),
+                out=planes[0][:, W1_COL : W1_COL + H].rearrange("p (a t m) -> p a t m", a=2, t=PACK),
                 in_=w1_sc[:].rearrange("p (a m t) -> p a t m", a=2, t=PACK),
             )
             nc.vector.tensor_copy(got_sc[:], tab_sc[:].indirect(idx[:]))
-            nc.vector.tensor_copy(out=planes[0][:, 0:S].bitcast(I32), in_=got_sc[:].bitcast(I32))
+            nc.vector.tensor_copy(
+                out=planes[0][:].bitcast(I32).rearrange("p (u w) -> p u w", u=4)[:, 0:4:3, :],
+                in_=got_sc[:].bitcast(I32).rearrange("p (u w) -> p u w", u=2),
+            )
 
         def move_scales(k, cols):
             for q in ((1, 2, 3), (0, 2, 1, 3))[k]:
@@ -122,29 +127,33 @@ def tile_list_gift_interactions_kernel(
 
         ring = ctx.enter_context(tc.tile_pool(name="ring", bufs=1))
         tab1 = ring.tile([P, T], I32, name="tab1", tag="big1", align_bytes=64)
-        xs = ring.tile([P, SLICES * M], F32, name="xs")
+        xs = [ring.tile([P, PACK * M], F32, name="xs0", offset=0), ring.tile([P, PACK * M], F32, name="xs1")]
 
         def load_page(i):
-            page = ring.tile([P, T2], F32, name="page%d" % i, tag="page", bufs=PAGE_BUFS)
+            if i == SLICES - 1:
+                page = ring.tile([P, T2], F32, name="page7", offset=0)
+            else:
+                page = ring.tile([P, T2], F32, name="page%d" % i, tag="page", bufs=PAGE_BUFS)
             nc.sync.dma_start(out=page[:], in_=page_rows(i))
             return page
 
-        move_scales(0, slice(0, W1_COL + P))
+        move_scales(0, slice(0, EARLY_W))
         nc.sync.dma_start(out=tab1[:], in_=tab_words[1].rearrange("p c i -> p (c i)").bitcast(I32))
-        move_scales(1, slice(0, W1_COL + P))
+        move_scales(1, slice(0, EARLY_W))
         pages = [load_page(0)]
-        for k in range(2):
-            move_scales(k, slice(W1_COL + P, PLANE_W))
-        fw_parts = [(1, P * q, P * (q + 1)) for q in range(4)] + [(0, P * q, P * (q + 1)) for q in range(4)]
+        fw_parts = [(1, P * q, P * (q + 1)) for q in range(4)] + [(0, 0, P), (0, P, 2 * P), (0, 2 * P, N - 64), (0, N - 64, N)]
         fw_bf = ring.tile([P, 2 * N * PACK], BF16, name="fw_bf", align_bytes=64)
 
         def load_fw(i):
             a, lo, hi = fw_parts[i - 1]
-            if i == SLICES - 1:
-                raw = ring.tile([P, PACK * P], F32, name="fw_late", tag="late", align_bytes=64)[:]
+            width = PACK * (hi - lo)
+            if i == 6:
+                raw = ring.tile([P, width], F32, name="fw_part6", tag="held6", align_bytes=64)[:]
+            elif i == SLICES:
+                raw = ring.tile([P, width], F32, name="fw_part8", offset=4 * T2)[:]
             else:
-                first = M * (i - 1) + {6: M - 2 * P, SLICES: HALF - 2 * P}.get(i, 0)
-                raw = xs[:, first : first + PACK * P]
+                first = 5 * M - width // 2 if i == 5 else M * (i - 1)
+                raw = xs[first // (PACK * M)][:, first % (PACK * M) : first % (PACK * M) + width]
             nc.sync.dma_start(
                 out=raw.rearrange("p (t n) -> p t n", t=PACK),
                 in_=fw[HALF * a : HALF * (a + 1), lo:hi].rearrange("(p t) n -> p t n", t=PACK),
@@ -162,7 +171,10 @@ def tile_list_gift_interactions_kernel(
                 in_=raw.rearrange("p (t c i) -> p c t i", t=PACK, i=4),
             )
 
-        fw_raw = [load_page_and_fw(i) for i in range(1, PAGE_BUFS)]
+        pages.append(load_page(1))
+        for k in range(2):
+            move_scales(k, slice(EARLY_W, PLANE_W))
+        fw_raw = [load_fw(1)] + [load_page_and_fw(i) for i in range(2, PAGE_BUFS)]
 
         nc.vector.tensor_copy(
             out=w1_perm[:].bitcast(U16).rearrange("p (g t m) -> p g t m", g=4, t=PACK),
@@ -182,35 +194,33 @@ def tile_list_gift_interactions_kernel(
             )
 
         def slot(s):
-            return xs[:, M * s : M * (s + 1)]
+            return xs[s // PACK][:, M * (s % PACK) : M * (s % PACK + 1)]
 
-        def make_h(i):
-            h = h_rows[i // PACK][:, S * (i % PACK) : S * (i % PACK + 1)]
-            pieces = [(0, FIRST, 0), (FIRST, HALF, 4)] if i == 0 else [(0, HALF, (2 * i) % 8)]
-            for lo, hi, b in pieces + [(HALF, S, (2 * i + 1) % 8)]:
-                cols = slice(lo, hi)
-                j = lo // HALF
-                acc = bank(b)[:, 0 : hi - lo]
-                order = (0, 1) if (i, lo) == (0, 0) else (1, 0)
-                for k in order:
-                    first = 2 * (H * k + P * i)
-                    nc.tensor.matmul_mx(
-                        out=acc,
-                        lhsT=w1_perm[:, first : first + 2 * P].bitcast(FP4X4),
-                        lhsT_scale=planes[k][:, W1_COL + P * i : W1_COL + P * (i + 1)],
-                        rhs=(v0[:, cols] if k == 0 else v1[j][:, lo - HALF * j : hi - HALF * j]).bitcast(FP8X4),
-                        rhs_scale=planes[k][:, cols],
-                        start=(k == order[0]),
-                        stop=(k == order[1]),
-                    )
-                nc.scalar.copy(out=h[:, cols], in_=acc)
-            return h
+        def h_of(i):
+            return h_rows[i // PACK][:, S * (i % PACK) : S * (i % PACK + 1)]
 
-        def scatter(i):
-            for lo, hi in [(0, FIRST), (FIRST, S)] if i == 0 else [(0, S)]:
-                nc.vector.tensor_tensor(
-                    pages[i][:].indirect(idx2[:, lo // 16 : hi // 16]), hs[i][:, lo:hi], wg[i % PACK][:, lo:hi], MULT
+        def make_h(i, lo, hi, b):
+            j, first_col = divmod(lo, HALF)
+            width = hi - lo
+            acc = bank(b)[:, 0:width]
+            order = (0, 1) if i < 2 and j == 0 else (1, 0)
+            for k in order:
+                first = 2 * (H * k + P * i)
+                nc.tensor.matmul_mx(
+                    out=acc,
+                    lhsT=w1_perm[:, first : first + 2 * P].bitcast(FP4X4),
+                    lhsT_scale=planes[k][:, W1_COL + P * i : W1_COL + P * (i + 1)],
+                    rhs=(v0[:, lo:hi] if k == 0 else v1[j][:, first_col : first_col + width]).bitcast(FP8X4),
+                    rhs_scale=planes[k][:, V_COL[j] + first_col : V_COL[j] + first_col + width],
+                    start=(k == order[0]),
+                    stop=(k == order[1]),
                 )
+            nc.scalar.copy(out=h_of(i)[:, lo:hi], in_=acc)
+
+        def scatter(i, lo=0, hi=S):
+            nc.vector.tensor_tensor(
+                pages[i][:].indirect(idx2[:, lo // 16 : hi // 16]), h_of(i)[:, lo:hi], wg[i % PACK][:, lo:hi], MULT
+            )
 
         def gather(i, lo=0, hi=M):
             nc.vector.tensor_copy(slot(i)[:, lo:hi], pages[i][:].indirect(idx3[:, lo // 16 : hi // 16]))
@@ -220,17 +230,23 @@ def tile_list_gift_interactions_kernel(
             return part.rearrange("p (c i t) -> p c t i", i=4, t=PACK)[:, :, lo:hi, :]
 
         def x_rows(a, j, lo, hi, first, width):
-            rows = xs[:, M * PACK * a : M * PACK * (a + 1)].rearrange("p (t m) -> p t m", t=PACK)
+            rows = xs[a][:].rearrange("p (t m) -> p t m", t=PACK)
             cols = slice(HALF * j + first, HALF * j + first + width)
             return rows[:, lo:hi, cols].rearrange("p t (c i) -> p c t i", i=4)
 
         def quantize(codes, scales, src):
             nc.vector.quantize_mx(out=codes.bitcast(FP8X4), scales=scales, in_=src)
 
-        hs = [make_h(0), make_h(1)]
+        for b, (lo, hi) in enumerate(((0, 256), (256, FIRST), (FIRST, HALF))):
+            make_h(0, lo, hi, (0, 1, 4)[b])
+        make_h(1, 0, HALF, 5)
+        for i in range(2):
+            make_h(i, HALF, S, 2 + i)
         deal_weights(2, 0)
         deal_weights(3, 2)
-        hs.extend([make_h(i) for i in range(2, SLICES)])
+        for i in range(2, SLICES):
+            for j in range(2):
+                make_h(i, HALF * j, HALF * (j + 1), (2 * i + j) % 8)
 
         fw_codes = ring.tile([P, 2 * N], U32, name="fw_codes", align_bytes=64)
         fw_sc = ring.tile([P, 2 * N], U8, name="fw_sc", align_bytes=64)
@@ -268,39 +284,49 @@ def tile_list_gift_interactions_kernel(
         def quantize_part(kind, a, j):
             quantize(codes[kind, a, j], scales[kind, a, j], bf[kind, a, j])
 
-        pass0 = [ring.tile([P, M], U32, name="codes0%d" % j, align_bytes=64) for j in range(2)]
-        for j in range(2):
-            codes["x", 0, j], codes["z", 0, j] = pass0[j][:, halves[0]], pass0[j][:, halves[1]]
+        codes["x", 0, 0] = ring.tile([P, HALF], U32, name="codes_x00", align_bytes=64)[:]
 
-        scatter(0)
-        for i in range(1, SLICES - 1):
-            scatter(i)
+        scatter(0, 0, FIRST)
+        scatter(1, 0, HALF)
+        scatter(0, FIRST, S)
+        scatter(1, HALF, S)
+        for i in range(1, 6):
+            if i > 1:
+                scatter(i)
             gather(i - 1)
-            if i <= 2:
-                round_fw(i + 5, load_page_and_fw(i + 5))
-            if i == 2:
-                round_fw(SLICES, load_fw(SLICES))
             if i == 1:
+                pages.append(load_page(6))
+                round_fw(6, load_fw(6))
+                round_fw(7, load_fw(7))
                 nc.sync.dma_start(
                     out=sq_codes[:].rearrange("p (a c) -> p a c", a=2),
                     in_=sq_words.rearrange("a p c i -> p a (c i)").bitcast(I32),
                 )
             if i == 4:
                 quantize(fw_codes[:, N:], fw_sc[:, N:], fw_bf[:, PACK * N :])
-                for j in (1, 0):
+                for j in range(2):
                     for first in range(0, HALF, P):
                         round_x(nc.scalar.copy, 0, j, 0, PACK, first, P)
+                for j in (1, 0):
+                    for first in range(0, HALF, P):
                         round_z(0, j, 0, PACK, first, P)
-            if i == 5:
-                quantize_part("x", 0, 0)
-                quantize(pass0[1][:], sc0[1][:], bf0[1][:])
+        pages.append(load_page(7))
+        round_fw(8, load_fw(8))
+        gather(5)
+        quantize_part("x", 0, 0)
         for j in range(2):
-            round_x(nc.scalar.copy, 1, j, 0, 2)
+            for first in range(0, HALF, 2 * P):
+                round_x(nc.scalar.copy, 1, j, 0, 2, first, 2 * P)
+                round_z(1, j, 0, 2, first, 2 * P)
+        scatter(6)
+        pair = ring.tile([P, M], U32, name="codes01", tag="held6", align_bytes=64)
+        codes["x", 0, 1], codes["z", 0, 1] = pair[:, halves[0]], pair[:, halves[1]]
+        quantize(pair[:], sc0[1][:], bf0[1][:])
         gather(6)
         for j in range(2):
-            round_z(1, j, 0, 3)
+            round_z(1, j, 2, 3)
         scatter(7)
-        codes["z", 0, 0] = ring.tile([P, HALF], U32, name="codes_z00", tag="late", align_bytes=64)[:]
+        codes["z", 0, 0] = ring.tile([P, HALF], U32, name="codes_z00", offset=4 * T2, align_bytes=64)[:]
         quantize_part("z", 0, 0)
 
         def product(acc, kind, n, a, j):

@@ -63,7 +63,7 @@ def tile_list_gift_interactions_kernel(
         halves = [slice(0, HALF), slice(HALF, M)]
         with tc.tile_pool(name="head", bufs=1) as head:
             tab_sc = head.tile([P, T], U8, name="tab_sc", align_bytes=64)
-            w1_sc = head.tile([P, H], U8, name="w1_sc", align_bytes=64)
+            w1_sc = keep.tile([P, H], U8, name="w1_sc", align_bytes=64)
             got_sc = head.tile([P, S], U8, name="got_sc", align_bytes=64)
             ident = keep.tile([P, P], F32, name="ident")
             make_identity(nc, ident[:])
@@ -108,15 +108,17 @@ def tile_list_gift_interactions_kernel(
                 nc.vector.memset(tab_sc[lo:hi, :].bitcast(I32), 0)
             nc.vector.memset(planes[1][:].bitcast(I32), 0)
 
-            nc.vector.tensor_copy(
-                out=planes[0][:, W1_COL : W1_COL + H].rearrange("p (a t m) -> p a t m", a=2, t=PACK),
-                in_=w1_sc[:].rearrange("p (a m t) -> p a t m", a=2, t=PACK),
-            )
+            dealt_sc = planes[0][:, W1_COL : W1_COL + H].rearrange("p (a t m) -> p a t m", a=2, t=PACK)
+            given_sc = w1_sc[:].rearrange("p (a m t) -> p a t m", a=2, t=PACK)
+            nc.vector.tensor_copy(out=dealt_sc[:, 0, 0:2, :], in_=given_sc[:, 0, 0:2, :])
             nc.vector.tensor_copy(got_sc[:], tab_sc[:].indirect(idx[:]))
             nc.vector.tensor_copy(
                 out=planes[0][:].bitcast(I32).rearrange("p (u w) -> p u w", u=4)[:, 0:4:3, :],
                 in_=got_sc[:].bitcast(I32).rearrange("p (u w) -> p u w", u=2),
             )
+
+        nc.vector.tensor_copy(out=dealt_sc[:, 0, 2:4, :], in_=given_sc[:, 0, 2:4, :])
+        nc.vector.tensor_copy(out=dealt_sc[:, 1, :, :], in_=given_sc[:, 1, :, :])
 
         def move_scales(k, cols):
             for q in ((1, 2, 3), (0, 2, 1, 3))[k]:
@@ -150,7 +152,7 @@ def tile_list_gift_interactions_kernel(
             if i == 6:
                 raw = ring.tile([P, width], F32, name="fw_part6", tag="held6", align_bytes=64)[:]
             elif i == SLICES:
-                raw = ring.tile([P, width], F32, name="fw_part8", offset=4 * T2)[:]
+                raw = ring.tile([P, width], F32, name="fw_part8", offset=6 * T2 - 512)[:]
             else:
                 first = 5 * M - width // 2 if i == 5 else M * (i - 1)
                 raw = xs[first // (PACK * M)][:, first % (PACK * M) : first % (PACK * M) + width]
@@ -222,8 +224,9 @@ def tile_list_gift_interactions_kernel(
                 pages[i][:].indirect(idx2[:, lo // 16 : hi // 16]), h_of(i)[:, lo:hi], wg[i % PACK][:, lo:hi], MULT
             )
 
-        def gather(i, lo=0, hi=M):
-            nc.vector.tensor_copy(slot(i)[:, lo:hi], pages[i][:].indirect(idx3[:, lo // 16 : hi // 16]))
+        def gather(i, lo=0, hi=M, into=None):
+            into = slot(i)[:, lo:hi] if into is None else into
+            nc.vector.tensor_copy(into, pages[i][:].indirect(idx3[:, lo // 16 : hi // 16]))
 
         def woven(tile, lo, hi, first, width):
             part = tile[:, PACK * first : PACK * (first + width)]
@@ -322,11 +325,10 @@ def tile_list_gift_interactions_kernel(
         pair = ring.tile([P, M], U32, name="codes01", tag="held6", align_bytes=64)
         codes["x", 0, 1], codes["z", 0, 1] = pair[:, halves[0]], pair[:, halves[1]]
         quantize(pair[:], sc0[1][:], bf0[1][:])
-        gather(6)
-        for j in range(2):
-            round_z(1, j, 2, 3)
+        gather(6, 0, HALF)
+        round_z(1, 0, 2, 3)
         scatter(7)
-        codes["z", 0, 0] = ring.tile([P, HALF], U32, name="codes_z00", offset=4 * T2, align_bytes=64)[:]
+        codes["z", 0, 0] = ring.tile([P, HALF], U32, name="codes_z00", offset=6 * T2, align_bytes=64)[:]
         quantize_part("z", 0, 0)
 
         def product(acc, kind, n, a, j):
@@ -349,44 +351,55 @@ def tile_list_gift_interactions_kernel(
             (keep, ring)[j].tile([P, PACK * N], F32, name="staged%d" % j, tag="big%d" % j, align_bytes=64) for j in range(2)
         ]
 
+        late_x = ring.tile([P, M], F32, name="late_x", offset=4 * T2)
+        late_rows = late_x[:].rearrange("p (t c i) -> p c t i", t=2, i=4)
         gather(7, 0, HALF)
         round_z(1, 0, 3, 4)
         quantize(fw_codes[:, :N], fw_sc[:, :N], fw_bf[:, : PACK * N])
         round_x(nc.vector.tensor_copy, 1, 0, 2, 4)
-        gather(7, HALF, M)
-        round_z(1, 1, 3, 4)
+        gather(6, HALF, M, late_x[:, halves[0]])
         quantize_part("x", 1, 0)
         quantize_part("z", 1, 0)
-        round_x(nc.vector.tensor_copy, 1, 1, 2, 4)
-        quantize_part("z", 1, 1)
-        quantize_part("x", 1, 1)
+        gather(7, HALF, M, late_x[:, halves[1]])
+        nc.scalar.activation(out=woven(bf["z", 1, 1], 2, 4, 0, HALF), in_=late_rows, func=SQUARE)
 
-        for j in range(2):
-            acc = {}
-            for kind, first_bank in (("x", 0), ("z", 4)):
-                for n in range(4):
-                    acc[kind, n] = bank(first_bank + n)
-            if j == 0:
-                for a in range(2):
-                    for kind in ("zx", "xz")[a]:
-                        for n in range(4):
-                            product(acc[kind, n], kind, n, a, j)
-            else:
-                for a in range(2):
-                    for n in range(2):
-                        product(acc["x", n], "x", n, a, j)
-                for kind, n in (("x", 2), ("z", 0), ("x", 3), ("z", 1), ("z", 2), ("z", 3)):
-                    for a in range(2):
-                        product(acc[kind, n], kind, n, a, j)
+        def open_banks():
+            return {(kind, n): bank(first + n) for kind, first in (("x", 0), ("z", 4)) for n in range(4)}
+
+        def finish(acc, n, j):
+            half_sq = ring.tile([P, HALF], F32, name="half_sq", tag="half_sq", bufs=4)
+            nc.scalar.activation(out=half_sq[:], in_=acc["x", n][:], func=SQUARE, scale=0.5**0.5)
+            pieces = 2 if (j, n) == (1, 3) else 1
+            width = HALF // pieces
+            for piece in range(pieces):
+                cols = slice(width * piece, width * (piece + 1))
+                res = staged[j][:, HALF * n : HALF * (n + 1)][:, cols]
+                nc.vector.scalar_tensor_tensor(
+                    out=res, in0=acc["z", n][:, cols], scalar=-0.5, in1=half_sq[:, cols], op0=MULT, op1=ADD
+                )
+                nc.sync.dma_start(out=out[P * n : P * (n + 1), halves[j]][:, cols], in_=res)
+
+        acc = open_banks()
+        for kind in "zx":
             for n in range(4):
-                half_sq = ring.tile([P, HALF], F32, name="half_sq", tag="half_sq", bufs=4)
-                nc.scalar.activation(out=half_sq[:], in_=acc["x", n][:], func=SQUARE, scale=0.5**0.5)
-                pieces = 2 if (j, n) == (1, 3) else 1
-                width = HALF // pieces
-                for piece in range(pieces):
-                    cols = slice(width * piece, width * (piece + 1))
-                    res = staged[j][:, HALF * n : HALF * (n + 1)][:, cols]
-                    nc.vector.scalar_tensor_tensor(
-                        out=res, in0=acc["z", n][:, cols], scalar=-0.5, in1=half_sq[:, cols], op0=MULT, op1=ADD
-                    )
-                    nc.sync.dma_start(out=out[P * n : P * (n + 1), halves[j]][:, cols], in_=res)
+                product(acc[kind, n], kind, n, 0, 0)
+        for kind, n in (("x", 0), ("x", 1), ("z", 0), ("x", 2), ("z", 1), ("x", 3), ("z", 2), ("z", 3)):
+            product(acc[kind, n], kind, n, 1, 0)
+        finish(acc, 0, 0)
+        nc.vector.tensor_copy(out=woven(bf["x", 1, 1], 2, 4, 0, HALF), in_=late_rows)
+        finish(acc, 1, 0)
+        quantize_part("x", 1, 1)
+        quantize_part("z", 1, 1)
+        for n in range(2, 4):
+            finish(acc, n, 0)
+
+        acc = open_banks()
+        early = [("x", 0), ("x", 1), ("z", 0), ("x", 2), ("x", 3), ("z", 1)]
+        for a in range(2):
+            for kind, n in early:
+                product(acc[kind, n], kind, n, a, 1)
+        for n in range(2, 4):
+            for a in range(2):
+                product(acc["z", n], "z", n, a, 1)
+        for n in range(4):
+            finish(acc, n, 1)

@@ -28,7 +28,7 @@ V_COL = (0, HALF + H)
 PLANE_W = S + H
 EARLY_W = W1_COL + 2 * P
 PAGE_BUFS = 6
-FIRST = 384
+FIRST = 448
 
 
 def tile_list_gift_interactions_kernel(
@@ -48,7 +48,7 @@ def tile_list_gift_interactions_kernel(
         w1_perm = keep.tile([P, 2 * 2 * H], U8, name="w1_perm", align_bytes=64)
         tab0 = keep.tile([P, T], I32, name="tab0", tag="big0", align_bytes=64)
         w1_raw = keep.tile([P, 2 * 2 * H], U8, name="w1_raw", align_bytes=64)
-        wgs_raw = keep.tile([P, S], F32, name="wgs_raw", tag="dealt", bufs=2)
+        wgs_first = keep.tile([P, HALF], F32, name="wgs_first")
         v0 = keep.tile([P, S], U32, name="v0", align_bytes=64)
         v1 = [keep.tile([P, HALF], U32, name="v1_%d" % j, align_bytes=64) for j in range(2)]
         wg = [keep.tile([P, S], F32, name="wg%d" % t, tag="wg%d" % t, align_bytes=64) for t in range(PACK)]
@@ -68,10 +68,10 @@ def tile_list_gift_interactions_kernel(
             ident = keep.tile([P, P], F32, name="ident")
             make_identity(nc, ident[:])
 
-            nc.sync.dma_start(out=w1_sc[0:32, :].bitcast(I32), in_=w1_scales.rearrange("a q c -> (a q) c").bitcast(I32))
             nc.sync.dma_start(idx[:], offs)
             nc.sync.dma_start(out=tab_sc[0:32, :].bitcast(I32), in_=tab_scales.rearrange("a q c -> (a q) c").bitcast(I32))
-            nc.sync.dma_start(out=wgs_raw[:], in_=wgs)
+            nc.sync.dma_start(out=w1_sc[0:32, :].bitcast(I32), in_=w1_scales.rearrange("a q c -> (a q) c").bitcast(I32))
+            nc.sync.dma_start(out=wgs_first[:], in_=wgs[:, halves[0]])
             nc.sync.dma_start(idx2[:], offs2)
             nc.sync.dma_start(idx3[:], offs3)
             nc.sync.dma_start(
@@ -86,32 +86,30 @@ def tile_list_gift_interactions_kernel(
                     nc.tensor.transpose(acc[:, P * c : P * (c + 1)], src[:, P * c : P * (c + 1)], ident[:])
                 return acc
 
-            turned = [turn(wgs_raw[:, halves[j]], 6 + j) for j in range(2)]
+            turned = [turn(wgs_first[:], 6)]
 
-            def deal_weights(t, first_bank):
-                dealt = keep.tile([P, S], F32, name="dealt", tag="dealt", bufs=2)
-                for j in range(2):
-                    rows = turned[j][:].rearrange("p (c q t) -> p c t q", c=4, t=PACK)[:, :, t, :]
-                    nc.scalar.copy(
-                        out=dealt[:, halves[j]].rearrange("p (c g q) -> p c g q", c=4, g=4),
-                        in_=rows.unsqueeze(2).to_broadcast([P, 4, 4, 32]),
-                    )
-                for j in range(2):
-                    nc.scalar.copy(out=wg[t][:, halves[j]], in_=turn(dealt[:, halves[j]], first_bank + j)[:])
+            def deal_weights(t, j, b):
+                dealt = keep.tile([P, HALF], F32, name="dealt", tag="dealt", bufs=2)
+                rows = turned[j][:].rearrange("p (c q t) -> p c t q", c=4, t=PACK)[:, :, t, :]
+                nc.scalar.copy(
+                    out=dealt[:].rearrange("p (c g q) -> p c g q", c=4, g=4),
+                    in_=rows.unsqueeze(2).to_broadcast([P, 4, 4, 32]),
+                )
+                nc.scalar.copy(out=wg[t][:, halves[j]], in_=turn(dealt[:], b)[:])
 
-            deal_weights(0, 2)
-            deal_weights(1, 4)
+            for t in range(PACK):
+                deal_weights(t, 0, 2 + t)
 
-            for lo, hi in ((32, 64), (64, 128)):
-                nc.vector.memset(w1_sc[lo:hi, :].bitcast(I32), 0)
             for lo, hi in ((32, 64), (64, 128)):
                 nc.vector.memset(tab_sc[lo:hi, :].bitcast(I32), 0)
+            for lo, hi in ((32, 64), (64, 128)):
+                nc.vector.memset(w1_sc[lo:hi, :].bitcast(I32), 0)
             nc.vector.memset(planes[1][:].bitcast(I32), 0)
 
+            nc.vector.tensor_copy(got_sc[:], tab_sc[:].indirect(idx[:]))
             dealt_sc = planes[0][:, W1_COL : W1_COL + H].rearrange("p (a t m) -> p a t m", a=2, t=PACK)
             given_sc = w1_sc[:].rearrange("p (a m t) -> p a t m", a=2, t=PACK)
             nc.vector.tensor_copy(out=dealt_sc[:, 0, 0:2, :], in_=given_sc[:, 0, 0:2, :])
-            nc.vector.tensor_copy(got_sc[:], tab_sc[:].indirect(idx[:]))
             nc.vector.tensor_copy(
                 out=planes[0][:].bitcast(I32).rearrange("p (u w) -> p u w", u=4)[:, 0:4:3, :],
                 in_=got_sc[:].bitcast(I32).rearrange("p (u w) -> p u w", u=2),
@@ -143,6 +141,8 @@ def tile_list_gift_interactions_kernel(
         nc.sync.dma_start(out=tab1[:], in_=tab_words[1].rearrange("p c i -> p (c i)").bitcast(I32))
         move_scales(1, slice(0, EARLY_W))
         pages = [load_page(0)]
+        wgs_second = ring.tile([P, HALF], F32, name="wgs_second")
+        nc.sync.dma_start(out=wgs_second[:], in_=wgs[:, halves[1]])
         fw_parts = [(1, P * q, P * (q + 1)) for q in range(4)] + [(0, 0, P), (0, P, 2 * P), (0, 2 * P, N - 64), (0, N - 64, N)]
         fw_bf = ring.tile([P, 2 * N * PACK], BF16, name="fw_bf", align_bytes=64)
 
@@ -240,16 +240,19 @@ def tile_list_gift_interactions_kernel(
         def quantize(codes, scales, src):
             nc.vector.quantize_mx(out=codes.bitcast(FP8X4), scales=scales, in_=src)
 
-        for b, (lo, hi) in enumerate(((0, 256), (256, FIRST), (FIRST, HALF))):
-            make_h(0, lo, hi, (0, 1, 4)[b])
+        for b in range(2):
+            make_h(0, 256 * b, 256 * (b + 1), b)
         make_h(1, 0, HALF, 5)
+        turned.append(turn(wgs_second[:], 0))
+        deal_weights(0, 1, 1)
+        deal_weights(1, 1, 4)
         for i in range(2):
             make_h(i, HALF, S, 2 + i)
-        deal_weights(2, 0)
-        deal_weights(3, 2)
+        deal_weights(2, 1, 2)
+        deal_weights(3, 1, 3)
         for i in range(2, SLICES):
             for j in range(2):
-                make_h(i, HALF * j, HALF * (j + 1), (2 * i + j) % 8)
+                make_h(i, HALF * j, HALF * (j + 1), (2 * i + j - 2) % 8)
 
         fw_codes = ring.tile([P, 2 * N], U32, name="fw_codes", align_bytes=64)
         fw_sc = ring.tile([P, 2 * N], U8, name="fw_sc", align_bytes=64)

@@ -51,7 +51,7 @@ def tile_list_gift_interactions_kernel(
         wgs_first = keep.tile([P, HALF], F32, name="wgs_first")
         v0 = keep.tile([P, S], U32, name="v0", align_bytes=64)
         v1 = [keep.tile([P, HALF], U32, name="v1_%d" % j, align_bytes=64) for j in range(2)]
-        wg = [keep.tile([P, S], F32, name="wg%d" % t, tag="wg%d" % t, align_bytes=64) for t in range(PACK)]
+        wg = [keep.tile([P, S], F32, name="wg%d" % t, tag="wg%d" % t, align_bytes=64) for t in range(2)]
 
         def page_rows(i):
             a, t = divmod(i, PACK)
@@ -97,7 +97,7 @@ def tile_list_gift_interactions_kernel(
                 )
                 nc.scalar.copy(out=wg[t][:, halves[j]], in_=turn(dealt[:], b)[:])
 
-            for t in range(PACK):
+            for t in range(2):
                 deal_weights(t, 0, 2 + t)
 
             for lo, hi in ((32, 64), (64, 128)):
@@ -162,7 +162,15 @@ def tile_list_gift_interactions_kernel(
             )
             return raw
 
+        def load_weights(t):
+            wg.append(ring.tile([P, S], F32, name="wg%d" % t))
+            rows = wgs.rearrange("(q t) j -> t q j", t=PACK)[t]
+            for g in (0, 2, 1, 3):
+                nc.sync.dma_start(out=wg[t][32 * g : 32 * (g + 1), :], in_=rows)
+
         def load_page_and_fw(i):
+            if i < PACK:
+                load_weights(i)
             pages.append(load_page(i))
             return load_fw(i)
 
@@ -248,11 +256,9 @@ def tile_list_gift_interactions_kernel(
         deal_weights(1, 1, 4)
         for i in range(2):
             make_h(i, HALF, S, 2 + i)
-        deal_weights(2, 1, 2)
-        deal_weights(3, 1, 3)
         for i in range(2, SLICES):
             for j in range(2):
-                make_h(i, HALF * j, HALF * (j + 1), (2 * i + j - 2) % 8)
+                make_h(i, HALF * j, HALF * (j + 1), (1, 4, 2, 3)[(2 * i + j) % 4])
 
         fw_codes = ring.tile([P, 2 * N], U32, name="fw_codes", align_bytes=64)
         fw_sc = ring.tile([P, 2 * N], U8, name="fw_sc", align_bytes=64)

@@ -22,13 +22,14 @@ P = 128
 PACK = 4
 SLICES = 8
 HALF = 512
-LIST_HALF = HALF // 16
 W1_COL = HALF
 V_COL = (0, HALF + H)
 PLANE_W = S + H
 EARLY_W = W1_COL + 2 * P
-PAGE_BUFS = 6
-FIRST = 448
+TABLE_CUT = T // 4
+CHUNK = 256
+CHUNKS = M // CHUNK
+WOVEN = PACK * CHUNK
 
 
 def tile_list_gift_interactions_kernel(
@@ -44,371 +45,308 @@ def tile_list_gift_interactions_kernel(
         idx2 = lists.tile([P, S // 16], U16, name="idx2")
         idx3 = lists.tile([P, M // 16], U16, name="idx3")
 
-        planes = [keep.tile([P, PLANE_W], U8, name="plane%d" % k, align_bytes=64) for k in range(2)]
-        w1_perm = keep.tile([P, 2 * 2 * H], U8, name="w1_perm", align_bytes=64)
-        tab0 = keep.tile([P, T], I32, name="tab0", tag="big0", align_bytes=64)
-        w1_raw = keep.tile([P, 2 * 2 * H], U8, name="w1_raw", align_bytes=64)
-        wgs_first = keep.tile([P, HALF], F32, name="wgs_first")
-        v0 = keep.tile([P, S], U32, name="v0", align_bytes=64)
-        v1 = [keep.tile([P, HALF], U32, name="v1_%d" % j, align_bytes=64) for j in range(2)]
-        wg = [keep.tile([P, S], F32, name="wg%d" % t, tag="wg%d" % t, align_bytes=64) for t in range(2)]
-
-        def page_rows(i):
-            a, t = divmod(i, PACK)
-            return page0[HALF * a : HALF * (a + 1), :].rearrange("(p t) c -> t p c", t=PACK)[t]
-
         def bank(b):
             return psum.tile([P, HALF], F32, name="bank%d" % b, tag="bank%d" % b)
 
-        halves = [slice(0, HALF), slice(HALF, M)]
-        with tc.tile_pool(name="head", bufs=1) as head:
-            tab_sc = head.tile([P, T], U8, name="tab_sc", align_bytes=64)
-            w1_sc = keep.tile([P, H], U8, name="w1_sc", align_bytes=64)
-            got_sc = head.tile([P, S], U8, name="got_sc", align_bytes=64)
-            ident = keep.tile([P, P], F32, name="ident")
-            make_identity(nc, ident[:])
+        halves = [slice(0, HALF), slice(HALF, S)]
+        planes = [keep.tile([P, PLANE_W], U8, name="plane%d" % k, align_bytes=64) for k in range(2)]
+        tab_sc = keep.tile([P, T], U8, name="tab_sc", align_bytes=64)
+        w1_sc = keep.tile([P, H], U8, name="w1_sc", align_bytes=64)
+        tab = [keep.tile([P, T], I32, name="tab%d" % k, tag="big%d" % k, align_bytes=64) for k in range(2)]
+        w1_raw = [keep.tile([P, 2 * H], U8, name="w1_raw0", align_bytes=64)]
+        w1_perm = [keep.tile([P, 2 * H], U8, name="w1_perm%d" % a, align_bytes=64) for a in range(2)]
+        wgs_rows = [keep.tile([P, S // 4], F32, name="wgs_rows0")]
+        wg = [keep.tile([P, S], F32, name="wg%d" % t) for t in range(PACK)]
+        v = [keep.tile([P, S], U32, name="v%d" % k, align_bytes=64) for k in range(2)]
+        fw_bf = keep.tile([P, 2 * N * PACK], BF16, name="fw_bf", align_bytes=64)
+        fw_codes = keep.tile([P, 2 * N], U32, name="fw_codes", align_bytes=64)
+        fw_sc = keep.tile([P, 2 * N], U8, name="fw_sc", align_bytes=64)
+        ident = keep.tile([P, P], F32, name="ident")
+        make_identity(nc, ident[:])
 
-            nc.sync.dma_start(idx[:], offs)
-            nc.sync.dma_start(out=tab_sc[0:32, :].bitcast(I32), in_=tab_scales.rearrange("a q c -> (a q) c").bitcast(I32))
-            nc.sync.dma_start(out=w1_sc[0:32, :].bitcast(I32), in_=w1_scales.rearrange("a q c -> (a q) c").bitcast(I32))
-            nc.sync.dma_start(out=wgs_first[:], in_=wgs[:, halves[0]])
-            nc.sync.dma_start(idx2[:], offs2)
-            nc.sync.dma_start(idx3[:], offs3)
+        def load_table(k, lo, hi):
+            words = tab_words[k].rearrange("p c i -> p (c i)").bitcast(I32)
+            nc.sync.dma_start(out=tab[k][:, lo:hi], in_=words[:, lo:hi])
+
+        def load_wgs(t):
+            nc.sync.dma_start(out=wgs_rows[t][:], in_=wgs.rearrange("(q t) (u c) -> t q u c", t=PACK, u=4)[t])
+
+        def load_w1(a):
             nc.sync.dma_start(
-                out=w1_raw[:].bitcast(I32).rearrange("p (k c) -> p k c", k=2),
-                in_=w1_words.bitcast(I32).rearrange("k p c -> p k c"),
-            )
-            nc.sync.dma_start(out=tab0[:], in_=tab_words[0].rearrange("p c i -> p (c i)").bitcast(I32))
-
-            def turn(src, b):
-                acc = bank(b)
-                for c in range(4):
-                    nc.tensor.transpose(acc[:, P * c : P * (c + 1)], src[:, P * c : P * (c + 1)], ident[:])
-                return acc
-
-            turned = [turn(wgs_first[:], 6)]
-
-            def deal_weights(t, j, b):
-                dealt = keep.tile([P, HALF], F32, name="dealt", tag="dealt", bufs=2)
-                rows = turned[j][:].rearrange("p (c q t) -> p c t q", c=4, t=PACK)[:, :, t, :]
-                nc.scalar.copy(
-                    out=dealt[:].rearrange("p (c g q) -> p c g q", c=4, g=4),
-                    in_=rows.unsqueeze(2).to_broadcast([P, 4, 4, 32]),
-                )
-                nc.scalar.copy(out=wg[t][:, halves[j]], in_=turn(dealt[:], b)[:])
-
-            for t in range(2):
-                deal_weights(t, 0, 2 + t)
-
-            for lo, hi in ((32, 64), (64, 128)):
-                nc.vector.memset(tab_sc[lo:hi, :].bitcast(I32), 0)
-            for lo, hi in ((32, 64), (64, 128)):
-                nc.vector.memset(w1_sc[lo:hi, :].bitcast(I32), 0)
-            nc.vector.memset(planes[1][:].bitcast(I32), 0)
-
-            nc.vector.tensor_copy(got_sc[:], tab_sc[:].indirect(idx[:]))
-            dealt_sc = planes[0][:, W1_COL : W1_COL + H].rearrange("p (a t m) -> p a t m", a=2, t=PACK)
-            given_sc = w1_sc[:].rearrange("p (a m t) -> p a t m", a=2, t=PACK)
-            nc.vector.tensor_copy(out=dealt_sc[:, 0, 0:2, :], in_=given_sc[:, 0, 0:2, :])
-            nc.vector.tensor_copy(
-                out=planes[0][:].bitcast(I32).rearrange("p (u w) -> p u w", u=4)[:, 0:4:3, :],
-                in_=got_sc[:].bitcast(I32).rearrange("p (u w) -> p u w", u=2),
+                out=w1_raw[a][:].bitcast(I32).rearrange("p (k c) -> p k c", k=2),
+                in_=w1_words.bitcast(I32).rearrange("k p (a c) -> a p k c", a=2)[a],
             )
 
-        nc.vector.tensor_copy(out=dealt_sc[:, 0, 2:4, :], in_=given_sc[:, 0, 2:4, :])
-        nc.vector.tensor_copy(out=dealt_sc[:, 1, :, :], in_=given_sc[:, 1, :, :])
+        def load_page(i):
+            a, t = divmod(i, PACK)
+            nc.sync.dma_start(
+                out=pages[i][:], in_=page0[HALF * a : HALF * (a + 1), :].rearrange("(p t) c -> t p c", t=PACK)[t]
+            )
 
-        def move_scales(k, cols):
-            for q in ((1, 2, 3), (0, 2, 1, 3))[k]:
+        def move_scales(moves, cols):
+            for k, q in moves:
                 nc.sync.dma_start(
                     out=planes[k][32 * q : 32 * q + 4, cols].bitcast(I32),
                     in_=planes[0][16 * k + 4 * q : 16 * k + 4 * q + 4, cols].bitcast(I32),
                 )
 
+        def permute_w1(engine_copy, a):
+            engine_copy(
+                out=w1_perm[a][:].bitcast(U16).rearrange("p (k t m) -> p k t m", k=2, t=PACK),
+                in_=w1_raw[a][:].bitcast(U16).rearrange("p (k m t) -> p k t m", k=2, t=PACK),
+            )
+
+        def deal_weights(t):
+            turned = bank(7)
+            for c in range(2):
+                nc.tensor.transpose(turned[:, P * c : P * (c + 1)], wgs_rows[t][:, P * c : P * (c + 1)], ident[:])
+            rows = turned[:, 0 : 2 * P].rearrange("p (c q u) -> p u c q", c=2, u=4)
+            for j in range(2):
+                dealt = keep.tile([P, HALF], F32, name="dealt", tag="dealt", bufs=2)
+                nc.scalar.copy(
+                    out=dealt[:].rearrange("p (u c g q) -> p u c g q", u=2, c=2, g=4),
+                    in_=rows[:, 2 * j : 2 * j + 2].unsqueeze(3).to_broadcast([P, 2, 2, 4, 32]),
+                )
+                back = bank(5 + j)
+                for c in range(4):
+                    nc.tensor.transpose(back[:, P * c : P * (c + 1)], dealt[:, P * c : P * (c + 1)], ident[:])
+                nc.scalar.copy(out=wg[t][:, halves[j]], in_=back[:])
+
+        nc.sync.dma_start(idx[:], offs)
+        nc.sync.dma_start(out=tab_sc[0:32, :].bitcast(I32), in_=tab_scales.rearrange("a q c -> (a q) c").bitcast(I32))
+        nc.sync.dma_start(out=w1_sc[0:32, :].bitcast(I32), in_=w1_scales.rearrange("a q c -> (a q) c").bitcast(I32))
+        load_wgs(0)
+        load_w1(0)
+        nc.sync.dma_start(idx2[:], offs2)
+        nc.sync.dma_start(idx3[:], offs3)
+        load_table(0, 0, T)
+        load_table(1, 0, TABLE_CUT)
+
+        for rows_sc in (tab_sc, w1_sc):
+            for lo, hi in ((32, 64), (64, 128)):
+                nc.vector.memset(rows_sc[lo:hi, :].bitcast(I32), 0)
+        nc.vector.memset(planes[1][:].bitcast(I32), 0)
+
+        def gather_scales(j, got):
+            nc.vector.tensor_copy(got[:], tab_sc[:].indirect(idx[:, 32 * j : 32 * (j + 1)]))
+
+        def lay_scales(j, got):
+            nc.vector.tensor_copy(out=planes[0][:, V_COL[j] : V_COL[j] + HALF].bitcast(I32), in_=got[:].bitcast(I32))
+
+        dealt_sc = planes[0][:, W1_COL : W1_COL + H].rearrange("p (a t m) -> p a t m", a=2, t=PACK)
+        given_sc = w1_sc[:].rearrange("p (a m t) -> p a t m", a=2, t=PACK)
+        got_late = keep.tile([P, HALF], U8, name="got_late", align_bytes=64)
+        with tc.tile_pool(name="head", bufs=1) as head:
+            got_early = head.tile([P, HALF], U8, name="got_early", align_bytes=64)
+            gather_scales(0, got_early)
+            nc.vector.tensor_copy(out=dealt_sc[:, 0, 0:2, :], in_=given_sc[:, 0, 0:2, :])
+            lay_scales(0, got_early)
+        gather_scales(1, got_late)
+        nc.vector.tensor_copy(out=dealt_sc[:, 0, 2:4, :], in_=given_sc[:, 0, 2:4, :])
+        lay_scales(1, got_late)
+        nc.vector.tensor_copy(out=dealt_sc[:, 1, :, :], in_=given_sc[:, 1, :, :])
+        permute_w1(nc.vector.tensor_copy, 0)
+        deal_weights(0)
+
         ring = ctx.enter_context(tc.tile_pool(name="ring", bufs=1))
-        tab1 = ring.tile([P, T], I32, name="tab1", tag="big1", align_bytes=64)
-        xs = [ring.tile([P, PACK * M], F32, name="xs0", offset=0), ring.tile([P, PACK * M], F32, name="xs1")]
-
-        def load_page(i):
-            if i == SLICES - 1:
-                page = ring.tile([P, T2], F32, name="page7", offset=0)
-            else:
-                page = ring.tile([P, T2], F32, name="page%d" % i, tag="page", bufs=PAGE_BUFS)
-            nc.sync.dma_start(out=page[:], in_=page_rows(i))
-            return page
-
-        move_scales(0, slice(0, EARLY_W))
-        nc.sync.dma_start(out=tab1[:], in_=tab_words[1].rearrange("p c i -> p (c i)").bitcast(I32))
-        move_scales(1, slice(0, EARLY_W))
-        pages = [load_page(0)]
-        wgs_second = ring.tile([P, HALF], F32, name="wgs_second")
-        nc.sync.dma_start(out=wgs_second[:], in_=wgs[:, halves[1]])
-        fw_parts = [(1, P * q, P * (q + 1)) for q in range(4)] + [(0, 0, P), (0, P, 2 * P), (0, 2 * P, N - 64), (0, N - 64, N)]
-        fw_bf = ring.tile([P, 2 * N * PACK], BF16, name="fw_bf", align_bytes=64)
-
-        def load_fw(i):
-            a, lo, hi = fw_parts[i - 1]
-            width = PACK * (hi - lo)
-            if i == 6:
-                raw = ring.tile([P, width], F32, name="fw_part6", tag="held6", align_bytes=64)[:]
-            elif i == SLICES:
-                raw = ring.tile([P, width], F32, name="fw_part8", offset=6 * T2 - 512)[:]
-            else:
-                first = 5 * M - width // 2 if i == 5 else M * (i - 1)
-                raw = xs[first // (PACK * M)][:, first % (PACK * M) : first % (PACK * M) + width]
-            nc.sync.dma_start(
-                out=raw.rearrange("p (t n) -> p t n", t=PACK),
-                in_=fw[HALF * a : HALF * (a + 1), lo:hi].rearrange("(p t) n -> p t n", t=PACK),
-            )
-            return raw
-
-        def load_weights(t):
-            wg.append(ring.tile([P, S], F32, name="wg%d" % t))
-            rows = wgs.rearrange("(q t) j -> t q j", t=PACK)[t]
-            for g in (0, 2, 1, 3):
-                nc.sync.dma_start(out=wg[t][32 * g : 32 * (g + 1), :], in_=rows)
-
-        def load_page_and_fw(i):
-            if i < PACK:
-                load_weights(i)
-            pages.append(load_page(i))
-            return load_fw(i)
-
-        def round_fw(i, raw):
-            a, lo, hi = fw_parts[i - 1]
-            nc.scalar.copy(
-                out=fw_bf[:, PACK * (N * a + lo) : PACK * (N * a + hi)].rearrange("p (c i t) -> p c t i", i=4, t=PACK),
-                in_=raw.rearrange("p (t c i) -> p c t i", t=PACK, i=4),
-            )
-
-        pages.append(load_page(1))
-        for k in range(2):
-            move_scales(k, slice(EARLY_W, PLANE_W))
-        fw_raw = [load_fw(1)] + [load_page_and_fw(i) for i in range(2, PAGE_BUFS)]
-
-        nc.vector.tensor_copy(
-            out=w1_perm[:].bitcast(U16).rearrange("p (g t m) -> p g t m", g=4, t=PACK),
-            in_=w1_raw[:].bitcast(U16).rearrange("p (g m t) -> p g t m", g=4, t=PACK),
-        )
-        nc.vector.tensor_copy(v0[:], tab0[:].bitcast(U32).indirect(idx[:]))
-        for j in range(2):
-            nc.vector.tensor_copy(v1[j][:], tab1[:].bitcast(U32).indirect(idx[:, LIST_HALF * j : LIST_HALF * (j + 1)]))
-
-        h_rows = [(keep, ring)[a].tile([P, PACK * S], F32, name="h%d" % a, tag="big%d" % a, align_bytes=64) for a in range(2)]
+        pages = [ring.tile([P, T2], F32, name="page%d" % i) for i in range(SLICES)]
+        w1_raw.append(ring.tile([P, 2 * H], U8, name="w1_raw1", align_bytes=64))
+        wgs_rows.extend(ring.tile([P, S // 4], F32, name="wgs_rows%d" % t) for t in range(1, PACK))
+        xs0 = ring.tile([P, PACK * M], F32, name="xs0", tag="xs0", align_bytes=64)
+        xs1 = ring.tile([P, 2 * WOVEN], F32, name="xs1")
         sq_codes = ring.tile([P, 2 * N], I32, name="sq_codes", align_bytes=64)
         sq_sc = ring.tile([P, N], U8, name="sq_sc", align_bytes=64)
         nc.vector.memset(sq_sc[:].bitcast(I32), 0)
+
+        moves = [(0, 1), (0, 2), (0, 3), (1, 0), (1, 2), (1, 1), (1, 3)]
+        move_scales(moves[:5], slice(0, EARLY_W))
+        load_table(1, TABLE_CUT, T)
+        move_scales(moves[5:], slice(0, EARLY_W))
+        load_page(0)
+        load_wgs(1)
+        load_page(1)
+        move_scales(moves, slice(EARLY_W, PLANE_W))
+        load_wgs(2)
+        load_page(2)
+        load_wgs(3)
+        load_w1(1)
+        load_page(3)
+        x0_rows = xs0[:].rearrange("p (t m) -> p t m", t=PACK)
+        fw_rows = fw.rearrange("(a p t) n -> a p t n", a=2, t=PACK)
+        nc.sync.dma_start(out=x0_rows[:, :, 0:N], in_=fw_rows[0])
+        for i in range(PACK, SLICES):
+            load_page(i)
+        x1_rows = [xs1[:, WOVEN * b : WOVEN * (b + 1)].rearrange("p (t m) -> p t m", t=PACK) for b in range(2)]
+        for b in range(2):
+            nc.sync.dma_start(out=x1_rows[b], in_=fw_rows[1][:, :, CHUNK * b : CHUNK * (b + 1)])
         for q in range(4):
             nc.sync.dma_start(
                 out=sq_sc[32 * q : 32 * q + 8, :].bitcast(I32), in_=sq_scales[:, 4 * q : 4 * q + 4, :].bitcast(I32)
             )
+        nc.sync.dma_start(
+            out=sq_codes[:].rearrange("p (a c) -> p a c", a=2),
+            in_=sq_words.rearrange("a p c i -> p a (c i)").bitcast(I32),
+        )
 
-        def slot(s):
-            return xs[s // PACK][:, M * (s % PACK) : M * (s % PACK + 1)]
+        def gather_table(k, lo, hi):
+            nc.vector.tensor_copy(v[k][:, lo:hi], tab[k][:].bitcast(U32).indirect(idx[:, lo // 16 : hi // 16]))
+
+        gather_table(0, 0, S)
+        for lo, hi in ((0, 256), (256, HALF), (HALF, S)):
+            gather_table(1, lo, hi)
+
+        h_rows = [keep.tile([P, PACK * S], F32, name="h%d" % a, tag="big%d" % a, align_bytes=64) for a in range(2)]
 
         def h_of(i):
             return h_rows[i // PACK][:, S * (i % PACK) : S * (i % PACK + 1)]
 
         def make_h(i, lo, hi, b):
+            a, t = divmod(i, PACK)
             j, first_col = divmod(lo, HALF)
-            width = hi - lo
-            acc = bank(b)[:, 0:width]
-            order = (0, 1) if i < 2 and j == 0 else (1, 0)
-            for k in order:
-                first = 2 * (H * k + P * i)
+            acc = bank(b)[:, 0 : hi - lo]
+            for k in range(2):
+                first = 2 * (HALF * k + P * t)
                 nc.tensor.matmul_mx(
                     out=acc,
-                    lhsT=w1_perm[:, first : first + 2 * P].bitcast(FP4X4),
+                    lhsT=w1_perm[a][:, first : first + 2 * P].bitcast(FP4X4),
                     lhsT_scale=planes[k][:, W1_COL + P * i : W1_COL + P * (i + 1)],
-                    rhs=(v0[:, lo:hi] if k == 0 else v1[j][:, first_col : first_col + width]).bitcast(FP8X4),
-                    rhs_scale=planes[k][:, V_COL[j] + first_col : V_COL[j] + first_col + width],
-                    start=(k == order[0]),
-                    stop=(k == order[1]),
+                    rhs=v[k][:, lo:hi].bitcast(FP8X4),
+                    rhs_scale=planes[k][:, V_COL[j] + first_col : V_COL[j] + first_col + hi - lo],
+                    start=(k == 0),
+                    stop=(k == 1),
                 )
             nc.scalar.copy(out=h_of(i)[:, lo:hi], in_=acc)
+
+        for b in range(2):
+            make_h(0, 256 * b, 256 * (b + 1), b)
+        make_h(1, 0, HALF, 2)
+        deal_weights(1)
+        for i in range(2):
+            make_h(i, HALF, S, 3 + i)
+        for i in range(2, SLICES):
+            if i < PACK:
+                deal_weights(i)
+            if i == PACK:
+                permute_w1(nc.scalar.copy, 1)
+            for j in range(2):
+                make_h(i, HALF * j, HALF * (j + 1), (2 * i + j) % 4)
 
         def scatter(i, lo=0, hi=S):
             nc.vector.tensor_tensor(
                 pages[i][:].indirect(idx2[:, lo // 16 : hi // 16]), h_of(i)[:, lo:hi], wg[i % PACK][:, lo:hi], MULT
             )
 
-        def gather(i, lo=0, hi=M, into=None):
-            into = slot(i)[:, lo:hi] if into is None else into
+        def gather(i, into, lo, hi):
             nc.vector.tensor_copy(into, pages[i][:].indirect(idx3[:, lo // 16 : hi // 16]))
 
-        def woven(tile, lo, hi, first, width):
-            part = tile[:, PACK * first : PACK * (first + width)]
-            return part.rearrange("p (c i t) -> p c t i", i=4, t=PACK)[:, :, lo:hi, :]
+        def woven(part):
+            return part.rearrange("p (c i t) -> p c t i", i=4, t=PACK)
 
-        def x_rows(a, j, lo, hi, first, width):
-            rows = xs[a][:].rearrange("p (t m) -> p t m", t=PACK)
-            cols = slice(HALF * j + first, HALF * j + first + width)
-            return rows[:, lo:hi, cols].rearrange("p t (c i) -> p c t i", i=4)
+        def by_fours(rows):
+            return rows.rearrange("p t (c i) -> p c t i", i=4)
 
         def quantize(codes, scales, src):
             nc.vector.quantize_mx(out=codes.bitcast(FP8X4), scales=scales, in_=src)
 
+        def place(kind, a, c):
+            return 2 * (2 * c + a) + "xz".index(kind)
+
+        rounded = ring.tile([P, 4 * CHUNKS * WOVEN], BF16, name="rounded", align_bytes=64)
+        scales = ring.tile([P, 4 * M], U8, name="scales", align_bytes=64)
+
+        def round_chunk(a, c, rows):
+            u = place("x", a, c)
+            nc.scalar.copy(out=woven(rounded[:, WOVEN * u : WOVEN * (u + 1)]), in_=by_fours(rows))
+            nc.scalar.activation(out=woven(rounded[:, WOVEN * (u + 1) : WOVEN * (u + 2)]), in_=by_fours(rows), func=SQUARE)
+
+        for j in range(2):
+            for i in range(2):
+                scatter(i, HALF * j, HALF * (j + 1))
+        for i in range(2, PACK):
+            scatter(i)
+        nc.scalar.copy(out=woven(fw_bf[:, 0 : PACK * N]), in_=by_fours(x0_rows[:, :, 0:N]))
+        for t in range(PACK):
+            gather(t, x0_rows[:, t, :], 0, M)
         for b in range(2):
-            make_h(0, 256 * b, 256 * (b + 1), b)
-        make_h(1, 0, HALF, 5)
-        turned.append(turn(wgs_second[:], 0))
-        deal_weights(0, 1, 1)
-        deal_weights(1, 1, 4)
-        for i in range(2):
-            make_h(i, HALF, S, 2 + i)
-        for i in range(2, SLICES):
-            for j in range(2):
-                make_h(i, HALF * j, HALF * (j + 1), (1, 4, 2, 3)[(2 * i + j) % 4])
+            first = PACK * N + WOVEN * b
+            nc.scalar.copy(out=woven(fw_bf[:, first : first + WOVEN]), in_=by_fours(x1_rows[b]))
+        for c in range(CHUNKS):
+            round_chunk(0, c, x0_rows[:, :, CHUNK * c : CHUNK * (c + 1)])
+        for i in range(PACK, SLICES):
+            scatter(i)
 
-        fw_codes = ring.tile([P, 2 * N], U32, name="fw_codes", align_bytes=64)
-        fw_sc = ring.tile([P, 2 * N], U8, name="fw_sc", align_bytes=64)
-        for i in range(1, PAGE_BUFS):
-            round_fw(i, fw_raw[i - 1])
+        codes = ring.tile([P, 4 * M], U32, name="codes", tag="xs0", align_bytes=64)
 
-        bf = {}
-        codes = {}
-        scales = {}
-        for kind in "xz":
+        def quantize_places(lo, hi):
+            cols = slice(CHUNK * lo, CHUNK * hi)
+            quantize(codes[:, cols], scales[:, cols], rounded[:, WOVEN * lo : WOVEN * hi])
+
+        def fetch(c):
+            rows = x1_rows[c % 2]
+            for t in range(PACK):
+                gather(PACK + t, rows[:, t, :], CHUNK * c, CHUNK * (c + 1))
+            round_chunk(1, c, rows)
+
+        staged = [keep.tile([P, 8 * CHUNK], F32, name="staged%d" % j, tag="big%d" % j, align_bytes=64) for j in range(2)]
+        sums = {}
+        squares = {}
+
+        def multiply(c):
+            for kind in "xz":
+                for pair in range(2):
+                    sums[kind, c, pair] = bank(4 * (c % 2) + 2 * "xz".index(kind) + pair)
             for a in range(2):
-                for j in range(2):
-                    name = "%s%d%d" % (kind, a, j)
-                    if a == 1:
-                        bf[kind, a, j] = ring.tile([P, PACK * HALF], BF16, name="bf_" + name, align_bytes=64)[:]
-                        scales[kind, a, j] = ring.tile([P, HALF], U8, name="sc_" + name, align_bytes=64)[:]
-        bf0 = [ring.tile([P, 2 * PACK * HALF], BF16, name="bf0%d" % j, align_bytes=64) for j in range(2)]
-        sc0 = [ring.tile([P, M], U8, name="sc0%d" % j, align_bytes=64) for j in range(2)]
-        for j in range(2):
-            for u, kind in enumerate("xz"):
-                bf[kind, 0, j] = bf0[j][:, PACK * HALF * u : PACK * HALF * (u + 1)]
-                scales[kind, 0, j] = sc0[j][:, halves[u]]
-        for j in range(2):
-            pair = ring.tile([P, M], U32, name="codes1%d" % j, align_bytes=64)
-            codes["x", 1, j], codes["z", 1, j] = pair[:, halves[0]], pair[:, halves[1]]
+                for kind in "xz":
+                    u = place(kind, a, c)
+                    cols = slice(CHUNK * u, CHUNK * (u + 1))
+                    for n in range(4):
+                        ncols = slice(N * a + P * n, N * a + P * (n + 1))
+                        if kind == "x":
+                            lhs, lhs_sc = fw_codes[:, ncols], fw_sc[:, ncols]
+                        else:
+                            lhs, lhs_sc = sq_codes[:, ncols], sq_sc[4 * a : P, P * n : P * (n + 1)]
+                        nc.tensor.matmul_mx(
+                            out=sums[kind, c, n // 2][:, CHUNK * (n % 2) : CHUNK * (n % 2 + 1)],
+                            lhsT=lhs.bitcast(FP8X4),
+                            lhsT_scale=lhs_sc,
+                            rhs=codes[:, cols].bitcast(FP8X4),
+                            rhs_scale=scales[:, cols],
+                            start=(a == 0 and n % 2 == 0),
+                            stop=(a == 1 and n % 2 == 1),
+                        )
+            for pair in range(2):
+                squares[c, pair] = ring.tile([P, HALF], F32, name="half_sq", tag="half_sq", bufs=4)
+                nc.scalar.activation(out=squares[c, pair][:], in_=sums["x", c, pair][:], func=SQUARE, scale=0.5**0.5)
 
-        def round_x(engine_copy, a, j, lo, hi, first=0, width=HALF):
-            engine_copy(out=woven(bf["x", a, j], lo, hi, first, width), in_=x_rows(a, j, lo, hi, first, width))
+        def finish(c):
+            for pair in range(2):
+                first = 2 * HALF * (c % 2) + HALF * pair
+                tiles = ((0, 1), (1, 2)) if (c, pair) == (CHUNKS - 1, 1) else ((0, 2),)
+                for lo, hi in tiles:
+                    cols = slice(CHUNK * lo, CHUNK * hi)
+                    res = staged[c // 2][:, first : first + HALF][:, cols]
+                    nc.vector.scalar_tensor_tensor(
+                        out=res, in0=sums["z", c, pair][:, cols], scalar=-0.5, in1=squares[c, pair][:, cols], op0=MULT, op1=ADD
+                    )
+                    rows = out[P * (2 * pair + lo) : P * (2 * pair + hi), CHUNK * c : CHUNK * (c + 1)]
+                    nc.sync.dma_start(
+                        out=rows.rearrange("(n p) m -> p n m", p=P), in_=res.rearrange("p (n m) -> p n m", m=CHUNK)
+                    )
 
-        def round_z(a, j, lo, hi, first=0, width=HALF):
-            nc.scalar.activation(
-                out=woven(bf["z", a, j], lo, hi, first, width), in_=x_rows(a, j, lo, hi, first, width), func=SQUARE
-            )
-
-        def quantize_part(kind, a, j):
-            quantize(codes[kind, a, j], scales[kind, a, j], bf[kind, a, j])
-
-        codes["x", 0, 0] = ring.tile([P, HALF], U32, name="codes_x00", align_bytes=64)[:]
-
-        scatter(0, 0, FIRST)
-        scatter(1, 0, HALF)
-        scatter(0, FIRST, S)
-        scatter(1, HALF, S)
-        for i in range(1, 6):
-            if i > 1:
-                scatter(i)
-            gather(i - 1)
-            if i == 1:
-                pages.append(load_page(6))
-                round_fw(6, load_fw(6))
-                round_fw(7, load_fw(7))
-                nc.sync.dma_start(
-                    out=sq_codes[:].rearrange("p (a c) -> p a c", a=2),
-                    in_=sq_words.rearrange("a p c i -> p a (c i)").bitcast(I32),
-                )
-            if i == 4:
-                quantize(fw_codes[:, N:], fw_sc[:, N:], fw_bf[:, PACK * N :])
-                for j in range(2):
-                    for first in range(0, HALF, P):
-                        round_x(nc.scalar.copy, 0, j, 0, PACK, first, P)
-                for j in (1, 0):
-                    for first in range(0, HALF, P):
-                        round_z(0, j, 0, PACK, first, P)
-        pages.append(load_page(7))
-        round_fw(8, load_fw(8))
-        gather(5)
-        quantize_part("x", 0, 0)
-        for j in range(2):
-            for first in range(0, HALF, 2 * P):
-                round_x(nc.scalar.copy, 1, j, 0, 2, first, 2 * P)
-                round_z(1, j, 0, 2, first, 2 * P)
-        scatter(6)
-        pair = ring.tile([P, M], U32, name="codes01", tag="held6", align_bytes=64)
-        codes["x", 0, 1], codes["z", 0, 1] = pair[:, halves[0]], pair[:, halves[1]]
-        quantize(pair[:], sc0[1][:], bf0[1][:])
-        gather(6, 0, HALF)
-        round_z(1, 0, 2, 3)
-        scatter(7)
-        codes["z", 0, 0] = ring.tile([P, HALF], U32, name="codes_z00", offset=6 * T2, align_bytes=64)[:]
-        quantize_part("z", 0, 0)
-
-        def product(acc, kind, n, a, j):
-            ncols = slice(N * a + P * n, N * a + P * (n + 1))
-            if kind == "x":
-                lhs, lhs_sc = fw_codes[:, ncols], fw_sc[:, ncols]
-            else:
-                lhs, lhs_sc = sq_codes[:, ncols], sq_sc[4 * a : P, P * n : P * (n + 1)]
-            nc.tensor.matmul_mx(
-                out=acc[:],
-                lhsT=lhs.bitcast(FP8X4),
-                lhsT_scale=lhs_sc,
-                rhs=codes[kind, a, j].bitcast(FP8X4),
-                rhs_scale=scales[kind, a, j],
-                start=(a == 0),
-                stop=(a == 1),
-            )
-
-        staged = [
-            (keep, ring)[j].tile([P, PACK * N], F32, name="staged%d" % j, tag="big%d" % j, align_bytes=64) for j in range(2)
-        ]
-
-        late_x = ring.tile([P, M], F32, name="late_x", offset=4 * T2)
-        late_rows = late_x[:].rearrange("p (t c i) -> p c t i", t=2, i=4)
-        gather(7, 0, HALF)
-        round_z(1, 0, 3, 4)
-        quantize(fw_codes[:, :N], fw_sc[:, :N], fw_bf[:, : PACK * N])
-        round_x(nc.vector.tensor_copy, 1, 0, 2, 4)
-        gather(6, HALF, M, late_x[:, halves[0]])
-        quantize_part("x", 1, 0)
-        quantize_part("z", 1, 0)
-        gather(7, HALF, M, late_x[:, halves[1]])
-        nc.scalar.activation(out=woven(bf["z", 1, 1], 2, 4, 0, HALF), in_=late_rows, func=SQUARE)
-
-        def open_banks():
-            return {(kind, n): bank(first + n) for kind, first in (("x", 0), ("z", 4)) for n in range(4)}
-
-        def finish(acc, n, j):
-            half_sq = ring.tile([P, HALF], F32, name="half_sq", tag="half_sq", bufs=4)
-            nc.scalar.activation(out=half_sq[:], in_=acc["x", n][:], func=SQUARE, scale=0.5**0.5)
-            pieces = 2 if (j, n) == (1, 3) else 1
-            width = HALF // pieces
-            for piece in range(pieces):
-                cols = slice(width * piece, width * (piece + 1))
-                res = staged[j][:, HALF * n : HALF * (n + 1)][:, cols]
-                nc.vector.scalar_tensor_tensor(
-                    out=res, in0=acc["z", n][:, cols], scalar=-0.5, in1=half_sq[:, cols], op0=MULT, op1=ADD
-                )
-                nc.sync.dma_start(out=out[P * n : P * (n + 1), halves[j]][:, cols], in_=res)
-
-        acc = open_banks()
-        for kind in "zx":
-            for n in range(4):
-                product(acc[kind, n], kind, n, 0, 0)
-        for kind, n in (("x", 0), ("x", 1), ("z", 0), ("x", 2), ("z", 1), ("x", 3), ("z", 2), ("z", 3)):
-            product(acc[kind, n], kind, n, 1, 0)
-        finish(acc, 0, 0)
-        nc.vector.tensor_copy(out=woven(bf["x", 1, 1], 2, 4, 0, HALF), in_=late_rows)
-        finish(acc, 1, 0)
-        quantize_part("x", 1, 1)
-        quantize_part("z", 1, 1)
-        for n in range(2, 4):
-            finish(acc, n, 0)
-
-        acc = open_banks()
-        early = [("x", 0), ("x", 1), ("z", 0), ("x", 2), ("x", 3), ("z", 1)]
-        for a in range(2):
-            for kind, n in early:
-                product(acc[kind, n], kind, n, a, 1)
-        for n in range(2, 4):
-            for a in range(2):
-                product(acc["z", n], "z", n, a, 1)
-        for n in range(4):
-            finish(acc, n, 1)
+        quantize_places(0, 2)
+        fetch(0)
+        quantize(fw_codes[:], fw_sc[:], fw_bf[:])
+        fetch(1)
+        for c in range(2):
+            quantize_places(4 * c + 2, 4 * c + 6)
+            multiply(c)
+            fetch(c + 2)
+        finish(0)
+        quantize_places(10, 14)
+        multiply(2)
+        finish(1)
+        quantize_places(14, 15)
+        quantize_places(15, 16)
+        multiply(3)
+        finish(2)
+        finish(3)

@@ -17,6 +17,7 @@ FP4X4 = mybir.dt.float4_e2m1fn_x4
 MULT = mybir.AluOpType.mult
 ADD = mybir.AluOpType.add
 SQUARE = mybir.ActivationFunctionType.Square
+COPY = mybir.ActivationFunctionType.Copy
 
 P = 128
 PACK = 4
@@ -256,7 +257,13 @@ def tile_list_gift_interactions_kernel(
 
         def round_chunk(a, c, rows):
             u = place("x", a, c)
-            nc.scalar.copy(out=woven(rounded[:, WOVEN * u : WOVEN * (u + 1)]), in_=by_fours(rows))
+            if (a, c) == (1, 1):
+                nc.gpsimd.tensor_scalar(
+                    out=woven(rounded[:, WOVEN * u : WOVEN * (u + 1)]), in0=by_fours(rows),
+                    scalar1=1.0, scalar2=0.0, op0=MULT, op1=ADD,
+                )
+            else:
+                nc.scalar.copy(out=woven(rounded[:, WOVEN * u : WOVEN * (u + 1)]), in_=by_fours(rows))
             nc.scalar.activation(out=woven(rounded[:, WOVEN * (u + 1) : WOVEN * (u + 2)]), in_=by_fours(rows), func=SQUARE)
 
         for j in range(2):
@@ -275,11 +282,16 @@ def tile_list_gift_interactions_kernel(
         for i in range(PACK, SLICES):
             scatter(i)
 
-        codes = ring.tile([P, 4 * M], U32, name="codes", tag="xs0", align_bytes=64)
+        codes_first = ring.tile([P, 2 * CHUNK], U32, name="codes_first", align_bytes=64)
+        codes_rest = ring.tile([P, 4 * M - 2 * CHUNK], U32, name="codes_rest", tag="xs0", align_bytes=64)
+
+        def codes_of(lo, hi):
+            if lo < 2:
+                return codes_first[:, CHUNK * lo : CHUNK * hi]
+            return codes_rest[:, CHUNK * (lo - 2) : CHUNK * (hi - 2)]
 
         def quantize_places(lo, hi):
-            cols = slice(CHUNK * lo, CHUNK * hi)
-            quantize(codes[:, cols], scales[:, cols], rounded[:, WOVEN * lo : WOVEN * hi])
+            quantize(codes_of(lo, hi), scales[:, CHUNK * lo : CHUNK * hi], rounded[:, WOVEN * lo : WOVEN * hi])
 
         def fetch(c):
             rows = x1_rows[c % 2]
@@ -309,14 +321,26 @@ def tile_list_gift_interactions_kernel(
                             out=sums[kind, c, n // 2][:, CHUNK * (n % 2) : CHUNK * (n % 2 + 1)],
                             lhsT=lhs.bitcast(FP8X4),
                             lhsT_scale=lhs_sc,
-                            rhs=codes[:, cols].bitcast(FP8X4),
+                            rhs=codes_of(u, u + 1).bitcast(FP8X4),
                             rhs_scale=scales[:, cols],
                             start=(a == 0 and n % 2 == 0),
                             stop=(a == 1 and n % 2 == 1),
                         )
             for pair in range(2):
-                squares[c, pair] = ring.tile([P, HALF], F32, name="half_sq", tag="half_sq", bufs=4)
+                squares[c, pair] = ring.tile([P, HALF], F32, name="half_sq", tag="half_sq", bufs=6)
                 nc.scalar.activation(out=squares[c, pair][:], in_=sums["x", c, pair][:], func=SQUARE, scale=0.5**0.5)
+
+        def finish_aside(c):
+            for pair in range(2):
+                half_b = ring.tile([P, HALF], F32, name="half_b", tag="half_sq", bufs=6)
+                nc.scalar.activation(out=half_b[:], in_=sums["z", c, pair][:], func=COPY, scale=-0.5)
+                first = 2 * HALF * (c % 2) + HALF * pair
+                res = staged[c // 2][:, first : first + HALF]
+                nc.gpsimd.tensor_tensor(out=res, in0=squares[c, pair][:], in1=half_b[:], op=ADD)
+                rows = out[2 * P * pair : 2 * P * (pair + 1), CHUNK * c : CHUNK * (c + 1)]
+                nc.sync.dma_start(
+                    out=rows.rearrange("(n p) m -> p n m", p=P), in_=res.rearrange("p (n m) -> p n m", m=CHUNK)
+                )
 
         def finish(c):
             for pair in range(2):
@@ -340,8 +364,9 @@ def tile_list_gift_interactions_kernel(
         for c in range(2):
             quantize_places(4 * c + 2, 4 * c + 6)
             multiply(c)
+            if c == 0:
+                finish_aside(0)
             fetch(c + 2)
-        finish(0)
         quantize_places(10, 14)
         multiply(2)
         finish(1)

@@ -116,11 +116,9 @@ def tile_list_gift_interactions_kernel(
         nc.sync.dma_start(idx[:], offs)
         nc.sync.dma_start(out=tab_sc[0:32, :].bitcast(I32), in_=tab_scales.rearrange("a q c -> (a q) c").bitcast(I32))
         nc.sync.dma_start(out=w1_sc[0:32, :].bitcast(I32), in_=w1_scales.rearrange("a q c -> (a q) c").bitcast(I32))
+        load_table(0, 0, T)
         load_wgs(0)
         load_w1(0)
-        nc.sync.dma_start(idx2[:], offs2)
-        nc.sync.dma_start(idx3[:], offs3)
-        load_table(0, 0, T)
         load_table(1, 0, TABLE_CUT)
 
         for rows_sc in (tab_sc, w1_sc):
@@ -160,13 +158,15 @@ def tile_list_gift_interactions_kernel(
         nc.vector.memset(sq_sc[:].bitcast(I32), 0)
 
         moves = [(0, 1), (0, 2), (0, 3), (1, 0), (1, 2), (1, 1), (1, 3)]
-        move_scales(moves[:5], slice(0, EARLY_W))
+        move_scales(moves[:3], slice(0, EARLY_W))
         load_table(1, TABLE_CUT, T)
-        move_scales(moves[5:], slice(0, EARLY_W))
+        move_scales(moves[3:], slice(0, EARLY_W))
+        nc.sync.dma_start(idx2[:], offs2)
         load_page(0)
         load_wgs(1)
         load_page(1)
         move_scales(moves, slice(EARLY_W, PLANE_W))
+        nc.sync.dma_start(idx3[:], offs3)
         load_wgs(2)
         load_page(2)
         load_wgs(3)
@@ -257,13 +257,15 @@ def tile_list_gift_interactions_kernel(
 
         def round_chunk(a, c, rows):
             u = place("x", a, c)
-            if (a, c) == (1, 1):
+            aside = (0, CHUNK, 0, CHUNK // 2)[c] if a == 1 else 0
+            x_bf = rounded[:, WOVEN * u : WOVEN * (u + 1)]
+            if aside > 0:
                 nc.gpsimd.tensor_scalar(
-                    out=woven(rounded[:, WOVEN * u : WOVEN * (u + 1)]), in0=by_fours(rows),
+                    out=woven(x_bf[:, 0 : PACK * aside]), in0=by_fours(rows[:, :, 0:aside]),
                     scalar1=1.0, scalar2=0.0, op0=MULT, op1=ADD,
                 )
-            else:
-                nc.scalar.copy(out=woven(rounded[:, WOVEN * u : WOVEN * (u + 1)]), in_=by_fours(rows))
+            if aside < CHUNK:
+                nc.scalar.copy(out=woven(x_bf[:, PACK * aside :]), in_=by_fours(rows[:, :, aside:]))
             nc.scalar.activation(out=woven(rounded[:, WOVEN * (u + 1) : WOVEN * (u + 2)]), in_=by_fours(rows), func=SQUARE)
 
         for j in range(2):
@@ -307,11 +309,16 @@ def tile_list_gift_interactions_kernel(
             for kind in "xz":
                 for pair in range(2):
                     sums[kind, c, pair] = bank(4 * (c % 2) + 2 * "xz".index(kind) + pair)
-            for a in range(2):
-                for kind in "xz":
+            steps = [(kind, a, n) for a in range(2) for kind in "xz" for n in range(4)]
+            if c == CHUNKS - 1:
+                steps = [s for s in steps if s[0] == "x"]
+                steps += [("z", a, 2 * pair + n) for pair in range(2) for a in (1, 0) for n in range(2)]
+            for kind, a, n in steps:
+                in_bank = [s for s in steps if s[0] == kind and s[2] // 2 == n // 2]
+                if True:
                     u = place(kind, a, c)
                     cols = slice(CHUNK * u, CHUNK * (u + 1))
-                    for n in range(4):
+                    if True:
                         ncols = slice(N * a + P * n, N * a + P * (n + 1))
                         if kind == "x":
                             lhs, lhs_sc = fw_codes[:, ncols], fw_sc[:, ncols]
@@ -323,20 +330,21 @@ def tile_list_gift_interactions_kernel(
                             lhsT_scale=lhs_sc,
                             rhs=codes_of(u, u + 1).bitcast(FP8X4),
                             rhs_scale=scales[:, cols],
-                            start=(a == 0 and n % 2 == 0),
-                            stop=(a == 1 and n % 2 == 1),
+                            start=((kind, a, n) == in_bank[0]),
+                            stop=((kind, a, n) == in_bank[-1]),
                         )
             for pair in range(2):
-                squares[c, pair] = ring.tile([P, HALF], F32, name="half_sq", tag="half_sq", bufs=6)
+                squares[c, pair] = ring.tile([P, HALF], F32, name="half_sq", tag="half_sq", bufs=4)
                 nc.scalar.activation(out=squares[c, pair][:], in_=sums["x", c, pair][:], func=SQUARE, scale=0.5**0.5)
 
         def finish_aside(c):
             for pair in range(2):
-                half_b = ring.tile([P, HALF], F32, name="half_b", tag="half_sq", bufs=6)
-                nc.scalar.activation(out=half_b[:], in_=sums["z", c, pair][:], func=COPY, scale=-0.5)
+                u = place("zx"[pair], 1, CHUNKS - 1)
+                half_b = rounded[:, WOVEN * u : WOVEN * (u + 1)].bitcast(F32)
+                nc.scalar.activation(out=half_b, in_=sums["z", c, pair][:], func=COPY, scale=-0.5)
                 first = 2 * HALF * (c % 2) + HALF * pair
                 res = staged[c // 2][:, first : first + HALF]
-                nc.gpsimd.tensor_tensor(out=res, in0=squares[c, pair][:], in1=half_b[:], op=ADD)
+                nc.gpsimd.tensor_tensor(out=res, in0=squares[c, pair][:], in1=half_b, op=ADD)
                 rows = out[2 * P * pair : 2 * P * (pair + 1), CHUNK * c : CHUNK * (c + 1)]
                 nc.sync.dma_start(
                     out=rows.rearrange("(n p) m -> p n m", p=P), in_=res.rearrange("p (n m) -> p n m", m=CHUNK)

@@ -23,11 +23,10 @@ P = 128
 PACK = 4
 SLICES = 8
 HALF = 512
-W1_COL = HALF
-V_COL = (0, HALF + H)
 PLANE_W = S + H
-EARLY_W = W1_COL + 2 * P
-TABLE_CUT = T // 4
+EARLY_W = HALF + 2 * P
+LATE_W = PLANE_W - EARLY_W
+TABLE_CUT = 3 * T // 8
 CHUNK = 256
 CHUNKS = M // CHUNK
 WOVEN = PACK * CHUNK
@@ -50,18 +49,16 @@ def tile_list_gift_interactions_kernel(
             return psum.tile([P, HALF], F32, name="bank%d" % b, tag="bank%d" % b)
 
         halves = [slice(0, HALF), slice(HALF, S)]
-        planes = [keep.tile([P, PLANE_W], U8, name="plane%d" % k, align_bytes=64) for k in range(2)]
+        planes = keep.tile([P, 2 * PLANE_W], U8, name="planes", align_bytes=64)
+        stage = keep.tile([P, PLANE_W], U8, name="stage", align_bytes=64)
         tab_sc = keep.tile([P, T], U8, name="tab_sc", align_bytes=64)
         w1_sc = keep.tile([P, H], U8, name="w1_sc", align_bytes=64)
         tab = [keep.tile([P, T], I32, name="tab%d" % k, tag="big%d" % k, align_bytes=64) for k in range(2)]
         w1_raw = [keep.tile([P, 2 * H], U8, name="w1_raw0", align_bytes=64)]
         w1_perm = [keep.tile([P, 2 * H], U8, name="w1_perm%d" % a, align_bytes=64) for a in range(2)]
         wgs_rows = [keep.tile([P, S // 4], F32, name="wgs_rows0")]
-        wg = [keep.tile([P, S], F32, name="wg%d" % t) for t in range(PACK)]
-        v = [keep.tile([P, S], U32, name="v%d" % k, align_bytes=64) for k in range(2)]
+        wg = [keep.tile([P, S], F32, name="wg%d" % t, tag="wg%d" % t) for t in range(PACK)]
         fw_bf = keep.tile([P, 2 * N * PACK], BF16, name="fw_bf", align_bytes=64)
-        fw_codes = keep.tile([P, 2 * N], U32, name="fw_codes", align_bytes=64)
-        fw_sc = keep.tile([P, 2 * N], U8, name="fw_sc", align_bytes=64)
         ident = keep.tile([P, P], F32, name="ident")
         make_identity(nc, ident[:])
 
@@ -84,11 +81,16 @@ def tile_list_gift_interactions_kernel(
                 out=pages[i][:], in_=page0[HALF * a : HALF * (a + 1), :].rearrange("(p t) c -> t p c", t=PACK)[t]
             )
 
-        def move_scales(moves, cols):
-            for k, q in moves:
+        def v_col(k, j):
+            return EARLY_W * k if j == 0 else 2 * EARLY_W + LATE_W * (k + 1) - HALF
+
+        def w1_col(k, i):
+            return EARLY_W * k + HALF + P * i if i < 2 else 2 * EARLY_W + LATE_W * k + P * (i - 2)
+
+        def move_scales(lo, hi):
+            for q in range(4):
                 nc.sync.dma_start(
-                    out=planes[k][32 * q : 32 * q + 4, cols].bitcast(I32),
-                    in_=planes[0][16 * k + 4 * q : 16 * k + 4 * q + 4, cols].bitcast(I32),
+                    out=planes[32 * q : 32 * q + 4, 2 * lo : 2 * hi].bitcast(I32), in_=stage[8 * q : 8 * q + 8, lo:hi].bitcast(I32)
                 )
 
         def permute_w1(engine_copy, a):
@@ -114,58 +116,55 @@ def tile_list_gift_interactions_kernel(
                 nc.scalar.copy(out=wg[t][:, halves[j]], in_=back[:])
 
         nc.sync.dma_start(idx[:], offs)
-        nc.sync.dma_start(out=tab_sc[0:32, :].bitcast(I32), in_=tab_scales.rearrange("a q c -> (a q) c").bitcast(I32))
-        nc.sync.dma_start(out=w1_sc[0:32, :].bitcast(I32), in_=w1_scales.rearrange("a q c -> (a q) c").bitcast(I32))
+        nc.sync.dma_start(out=tab_sc[0:32, :].bitcast(I32), in_=tab_scales.rearrange("a q c -> q a c").bitcast(I32))
+        nc.sync.dma_start(out=w1_sc[0:32, :].bitcast(I32), in_=w1_scales.rearrange("a q c -> q a c").bitcast(I32))
         load_table(0, 0, T)
         load_wgs(0)
         load_w1(0)
         load_table(1, 0, TABLE_CUT)
-
         for rows_sc in (tab_sc, w1_sc):
             for lo, hi in ((32, 64), (64, 128)):
                 nc.vector.memset(rows_sc[lo:hi, :].bitcast(I32), 0)
-        nc.vector.memset(planes[1][:].bitcast(I32), 0)
+        nc.vector.memset(planes[:].bitcast(I32), 0)
 
         def gather_scales(j, got):
             nc.vector.tensor_copy(got[:], tab_sc[:].indirect(idx[:, 32 * j : 32 * (j + 1)]))
 
-        def lay_scales(j, got):
-            nc.vector.tensor_copy(out=planes[0][:, V_COL[j] : V_COL[j] + HALF].bitcast(I32), in_=got[:].bitcast(I32))
-
-        dealt_sc = planes[0][:, W1_COL : W1_COL + H].rearrange("p (a t m) -> p a t m", a=2, t=PACK)
+        dealt_sc = stage[:, HALF : HALF + H].rearrange("p (a t m) -> p a t m", a=2, t=PACK)
         given_sc = w1_sc[:].rearrange("p (a m t) -> p a t m", a=2, t=PACK)
         got_late = keep.tile([P, HALF], U8, name="got_late", align_bytes=64)
         with tc.tile_pool(name="head", bufs=1) as head:
             got_early = head.tile([P, HALF], U8, name="got_early", align_bytes=64)
             gather_scales(0, got_early)
             nc.vector.tensor_copy(out=dealt_sc[:, 0, 0:2, :], in_=given_sc[:, 0, 0:2, :])
-            lay_scales(0, got_early)
+            nc.vector.tensor_copy(out=stage[:, 0:HALF].bitcast(I32), in_=got_early[:].bitcast(I32))
+        permute_w1(nc.vector.tensor_copy, 0)
         gather_scales(1, got_late)
         nc.vector.tensor_copy(out=dealt_sc[:, 0, 2:4, :], in_=given_sc[:, 0, 2:4, :])
-        lay_scales(1, got_late)
         nc.vector.tensor_copy(out=dealt_sc[:, 1, :, :], in_=given_sc[:, 1, :, :])
-        permute_w1(nc.vector.tensor_copy, 0)
+        nc.vector.tensor_copy(out=stage[:, HALF + H :].bitcast(I32), in_=got_late[:].bitcast(I32))
         deal_weights(0)
 
         ring = ctx.enter_context(tc.tile_pool(name="ring", bufs=1))
-        pages = [ring.tile([P, T2], F32, name="page%d" % i) for i in range(SLICES)]
+        pages = [ring.tile([P, T2], F32, name="page%d" % i, tag="page%d" % i, align_bytes=64) for i in range(SLICES)]
+        v = [ring.tile([P, S], U32, name="v%d" % k, tag="v%d" % k, align_bytes=64) for k in range(2)]
         w1_raw.append(ring.tile([P, 2 * H], U8, name="w1_raw1", align_bytes=64))
         wgs_rows.extend(ring.tile([P, S // 4], F32, name="wgs_rows%d" % t) for t in range(1, PACK))
         xs0 = ring.tile([P, PACK * M], F32, name="xs0", tag="xs0", align_bytes=64)
         xs1 = ring.tile([P, 2 * WOVEN], F32, name="xs1")
+        fw_codes = ring.tile([P, 2 * N], U32, name="fw_codes", align_bytes=64)
         sq_codes = ring.tile([P, 2 * N], I32, name="sq_codes", align_bytes=64)
         sq_sc = ring.tile([P, N], U8, name="sq_sc", align_bytes=64)
+        fw_sc = ring.tile([P, 2 * N], U8, name="fw_sc", align_bytes=64)
         nc.vector.memset(sq_sc[:].bitcast(I32), 0)
 
-        moves = [(0, 1), (0, 2), (0, 3), (1, 0), (1, 2), (1, 1), (1, 3)]
-        move_scales(moves[:3], slice(0, EARLY_W))
+        move_scales(0, EARLY_W)
         load_table(1, TABLE_CUT, T)
-        move_scales(moves[3:], slice(0, EARLY_W))
         nc.sync.dma_start(idx2[:], offs2)
         load_page(0)
         load_wgs(1)
         load_page(1)
-        move_scales(moves, slice(EARLY_W, PLANE_W))
+        move_scales(EARLY_W, PLANE_W)
         nc.sync.dma_start(idx3[:], offs3)
         load_wgs(2)
         load_page(2)
@@ -207,12 +206,14 @@ def tile_list_gift_interactions_kernel(
             acc = bank(b)[:, 0 : hi - lo]
             for k in range(2):
                 first = 2 * (HALF * k + P * t)
+                w1_at = w1_col(k, i)
+                v_at = v_col(k, j) + first_col
                 nc.tensor.matmul_mx(
                     out=acc,
                     lhsT=w1_perm[a][:, first : first + 2 * P].bitcast(FP4X4),
-                    lhsT_scale=planes[k][:, W1_COL + P * i : W1_COL + P * (i + 1)],
+                    lhsT_scale=planes[:, w1_at : w1_at + P],
                     rhs=v[k][:, lo:hi].bitcast(FP8X4),
-                    rhs_scale=planes[k][:, V_COL[j] + first_col : V_COL[j] + first_col + hi - lo],
+                    rhs_scale=planes[:, v_at : v_at + hi - lo],
                     start=(k == 0),
                     stop=(k == 1),
                 )
@@ -315,24 +316,22 @@ def tile_list_gift_interactions_kernel(
                 steps += [("z", a, 2 * pair + n) for pair in range(2) for a in (1, 0) for n in range(2)]
             for kind, a, n in steps:
                 in_bank = [s for s in steps if s[0] == kind and s[2] // 2 == n // 2]
-                if True:
-                    u = place(kind, a, c)
-                    cols = slice(CHUNK * u, CHUNK * (u + 1))
-                    if True:
-                        ncols = slice(N * a + P * n, N * a + P * (n + 1))
-                        if kind == "x":
-                            lhs, lhs_sc = fw_codes[:, ncols], fw_sc[:, ncols]
-                        else:
-                            lhs, lhs_sc = sq_codes[:, ncols], sq_sc[4 * a : P, P * n : P * (n + 1)]
-                        nc.tensor.matmul_mx(
-                            out=sums[kind, c, n // 2][:, CHUNK * (n % 2) : CHUNK * (n % 2 + 1)],
-                            lhsT=lhs.bitcast(FP8X4),
-                            lhsT_scale=lhs_sc,
-                            rhs=codes_of(u, u + 1).bitcast(FP8X4),
-                            rhs_scale=scales[:, cols],
-                            start=((kind, a, n) == in_bank[0]),
-                            stop=((kind, a, n) == in_bank[-1]),
-                        )
+                u = place(kind, a, c)
+                cols = slice(CHUNK * u, CHUNK * (u + 1))
+                ncols = slice(N * a + P * n, N * a + P * (n + 1))
+                if kind == "x":
+                    lhs, lhs_sc = fw_codes[:, ncols], fw_sc[:, ncols]
+                else:
+                    lhs, lhs_sc = sq_codes[:, ncols], sq_sc[4 * a : P, P * n : P * (n + 1)]
+                nc.tensor.matmul_mx(
+                    out=sums[kind, c, n // 2][:, CHUNK * (n % 2) : CHUNK * (n % 2 + 1)],
+                    lhsT=lhs.bitcast(FP8X4),
+                    lhsT_scale=lhs_sc,
+                    rhs=codes_of(u, u + 1).bitcast(FP8X4),
+                    rhs_scale=scales[:, cols],
+                    start=((kind, a, n) == in_bank[0]),
+                    stop=((kind, a, n) == in_bank[-1]),
+                )
             for pair in range(2):
                 squares[c, pair] = ring.tile([P, HALF], F32, name="half_sq", tag="half_sq", bufs=4)
                 nc.scalar.activation(out=squares[c, pair][:], in_=sums["x", c, pair][:], func=SQUARE, scale=0.5**0.5)

@@ -26,7 +26,7 @@ HALF = 512
 PLANE_W = S + H
 EARLY_W = HALF + 2 * P
 LATE_W = PLANE_W - EARLY_W
-TABLE_CUT = 3 * T // 8
+TABLE_CUT = 5 * T // 8
 CHUNK = 256
 CHUNKS = M // CHUNK
 WOVEN = PACK * CHUNK
@@ -54,8 +54,8 @@ def tile_list_gift_interactions_kernel(
         tab_sc = keep.tile([P, T], U8, name="tab_sc", align_bytes=64)
         w1_sc = keep.tile([P, H], U8, name="w1_sc", align_bytes=64)
         tab = [keep.tile([P, T], I32, name="tab%d" % k, tag="big%d" % k, align_bytes=64) for k in range(2)]
-        w1_raw = [keep.tile([P, 2 * H], U8, name="w1_raw0", align_bytes=64)]
-        w1_perm = [keep.tile([P, 2 * H], U8, name="w1_perm%d" % a, align_bytes=64) for a in range(2)]
+        w1_raw = {(0, 0): keep.tile([P, H], U8, name="w1_raw00", align_bytes=64)}
+        w1_perm = {(a, k): keep.tile([P, H], U8, name="w1_perm%d%d" % (a, k), align_bytes=64) for a in range(2) for k in range(2)}
         wgs_rows = [keep.tile([P, S // 4], F32, name="wgs_rows0")]
         wg = [keep.tile([P, S], F32, name="wg%d" % t, tag="wg%d" % t) for t in range(PACK)]
         fw_bf = keep.tile([P, 2 * N * PACK], BF16, name="fw_bf", align_bytes=64)
@@ -69,11 +69,8 @@ def tile_list_gift_interactions_kernel(
         def load_wgs(t):
             nc.sync.dma_start(out=wgs_rows[t][:], in_=wgs.rearrange("(q t) (u c) -> t q u c", t=PACK, u=4)[t])
 
-        def load_w1(a):
-            nc.sync.dma_start(
-                out=w1_raw[a][:].bitcast(I32).rearrange("p (k c) -> p k c", k=2),
-                in_=w1_words.bitcast(I32).rearrange("k p (a c) -> a p k c", a=2)[a],
-            )
+        def load_w1(a, k):
+            nc.sync.dma_start(out=w1_raw[a, k][:].bitcast(I32), in_=w1_words[k][:, H * a : H * (a + 1)].bitcast(I32))
 
         def load_page(i):
             a, t = divmod(i, PACK)
@@ -93,10 +90,10 @@ def tile_list_gift_interactions_kernel(
                     out=planes[32 * q : 32 * q + 4, 2 * lo : 2 * hi].bitcast(I32), in_=stage[8 * q : 8 * q + 8, lo:hi].bitcast(I32)
                 )
 
-        def permute_w1(engine_copy, a):
+        def permute_w1(engine_copy, a, k, lo=0, hi=PACK):
             engine_copy(
-                out=w1_perm[a][:].bitcast(U16).rearrange("p (k t m) -> p k t m", k=2, t=PACK),
-                in_=w1_raw[a][:].bitcast(U16).rearrange("p (k m t) -> p k t m", k=2, t=PACK),
+                out=w1_perm[a, k][:].bitcast(U16).rearrange("p (t m) -> p t m", t=PACK)[:, lo:hi, :],
+                in_=w1_raw[a, k][:].bitcast(U16).rearrange("p (m t) -> p t m", t=PACK)[:, lo:hi, :],
             )
 
         def deal_weights(t):
@@ -120,7 +117,7 @@ def tile_list_gift_interactions_kernel(
         nc.sync.dma_start(out=w1_sc[0:32, :].bitcast(I32), in_=w1_scales.rearrange("a q c -> q a c").bitcast(I32))
         load_table(0, 0, T)
         load_wgs(0)
-        load_w1(0)
+        load_w1(0, 0)
         load_table(1, 0, TABLE_CUT)
         for rows_sc in (tab_sc, w1_sc):
             for lo, hi in ((32, 64), (64, 128)):
@@ -138,7 +135,7 @@ def tile_list_gift_interactions_kernel(
             gather_scales(0, got_early)
             nc.vector.tensor_copy(out=dealt_sc[:, 0, 0:2, :], in_=given_sc[:, 0, 0:2, :])
             nc.vector.tensor_copy(out=stage[:, 0:HALF].bitcast(I32), in_=got_early[:].bitcast(I32))
-        permute_w1(nc.vector.tensor_copy, 0)
+        permute_w1(nc.vector.tensor_copy, 0, 0)
         gather_scales(1, got_late)
         nc.vector.tensor_copy(out=dealt_sc[:, 0, 2:4, :], in_=given_sc[:, 0, 2:4, :])
         nc.vector.tensor_copy(out=dealt_sc[:, 1, :, :], in_=given_sc[:, 1, :, :])
@@ -148,7 +145,8 @@ def tile_list_gift_interactions_kernel(
         ring = ctx.enter_context(tc.tile_pool(name="ring", bufs=1))
         pages = [ring.tile([P, T2], F32, name="page%d" % i, tag="page%d" % i, align_bytes=64) for i in range(SLICES)]
         v = [ring.tile([P, S], U32, name="v%d" % k, tag="v%d" % k, align_bytes=64) for k in range(2)]
-        w1_raw.append(ring.tile([P, 2 * H], U8, name="w1_raw1", align_bytes=64))
+        for a, k in ((0, 1), (1, 0), (1, 1)):
+            w1_raw[a, k] = ring.tile([P, H], U8, name="w1_raw%d%d" % (a, k), align_bytes=64)
         wgs_rows.extend(ring.tile([P, S // 4], F32, name="wgs_rows%d" % t) for t in range(1, PACK))
         xs0 = ring.tile([P, PACK * M], F32, name="xs0", tag="xs0", align_bytes=64)
         xs1 = ring.tile([P, 2 * WOVEN], F32, name="xs1")
@@ -160,6 +158,7 @@ def tile_list_gift_interactions_kernel(
 
         move_scales(0, EARLY_W)
         load_table(1, TABLE_CUT, T)
+        load_w1(0, 1)
         nc.sync.dma_start(idx2[:], offs2)
         load_page(0)
         load_wgs(1)
@@ -169,7 +168,8 @@ def tile_list_gift_interactions_kernel(
         load_wgs(2)
         load_page(2)
         load_wgs(3)
-        load_w1(1)
+        for k in range(2):
+            load_w1(1, k)
         load_page(3)
         x0_rows = xs0[:].rearrange("p (t m) -> p t m", t=PACK)
         fw_rows = fw.rearrange("(a p t) n -> a p t n", a=2, t=PACK)
@@ -205,12 +205,11 @@ def tile_list_gift_interactions_kernel(
             j, first_col = divmod(lo, HALF)
             acc = bank(b)[:, 0 : hi - lo]
             for k in range(2):
-                first = 2 * (HALF * k + P * t)
                 w1_at = w1_col(k, i)
                 v_at = v_col(k, j) + first_col
                 nc.tensor.matmul_mx(
                     out=acc,
-                    lhsT=w1_perm[a][:, first : first + 2 * P].bitcast(FP4X4),
+                    lhsT=w1_perm[a, k][:, 2 * P * t : 2 * P * (t + 1)].bitcast(FP4X4),
                     lhsT_scale=planes[:, w1_at : w1_at + P],
                     rhs=v[k][:, lo:hi].bitcast(FP8X4),
                     rhs_scale=planes[:, v_at : v_at + hi - lo],
@@ -219,6 +218,7 @@ def tile_list_gift_interactions_kernel(
                 )
             nc.scalar.copy(out=h_of(i)[:, lo:hi], in_=acc)
 
+        permute_w1(nc.scalar.copy, 0, 1, 0, 2)
         for b in range(2):
             make_h(0, 256 * b, 256 * (b + 1), b)
         make_h(1, 0, HALF, 2)
@@ -228,8 +228,11 @@ def tile_list_gift_interactions_kernel(
         for i in range(2, SLICES):
             if i < PACK:
                 deal_weights(i)
+            if i == 2:
+                permute_w1(nc.scalar.copy, 0, 1, 2, PACK)
             if i == PACK:
-                permute_w1(nc.scalar.copy, 1)
+                for k in range(2):
+                    permute_w1(nc.scalar.copy, 1, k)
             for j in range(2):
                 make_h(i, HALF * j, HALF * (j + 1), (2 * i + j) % 4)
 
@@ -288,7 +291,11 @@ def tile_list_gift_interactions_kernel(
         codes_first = ring.tile([P, 2 * CHUNK], U32, name="codes_first", align_bytes=64)
         codes_rest = ring.tile([P, 4 * M - 2 * CHUNK], U32, name="codes_rest", tag="xs0", align_bytes=64)
 
+        codes_last = []
+
         def codes_of(lo, hi):
+            if 12 <= lo < 14:
+                return codes_last[0][:, CHUNK * (lo - 12) : CHUNK * (hi - 12)]
             if lo < 2:
                 return codes_first[:, CHUNK * lo : CHUNK * hi]
             return codes_rest[:, CHUNK * (lo - 2) : CHUNK * (hi - 2)]
@@ -299,6 +306,9 @@ def tile_list_gift_interactions_kernel(
         def fetch(c):
             rows = x1_rows[c % 2]
             for t in range(PACK):
+                if (c, t) == (CHUNKS - 1, PACK - 1):
+                    codes_last.append(ring.tile([P, 2 * CHUNK], U32, name="codes_last", tag="page5", align_bytes=64))
+                    quantize_places(12, 14)
                 gather(PACK + t, rows[:, t, :], CHUNK * c, CHUNK * (c + 1))
             round_chunk(1, c, rows)
 
@@ -374,7 +384,7 @@ def tile_list_gift_interactions_kernel(
             if c == 0:
                 finish_aside(0)
             fetch(c + 2)
-        quantize_places(10, 14)
+        quantize_places(10, 12)
         multiply(2)
         finish(1)
         quantize_places(14, 15)

@@ -259,10 +259,13 @@ def tile_list_gift_interactions_kernel(
         rounded = ring.tile([P, 4 * CHUNKS * WOVEN], BF16, name="rounded", align_bytes=64)
         scales = ring.tile([P, 4 * M], U8, name="scales", align_bytes=64)
 
+        def start_of(u):
+            return WOVEN * u - (WOVEN // 2 if u >= place("x", 1, CHUNKS - 1) else 0)
+
         def round_chunk(a, c, rows):
             u = place("x", a, c)
             aside = (0, CHUNK, 0, CHUNK // 2)[c] if a == 1 else 0
-            x_bf = rounded[:, WOVEN * u : WOVEN * (u + 1)]
+            x_bf = rounded[:, start_of(u) : start_of(u) + WOVEN]
             if aside > 0:
                 nc.gpsimd.tensor_scalar(
                     out=woven(x_bf[:, 0 : PACK * aside]), in0=by_fours(rows[:, :, 0:aside]),
@@ -270,7 +273,7 @@ def tile_list_gift_interactions_kernel(
                 )
             if aside < CHUNK:
                 nc.scalar.copy(out=woven(x_bf[:, PACK * aside :]), in_=by_fours(rows[:, :, aside:]))
-            nc.scalar.activation(out=woven(rounded[:, WOVEN * (u + 1) : WOVEN * (u + 2)]), in_=by_fours(rows), func=SQUARE)
+            nc.scalar.activation(out=woven(rounded[:, start_of(u + 1) : start_of(u + 1) + WOVEN]), in_=by_fours(rows), func=SQUARE)
 
         for j in range(2):
             for i in range(2):
@@ -301,15 +304,15 @@ def tile_list_gift_interactions_kernel(
             return codes_rest[:, CHUNK * (lo - 2) : CHUNK * (hi - 2)]
 
         def quantize_places(lo, hi):
-            quantize(codes_of(lo, hi), scales[:, CHUNK * lo : CHUNK * hi], rounded[:, WOVEN * lo : WOVEN * hi])
+            quantize(codes_of(lo, hi), scales[:, CHUNK * lo : CHUNK * hi], rounded[:, start_of(lo) : start_of(lo) + WOVEN * (hi - lo)])
 
         def fetch(c):
             rows = x1_rows[c % 2]
             for t in range(PACK):
-                if (c, t) == (CHUNKS - 1, PACK - 1):
-                    codes_last.append(ring.tile([P, 2 * CHUNK], U32, name="codes_last", tag="page5", align_bytes=64))
-                    quantize_places(12, 14)
                 gather(PACK + t, rows[:, t, :], CHUNK * c, CHUNK * (c + 1))
+            if c == CHUNKS - 1:
+                codes_last.append(ring.tile([P, 2 * CHUNK], U32, name="codes_last", tag="page5", align_bytes=64))
+                quantize_places(12, 14)
             round_chunk(1, c, rows)
 
         staged = [keep.tile([P, 8 * CHUNK], F32, name="staged%d" % j, tag="big%d" % j, align_bytes=64) for j in range(2)]
@@ -348,7 +351,7 @@ def tile_list_gift_interactions_kernel(
 
         def finish_aside(c):
             for pair in range(2):
-                u = place("zx"[pair], 1, CHUNKS - 1)
+                u = place("xz"[pair], 1, CHUNKS - 1)
                 half_b = rounded[:, WOVEN * u : WOVEN * (u + 1)].bitcast(F32)
                 nc.scalar.activation(out=half_b, in_=sums["z", c, pair][:], func=COPY, scale=-0.5)
                 first = 2 * HALF * (c % 2) + HALF * pair

from contextlib import ExitStack

import concourse.mybir as mybir
from concourse.masks import make_identity

K, T, S, H, T2, M, N = 1024, 4096, 1024, 1024, 2048, 1024, 512
FLOPS = 2 * K * H * S + 2 * 2 * H * N * M

F32 = mybir.dt.float32
BF16 = mybir.dt.bfloat16
I32 = mybir.dt.int32
U32 = mybir.dt.uint32
U16 = mybir.dt.uint16
U8 = mybir.dt.uint8
FP8X4 = mybir.dt.float8_e4m3fn_x4
FP4X4 = mybir.dt.float4_e2m1fn_x4
MULT = mybir.AluOpType.mult
ADD = mybir.AluOpType.add
SQUARE = mybir.ActivationFunctionType.Square
COPY = mybir.ActivationFunctionType.Copy

P = 128
PACK = 4
SLICES = 8
HALF = 512
PLANE_W = S + H
EARLY_W = HALF + 2 * P
LATE_W = PLANE_W - EARLY_W
TABLE_CUT = 5 * T // 8
CHUNK = 256
CHUNKS = M // CHUNK
WOVEN = PACK * CHUNK


def tile_list_gift_interactions_kernel(
    tc, tab_words, tab_scales, offs, w1_words, w1_scales, wgs, page0, offs2, offs3, fw, sq_words, sq_scales, out
):
    nc = tc.nc
    with ExitStack() as ctx:
        lists = ctx.enter_context(tc.tile_pool(name="lists", bufs=1))
        keep = ctx.enter_context(tc.tile_pool(name="keep", bufs=1))
        psum = ctx.enter_context(tc.psum_pool(name="psum", bufs=1))

        idx = lists.tile([P, S // 16], U16, name="idx")
        idx2 = lists.tile([P, S // 16], U16, name="idx2")
        idx3 = lists.tile([P, M // 16], U16, name="idx3")

        def bank(b):
            return psum.tile([P, HALF], F32, name="bank%d" % b, tag="bank%d" % b)

        halves = [slice(0, HALF), slice(HALF, S)]
        planes = keep.tile([P, 2 * PLANE_W], U8, name="planes", align_bytes=64)
        stage = keep.tile([P, PLANE_W], U8, name="stage", align_bytes=64)
        tab_sc = keep.tile([P, T], U8, name="tab_sc", align_bytes=64)
        w1_sc = keep.tile([P, H], U8, name="w1_sc", align_bytes=64)
        tab = [keep.tile([P, T], I32, name="tab%d" % k, tag="big%d" % k, align_bytes=64) for k in range(2)]
        w1_raw = {(0, 0): keep.tile([P, H], U8, name="w1_raw00", align_bytes=64)}
        w1_perm = {(a, k): keep.tile([P, H], U8, name="w1_perm%d%d" % (a, k), align_bytes=64) for a in range(2) for k in range(2)}
        wgs_rows = [keep.tile([P, S // 4], F32, name="wgs_rows0")]
        wg = [keep.tile([P, S], F32, name="wg%d" % t, tag="wg%d" % t) for t in range(PACK)]
        fw_bf = keep.tile([P, 2 * N * PACK], BF16, name="fw_bf", align_bytes=64)
        ident = keep.tile([P, P], F32, name="ident")
        make_identity(nc, ident[:])

        def load_table(k, lo, hi):
            words = tab_words[k].rearrange("p c i -> p (c i)").bitcast(I32)
            nc.sync.dma_start(out=tab[k][:, lo:hi], in_=words[:, lo:hi])

        def load_wgs(t):
            nc.sync.dma_start(out=wgs_rows[t][:], in_=wgs.rearrange("(q t) (u c) -> t q u c", t=PACK, u=4)[t])

        def load_w1(a, k):
            nc.sync.dma_start(out=w1_raw[a, k][:].bitcast(I32), in_=w1_words[k][:, H * a : H * (a + 1)].bitcast(I32))

        def load_page(i):
            a, t = divmod(i, PACK)
            nc.sync.dma_start(
                out=pages[i][:], in_=page0[HALF * a : HALF * (a + 1), :].rearrange("(p t) c -> t p c", t=PACK)[t]
            )

        def v_col(k, j):
            return EARLY_W * k if j == 0 else 2 * EARLY_W + LATE_W * (k + 1) - HALF

        def w1_col(k, i):
            return EARLY_W * k + HALF + P * i if i < 2 else 2 * EARLY_W + LATE_W * k + P * (i - 2)

        def move_scales(lo, hi):
            for q in range(4):
                nc.sync.dma_start(
                    out=planes[32 * q : 32 * q + 4, 2 * lo : 2 * hi].bitcast(I32), in_=stage[8 * q : 8 * q + 8, lo:hi].bitcast(I32)
                )

        def permute_w1(engine_copy, a, k, lo=0, hi=PACK):
            engine_copy(
                out=w1_perm[a, k][:].bitcast(U16).rearrange("p (t m) -> p t m", t=PACK)[:, lo:hi, :],
                in_=w1_raw[a, k][:].bitcast(U16).rearrange("p (m t) -> p t m", t=PACK)[:, lo:hi, :],
            )

        def deal_weights(t):
            turned = bank(7)
            for c in range(2):
                nc.tensor.transpose(turned[:, P * c : P * (c + 1)], wgs_rows[t][:, P * c : P * (c + 1)], ident[:])
            rows = turned[:, 0 : 2 * P].rearrange("p (c q u) -> p u c q", c=2, u=4)
            for j in range(2):
                dealt = keep.tile([P, HALF], F32, name="dealt", tag="dealt", bufs=2)
                nc.scalar.copy(
                    out=dealt[:].rearrange("p (u c g q) -> p u c g q", u=2, c=2, g=4),
                    in_=rows[:, 2 * j : 2 * j + 2].unsqueeze(3).to_broadcast([P, 2, 2, 4, 32]),
                )
                back = bank(5 + j)
                for c in range(4):
                    nc.tensor.transpose(back[:, P * c : P * (c + 1)], dealt[:, P * c : P * (c + 1)], ident[:])
                nc.scalar.copy(out=wg[t][:, halves[j]], in_=back[:])

        nc.sync.dma_start(idx[:], offs)
        nc.sync.dma_start(out=tab_sc[0:32, :].bitcast(I32), in_=tab_scales.rearrange("a q c -> q a c").bitcast(I32))
        nc.sync.dma_start(out=w1_sc[0:32, :].bitcast(I32), in_=w1_scales.rearrange("a q c -> q a c").bitcast(I32))
        load_table(0, 0, T)
        load_wgs(0)
        load_w1(0, 0)
        load_table(1, 0, TABLE_CUT)
        for rows_sc in (tab_sc, w1_sc):
            for lo, hi in ((32, 64), (64, 128)):
                nc.vector.memset(rows_sc[lo:hi, :].bitcast(I32), 0)
        nc.vector.memset(planes[:].bitcast(I32), 0)

        def gather_scales(j, got):
            nc.vector.tensor_copy(got[:], tab_sc[:].indirect(idx[:, 32 * j : 32 * (j + 1)]))

        dealt_sc = stage[:, HALF : HALF + H].rearrange("p (a t m) -> p a t m", a=2, t=PACK)
        given_sc = w1_sc[:].rearrange("p (a m t) -> p a t m", a=2, t=PACK)
        got_late = keep.tile([P, HALF], U8, name="got_late", align_bytes=64)
        with tc.tile_pool(name="head", bufs=1) as head:
            got_early = head.tile([P, HALF], U8, name="got_early", align_bytes=64)
            gather_scales(0, got_early)
            nc.vector.tensor_copy(out=dealt_sc[:, 0, 0:2, :], in_=given_sc[:, 0, 0:2, :])
            nc.vector.tensor_copy(out=stage[:, 0:HALF].bitcast(I32), in_=got_early[:].bitcast(I32))
        permute_w1(nc.vector.tensor_copy, 0, 0)
        gather_scales(1, got_late)
        nc.vector.tensor_copy(out=dealt_sc[:, 0, 2:4, :], in_=given_sc[:, 0, 2:4, :])
        nc.vector.tensor_copy(out=dealt_sc[:, 1, :, :], in_=given_sc[:, 1, :, :])
        nc.vector.tensor_copy(out=stage[:, HALF + H :].bitcast(I32), in_=got_late[:].bitcast(I32))
        deal_weights(0)

        ring = ctx.enter_context(tc.tile_pool(name="ring", bufs=1))
        pages = [ring.tile([P, T2], F32, name="page%d" % i, tag="page%d" % i, align_bytes=64) for i in range(SLICES)]
        v = [ring.tile([P, S], U32, name="v%d" % k, tag="v%d" % k, align_bytes=64) for k in range(2)]
        for a, k in ((0, 1), (1, 0), (1, 1)):
            w1_raw[a, k] = ring.tile([P, H], U8, name="w1_raw%d%d" % (a, k), align_bytes=64)
        wgs_rows.extend(ring.tile([P, S // 4], F32, name="wgs_rows%d" % t) for t in range(1, PACK))
        xs0 = ring.tile([P, PACK * M], F32, name="xs0", tag="xs0", align_bytes=64)
        xs1 = ring.tile([P, 2 * WOVEN], F32, name="xs1")
        fw_codes = ring.tile([P, 2 * N], U32, name="fw_codes", align_bytes=64)
        sq_codes = ring.tile([P, 2 * N], I32, name="sq_codes", align_bytes=64)
        sq_sc = ring.tile([P, N], U8, name="sq_sc", align_bytes=64)
        fw_sc = ring.tile([P, 2 * N], U8, name="fw_sc", align_bytes=64)
        nc.vector.memset(sq_sc[:].bitcast(I32), 0)

        move_scales(0, EARLY_W)
        load_table(1, TABLE_CUT, T)
        load_w1(0, 1)
        nc.sync.dma_start(idx2[:], offs2)
        load_page(0)
        load_wgs(1)
        load_page(1)
        move_scales(EARLY_W, PLANE_W)
        nc.sync.dma_start(idx3[:], offs3)
        load_wgs(2)
        load_page(2)
        load_wgs(3)
        for k in range(2):
            load_w1(1, k)
        load_page(3)
        x0_rows = xs0[:].rearrange("p (t m) -> p t m", t=PACK)
        fw_rows = fw.rearrange("(a p t) n -> a p t n", a=2, t=PACK)
        nc.sync.dma_start(out=x0_rows[:, :, 0:N], in_=fw_rows[0])
        for i in range(PACK, SLICES):
            load_page(i)
        x1_rows = [xs1[:, WOVEN * b : WOVEN * (b + 1)].rearrange("p (t m) -> p t m", t=PACK) for b in range(2)]
        for b in range(2):
            nc.sync.dma_start(out=x1_rows[b], in_=fw_rows[1][:, :, CHUNK * b : CHUNK * (b + 1)])
        for q in range(4):
            nc.sync.dma_start(
                out=sq_sc[32 * q : 32 * q + 8, :].bitcast(I32), in_=sq_scales[:, 4 * q : 4 * q + 4, :].bitcast(I32)
            )
        nc.sync.dma_start(
            out=sq_codes[:].rearrange("p (a c) -> p a c", a=2),
            in_=sq_words.rearrange("a p c i -> p a (c i)").bitcast(I32),
        )

        def gather_table(k, lo, hi):
            nc.vector.tensor_copy(v[k][:, lo:hi], tab[k][:].bitcast(U32).indirect(idx[:, lo // 16 : hi // 16]))

        gather_table(0, 0, S)
        for lo, hi in ((0, 256), (256, HALF), (HALF, S)):
            gather_table(1, lo, hi)

        h_rows = [keep.tile([P, PACK * S], F32, name="h%d" % a, tag="big%d" % a, align_bytes=64) for a in range(2)]

        def h_of(i):
            return h_rows[i // PACK][:, S * (i % PACK) : S * (i % PACK + 1)]

        def make_h(i, lo, hi, b):
            a, t = divmod(i, PACK)
            j, first_col = divmod(lo, HALF)
            acc = bank(b)[:, 0 : hi - lo]
            for k in range(2):
                w1_at = w1_col(k, i)
                v_at = v_col(k, j) + first_col
                nc.tensor.matmul_mx(
                    out=acc,
                    lhsT=w1_perm[a, k][:, 2 * P * t : 2 * P * (t + 1)].bitcast(FP4X4),
                    lhsT_scale=planes[:, w1_at : w1_at + P],
                    rhs=v[k][:, lo:hi].bitcast(FP8X4),
                    rhs_scale=planes[:, v_at : v_at + hi - lo],
                    start=(k == 0),
                    stop=(k == 1),
                )
            nc.scalar.copy(out=h_of(i)[:, lo:hi], in_=acc)

        permute_w1(nc.scalar.copy, 0, 1, 0, 2)
        for b in range(2):
            make_h(0, 256 * b, 256 * (b + 1), b)
        make_h(1, 0, HALF, 2)
        deal_weights(1)
        for i in range(2):
            make_h(i, HALF, S, 3 + i)
        for i in range(2, SLICES):
            if i < PACK:
                deal_weights(i)
            if i == 2:
                permute_w1(nc.scalar.copy, 0, 1, 2, PACK)
            if i == PACK:
                for k in range(2):
                    permute_w1(nc.scalar.copy, 1, k)
            for j in range(2):
                make_h(i, HALF * j, HALF * (j + 1), (2 * i + j) % 4)

        def scatter(i, lo=0, hi=S):
            nc.vector.tensor_tensor(
                pages[i][:].indirect(idx2[:, lo // 16 : hi // 16]), h_of(i)[:, lo:hi], wg[i % PACK][:, lo:hi], MULT
            )

        def gather(i, into, lo, hi):
            nc.vector.tensor_copy(into, pages[i][:].indirect(idx3[:, lo // 16 : hi // 16]))

        def woven(part):
            return part.rearrange("p (c i t) -> p c t i", i=4, t=PACK)

        def by_fours(rows):
            return rows.rearrange("p t (c i) -> p c t i", i=4)

        def quantize(codes, scales, src):
            nc.vector.quantize_mx(out=codes.bitcast(FP8X4), scales=scales, in_=src)

        def place(kind, a, c):
            return 2 * (2 * c + a) + "xz".index(kind)

        rounded = ring.tile([P, 4 * CHUNKS * WOVEN], BF16, name="rounded", align_bytes=64)
        scales = ring.tile([P, 4 * M], U8, name="scales", align_bytes=64)

        def start_of(u):
            return WOVEN * u - (WOVEN // 2 if u >= place("x", 1, CHUNKS - 1) else 0)

        def round_chunk(a, c, rows):
            u = place("x", a, c)
            aside = (0, CHUNK, 0, CHUNK // 2)[c] if a == 1 else 0
            x_bf = rounded[:, start_of(u) : start_of(u) + WOVEN]
            if aside > 0:
                nc.gpsimd.tensor_scalar(
                    out=woven(x_bf[:, 0 : PACK * aside]), in0=by_fours(rows[:, :, 0:aside]),
                    scalar1=1.0, scalar2=0.0, op0=MULT, op1=ADD,
                )
            if aside < CHUNK:
                nc.scalar.copy(out=woven(x_bf[:, PACK * aside :]), in_=by_fours(rows[:, :, aside:]))
            nc.scalar.activation(out=woven(rounded[:, start_of(u + 1) : start_of(u + 1) + WOVEN]), in_=by_fours(rows), func=SQUARE)

        for j in range(2):
            for i in range(2):
                scatter(i, HALF * j, HALF * (j + 1))
        for i in range(2, PACK):
            scatter(i)
        nc.scalar.copy(out=woven(fw_bf[:, 0 : PACK * N]), in_=by_fours(x0_rows[:, :, 0:N]))
        for t in range(PACK):
            gather(t, x0_rows[:, t, :], 0, M)
        for b in range(2):
            first = PACK * N + WOVEN * b
            nc.scalar.copy(out=woven(fw_bf[:, first : first + WOVEN]), in_=by_fours(x1_rows[b]))
        for c in range(CHUNKS):
            round_chunk(0, c, x0_rows[:, :, CHUNK * c : CHUNK * (c + 1)])
        for i in range(PACK, SLICES):
            scatter(i)

        codes_first = ring.tile([P, 2 * CHUNK], U32, name="codes_first", align_bytes=64)
        codes_rest = ring.tile([P, 4 * M - 2 * CHUNK], U32, name="codes_rest", tag="xs0", align_bytes=64)

        codes_last = []

        def codes_of(lo, hi):
            if 12 <= lo < 14:
                return codes_last[0][:, CHUNK * (lo - 12) : CHUNK * (hi - 12)]
            if lo < 2:
                return codes_first[:, CHUNK * lo : CHUNK * hi]
            return codes_rest[:, CHUNK * (lo - 2) : CHUNK * (hi - 2)]

        def quantize_places(lo, hi):
            quantize(codes_of(lo, hi), scales[:, CHUNK * lo : CHUNK * hi], rounded[:, start_of(lo) : start_of(lo) + WOVEN * (hi - lo)])

        def fetch(c):
            rows = x1_rows[c % 2]
            for t in range(PACK):
                gather(PACK + t, rows[:, t, :], CHUNK * c, CHUNK * (c + 1))
            if c == CHUNKS - 1:
                codes_last.append(ring.tile([P, 2 * CHUNK], U32, name="codes_last", tag="page5", align_bytes=64))
                quantize_places(12, 14)
            round_chunk(1, c, rows)

        staged = [keep.tile([P, 8 * CHUNK], F32, name="staged%d" % j, tag="big%d" % j, align_bytes=64) for j in range(2)]
        sums = {}
        squares = {}

        def multiply(c):
            for kind in "xz":
                for pair in range(2):
                    sums[kind, c, pair] = bank(4 * (c % 2) + 2 * "xz".index(kind) + pair)
            steps = [(kind, a, n) for a in range(2) for kind in "xz" for n in range(4)]
            if c == CHUNKS - 1:
                steps = [s for s in steps if s[0] == "x"]
                steps += [("z", a, 2 * pair + n) for pair in range(2) for a in (1, 0) for n in range(2)]
            for kind, a, n in steps:
                in_bank = [s for s in steps if s[0] == kind and s[2] // 2 == n // 2]
                u = place(kind, a, c)
                cols = slice(CHUNK * u, CHUNK * (u + 1))
                ncols = slice(N * a + P * n, N * a + P * (n + 1))
                if kind == "x":
                    lhs, lhs_sc = fw_codes[:, ncols], fw_sc[:, ncols]
                else:
                    lhs, lhs_sc = sq_codes[:, ncols], sq_sc[4 * a : P, P * n : P * (n + 1)]
                nc.tensor.matmul_mx(
                    out=sums[kind, c, n // 2][:, CHUNK * (n % 2) : CHUNK * (n % 2 + 1)],
                    lhsT=lhs.bitcast(FP8X4),
                    lhsT_scale=lhs_sc,
                    rhs=codes_of(u, u + 1).bitcast(FP8X4),
                    rhs_scale=scales[:, cols],
                    start=((kind, a, n) == in_bank[0]),
                    stop=((kind, a, n) == in_bank[-1]),
                )
            for pair in range(2):
                squares[c, pair] = ring.tile([P, HALF], F32, name="half_sq", tag="half_sq", bufs=4)
                nc.scalar.activation(out=squares[c, pair][:], in_=sums["x", c, pair][:], func=SQUARE, scale=0.5**0.5)

        def finish_aside(c):
            for pair in range(2):
                u = place("xz"[pair], 1, CHUNKS - 1)
                half_b = rounded[:, WOVEN * u : WOVEN * (u + 1)].bitcast(F32)
                nc.scalar.activation(out=half_b, in_=sums["z", c, pair][:], func=COPY, scale=-0.5)
                first = 2 * HALF * (c % 2) + HALF * pair
                res = staged[c // 2][:, first : first + HALF]
                nc.gpsimd.tensor_tensor(out=res, in0=squares[c, pair][:], in1=half_b, op=ADD)
                rows = out[2 * P * pair : 2 * P * (pair + 1), CHUNK * c : CHUNK * (c + 1)]
                nc.sync.dma_start(
                    out=rows.rearrange("(n p) m -> p n m", p=P), in_=res.rearrange("p (n m) -> p n m", m=CHUNK)
                )

        def finish(c):
            for pair in range(2):
                first = 2 * HALF * (c % 2) + HALF * pair
                tiles = ((0, 1), (1, 2)) if (c, pair) == (CHUNKS - 1, 1) else ((0, 2),)
                for lo, hi in tiles:
                    cols = slice(CHUNK * lo, CHUNK * hi)
                    res = staged[c // 2][:, first : first + HALF][:, cols]
                    nc.vector.scalar_tensor_tensor(
                        out=res, in0=sums["z", c, pair][:, cols], scalar=-0.5, in1=squares[c, pair][:, cols], op0=MULT, op1=ADD
                    )
                    rows = out[P * (2 * pair + lo) : P * (2 * pair + hi), CHUNK * c : CHUNK * (c + 1)]
                    nc.sync.dma_start(
                        out=rows.rearrange("(n p) m -> p n m", p=P), in_=res.rearrange("p (n m) -> p n m", m=CHUNK)
                    )

        quantize_places(0, 2)
        fetch(0)
        quantize(fw_codes[:], fw_sc[:], fw_bf[:])
        fetch(1)
        for c in range(2):
            quantize_places(4 * c + 2, 4 * c + 6)
            multiply(c)
            if c == 0:
                finish_aside(0)
            fetch(c + 2)
        quantize_places(10, 12)
        multiply(2)
        finish(1)
        quantize_places(14, 15)
        quantize_places(15, 16)
        multiply(3)
        finish(2)
        finish(3)
